import numpy as np, ml_dtypes
CORES = [24,25,26,27,28,29,30,31]
N = 8
import mx_ref
BF = ml_dtypes.bfloat16
def gentries(a):
    return np.ascontiguousarray(a.reshape(8, 16, -1).transpose(0, 2, 1)).reshape(8, -1)
def gtable(e):
    e = np.asarray(e); return np.ascontiguousarray(e.reshape(8, -1, 16).transpose(0, 2, 1)).reshape(128, -1).astype(np.int32)
def gcols(t, e):
    v = np.concatenate([t.reshape(8, 16, -1, 4), np.zeros((8, 16, 1, 4), BF)], axis=2)
    return np.ascontiguousarray(np.stack([v[g][:, e[g]] for g in range(8)])).reshape(128, -1)
def gpick(z, e):
    return np.concatenate([z[16 * g:16 * g + 16][:, e[g]] for g in range(8)])
def tile(rs):
    return np.stack(rs, axis=2).reshape(128, -1).astype(BF)
def pick(q, e):
    c = np.concatenate([q[0].reshape(128, -1, 4), np.zeros((128, 1, 4), np.uint8)], axis=1); s = np.concatenate([q[1], np.ones((16, 1), np.uint8)], axis=1)
    return (np.ascontiguousarray(c[:, e].reshape(128, -1)), np.ascontiguousarray(s[:, e]))
def join(*qs):
    return (np.concatenate([q[0] for q in qs], axis=1), np.concatenate([q[1] for q in qs], axis=1))
def put(q, e, v):
    c, s = q[0].reshape(128, -1, 4).copy(), q[1].copy(); c[:, e] = v[0].reshape(128, -1, 4); s[:, e] = v[1]
    return (c.reshape(128, -1), s)
def pk(c, s):
    return (np.ascontiguousarray(c), mx_ref.live(s))
def emit(q):
    return q[0], q[1]
def packed(v, rng):
    q = [mx_ref.quantize(np.ascontiguousarray(v[r])) for r in range(N)]
    return np.stack([a for a, b in q]), np.stack([mx_ref.plane(b, rng) for a, b in q])
def values_of_codes():
    e, c = np.zeros((128, 128, 4), np.float32), np.zeros((128, 2, 4), np.uint8)
    e[np.arange(128), np.arange(128), 0] = 1
    c[:127, :, 0] = np.arange(256).reshape(2, 128).T[:127]
    return mx_ref.matmul(mx_ref.quantize(e.reshape(128, 512).astype(BF)), (c.reshape(128, 8), np.full((16, 2), 127, np.uint8))).T.reshape(-1).astype(np.float64)
CODE_VALUE, SCALE_VALUE = values_of_codes(), 2.0 ** (np.arange(256) - 127.0)
def decode(q):
    return (CODE_VALUE[q[0]].reshape(16, 8, -1, 4) * SCALE_VALUE[q[1]][:, None, :, None] + 0.0).reshape(128, -1).astype(np.float32)
def f(rng, *shape):
    return mx_ref.flush((rng.standard_normal(shape, dtype=np.float32) * np.exp2(rng.integers(-2, 3, shape[:-1] + (1,)))).astype(BF))
def wide(rng, *shape, cols=0):
    v = rng.standard_normal(shape, dtype=np.float32) * np.exp2(rng.integers(-12, 13, shape)).astype(np.float32)
    if cols: v *= np.repeat(np.exp2(rng.integers(-cols, cols + 1, shape[:-2] + (1, shape[-1] // 4))) * (rng.random(shape[:-2] + (1, shape[-1] // 4)) > 0.0625), 4, axis=-1).astype(np.float32)
    return mx_ref.flush(v.astype(BF))
C = 320
STEP = [1, 2, 4]
def numbers_of(rng):
    return {"x": np.array(f(rng, N, 128, 4 * C)), "u": np.array(f(rng, N, 128, 512)), "v": np.array(f(rng, N, 128, 512))}
def orders(rng):
    return rng.permuted(np.tile(np.arange(C), (N, 8, 1)), axis=2), rng.permuted(np.tile(np.arange(8)[:, None], (N, 1, C)), axis=1)
def stored(p, o):
    return {"pg": np.stack([gtable(p[r]) for r in range(N)]), "og": np.stack([gtable(o[r]) for r in range(N)])}
def layers(rng, still=[]):
    w = np.array(f(rng, N, 128, 2048)).reshape(N, 8, 16, 4, 8, 16, 4)
    for i in still:
        w[:, :, i] = 0
        w[:, :, :, :, :, i] = 0
    return w
def weights(rng, w):
    c, s = packed(np.ascontiguousarray(w).reshape(N, 128, 2048), rng)
    return {"wc": c, "ws": s}
def setup_inputs(rng):
    return {**numbers_of(rng), **stored(*orders(rng)), **weights(rng, layers(rng))}
def setup_inputs_ties(rng):
    d = numbers_of(rng)
    n = rng.permutation(N)
    k = rng.integers(0, 4, (N, 8, C))
    k[n[1]] -= 4
    k[n[2]] = np.arange(8)[:, None]
    x = d["x"].reshape(N, 8, 16, C, 4)
    x[:, :, 0] = 0
    x[:, :, 0, :, 0] = k.astype(np.float32).astype(BF)
    u = d["u"].reshape(N, 128, 128, 4)
    u[:, :, ::16] = 0
    for r in range(N):
        for h in range(0, 128, 16): u[r, h, h, 0] = 0.0 if r == n[0] else 1.0
    p, o = orders(rng)
    o[n[2]] = 7 - np.arange(8)[:, None]
    return {"x": x.reshape(N, 128, 4 * C), "u": u.reshape(N, 128, 512), "v": d["v"], **stored(p, o), **weights(rng, layers(rng, [0]))}
def setup_inputs_near(rng):
    d = numbers_of(rng)
    x = d["x"].astype(np.float32).reshape(N, 8, 16, C, 4)
    x[:, :, 0] = 0
    x[:, :, 8:] = 0
    u = d["u"].reshape(N, 128, 128, 4)
    u[:, :, ::16] = 0
    w = layers(rng, [0, 8, 9, 10, 11, 12, 13, 14, 15])
    kind, size, least = np.zeros(N, np.int64), np.ones(N), 2.0 ** -30
    turn = rng.integers(2)
    for i, r in enumerate(rng.permutation([r for r in range(N) if r < r ^ STEP[0]])):
        both = [r, r ^ STEP[0]]
        kind[both] = 2 if i == 0 else rng.permutation(2)
        size[both] = least if (i + turn) % 2 else 1.0
    for r in range(N):
        s = rng.integers(0, 16, (8, C))
        digits = ((s[:, :, None] >> np.arange(4)) & 1) * np.exp2(np.arange(4) - 23.0)
        if kind[r] == 0:
            x[r, :, 0, :, 0] = rng.choice([-1.0, 1.0])
            x[r, :, 8] = digits
            x[r, :, 11, :, 0] = 2.0 ** -10
        if kind[r] == 1: x[r, :, 8] = digits * rng.choice([-1.0, 1.0], (8, C, 1))
        if kind[r] == 2:
            e = rng.integers(-1, 2, (8, C)) * least
            x[r, :, 8, :, 0] = 1.25 * e
            x[r, :, 9, :, 0] = -1.125 * e
            x[r, :, 13, :, 0] = rng.choice([-1.0, 1.0], (8, C)) * least
            for g in range(8): w[r, g, 13, 0, g, 12, 0] = 2.0 ** -8
        for g, j in zip(rng.permutation(8)[:4], [0, C - 1, int(rng.integers(C)), int(rng.integers(C))]): x[r, g, 0, j, 0] = 2.0 ** 29 * rng.choice([-1.0, 1.0])
        k = size[r] if kind[r] == 0 else least
        for h in range(0, 128, 16):
            u[r, h, h, 0] = k if kind[r] == 0 else 1.0
            if kind[r] == 0: u[r, h + 11, h, 0] = k
            if kind[r] < 2: u[r, h + 8, h] = k
            else:
                u[r, h + 8, h, 0] = k
                u[r, h + 9, h, 0] = 1.125 * k
                u[r, h + 12, h, 0] = k
    return {"x": x.reshape(N, 128, 4 * C).astype(BF), "u": u.reshape(N, 128, 512), "v": d["v"], **stored(*orders(rng)), **weights(rng, w)}
def setup_inputs_odd(rng):
    d = numbers_of(rng)
    x = (1.0 + (2 * rng.integers(0, 64, (N, 16, 8, C, 4)) + 1) * 2.0 ** -7) * np.exp2(-rng.integers(0, 7, (N, 16, 8, C, 4)).astype(np.float64)) * rng.choice([-1.0, 1.0], (N, 16, 8, C, 4))
    x[:, :, 0, :, 0] = 1.96875 * 2.0 ** 8 * rng.choice([-1.0, 1.0], (16, 1))
    u = d["u"].reshape(N, 16, 8, 128, 4)
    u[:, :, 0, ::16] = 0
    w = layers(rng, [0, 8])
    for g in range(8):
        for i in (0, 8): w[:, g, i, 0, g, i, 0] = -0.5
    return {"x": x.astype(np.float32).reshape(N, 128, 4 * C).astype(BF), "u": u.reshape(N, 128, 512), "v": d["v"], **stored(*orders(rng)), **weights(rng, w)}
def setup_inputs_ends(rng):
    d = numbers_of(rng)
    n, e, c = [rng.permutation(N) % 4 for _ in range(3)]
    low, tiny = 2.0 ** 29, 2.0 ** -30
    def small(*s): return (1 + 0.125 * rng.integers(0, 8, s)) * tiny
    x = np.zeros((N, 8, 16, C, 4))
    u = d["u"].astype(np.float32).reshape(N, 8, 16, 128, 4)
    v = d["v"].astype(np.float32)
    w = np.zeros((N, 128, 4, 128, 4), np.float32)
    i = np.arange(128)
    p, o = orders(rng)
    for r in range(N):
        h = rng.permutation(8)
        a = np.where(h < 2, 0.0, h % 2 * 2.0 - 1.0)[:, None]
        k = np.full(16, 4.0)
        k[15] = 0
        if n[r] < 2:
            x[r] = -(1 + 0.125 * rng.integers(0, 4, (8, 16, C, 4))) * low
            if n[r] == 1: x[r] *= rng.choice([-1.0, 1.0], (C, 1))
            x[r, :, 15] = 2.0 ** 16 * rng.choice([-1.0, 1.0], (8, C, 4))
            u[r, :, :, ::16] = a * 2.0 ** 30
            v[r] = rng.choice([-1.0, 1.0], (128, 512)) * (1 + 0.125 * rng.integers(4, 9, (128, 512))) * low
        elif n[r] == 2:
            x[r] = -small(8, 16, C, 4)
            u[r, :, :, ::16] = a * small(8, 16, 8, 4)
            u[r, :, 14:, ::16] = 0
            v[r] = rng.choice([-1.0, 1.0], (128, 512)) * small(128, 512)
            k[:] = 0
            k[14], k[15] = 2.0 ** -8, 2.0 ** 8
        else:
            x[r] = d["x"][r].astype(np.float32).reshape(8, 16, C, 4)[:, :, :1]
            u[r, :, :, ::16] *= np.abs(a).astype(np.float32)
        for b in range(4): w[r, i, b, i, b] = np.tile(k, 8)
        if e[r] < 3: p[r] = [np.arange(C), np.arange(C)[::-1], (np.arange(C) + 1) % C][e[r]]
        up = np.arange(8)[:, None]
        if c[r] < 3: o[r] = np.where([np.ones(C, bool), np.zeros(C, bool), rng.random(C) < 0.5][c[r]], up, 7 - up)
    return {"x": x.astype(np.float32).reshape(N, 128, 4 * C).astype(BF), "u": u.reshape(N, 128, 512).astype(BF), "v": v.astype(BF), **stored(p, o), **weights(rng, w.astype(BF))}
def setup_inputs_spread(rng):
    d = setup_inputs(rng)
    d["x"] = wide(rng, N, 128, 4 * C, cols=6)
    return d
def check_inputs(d):
    b = []
    for k in ("x", "u", "v"):
        a = np.abs(d[k].astype(np.float32))
        if not (np.isfinite(a).all() and ((a == 0) | (a >= 2.0 ** -30) & (a <= 2.0 ** 30)).all()): b.append("a value of " + k)
    none, least, most = [emit(mx_ref.quantize(np.full((128, 16), k, np.float32).astype(BF)))[1][0, 0] for k in (0.0, 2.0 ** -8, 2.0 ** 8)]
    for r in range(N):
        if not (np.sort(gentries(d["pg"][r]), axis=1) == np.arange(C)).all(): b.append("pg: a group's entries aren't all columns")
        if not (np.sort(gentries(d["og"][r]), axis=0) == np.arange(8)[:, None]).all(): b.append("og: a column's entries aren't all groups")
        if ((d["wc"][r] == 0x7F) | (d["wc"][r] == 0xFF)).any(): b.append("wc: a code that is no number")
        s = mx_ref.live(d["ws"][r])
        if ((s != none) & ((s < least) | (s > most))).any(): b.append("ws: a scale out of range")
        if (((d["wc"][r].reshape(16, 8, 512, 4) & 0x7F) != 0) & (s == none)[:, None, :, None]).any(): b.append("wc: a code other than zero under the scale of zeros")
    return b
def walk(p, o):
    a, at = np.arange(C), np.zeros((8, C), np.int64)
    for k in range(8):
        a = p[o[k], a]
        at[o[k], np.arange(C)] = a
    return at
def reference(x, u, v, pg, og, wc, ws):
    qu = [mx_ref.quantize(u[r]) for r in range(N)]
    lay = [pk(wc[r], ws[r]) for r in range(N)]
    p, o = [np.array(gentries(pg[r])) for r in range(N)], [np.array(gentries(og[r])) for r in range(N)]
    at = [walk(p[r], o[r]) for r in range(N)]
    now = [x[r] for r in range(N)]
    for t, step in enumerate(STEP):
        held, z = [], []
        for r in range(N):
            q = mx_ref.quantize(now[r])
            held.append(decode(q))
            s = mx_ref.matmul(qu[r], q)[::16]
            c = s[o[r], at[r][o[r], np.arange(C)]]
            for k in range(t % 2, 7, 2):
                turn = c[k] > c[k + 1]
                o[r][k], o[r][k + 1] = np.where(turn, o[r][k + 1], o[r][k]), np.where(turn, o[r][k], o[r][k + 1])
            at[r] = walk(p[r], o[r])
            z.append(mx_ref.quantize(gcols(held[r].astype(BF), at[r])))
        for r in range(N):
            e = np.take_along_axis(p[r], at[r], axis=1)
            now[r] = tile([held[r][:, b::4] + gpick(mx_ref.matmul(pick(lay[r], np.arange(128 * b, 128 * b + 128)), z[r ^ step]) * np.float32(0.03125), e) for b in range(4)])
    y, ol = np.zeros((N, 128, C), np.float32), np.zeros((N, 8, C), np.float32)
    oc, osc = np.zeros((N, 128, 4 * C), np.uint8), np.zeros((N, 16, C), np.uint8)
    for r in range(N):
        q = mx_ref.quantize(now[r])
        y[r] = mx_ref.matmul(mx_ref.quantize(v[r]), q)
        ol[r] = o[r]
        oc[r], osc[r] = emit(q)
    return {"y": y, "ol": ol, "oc": oc, "osc": osc}

@@ -1,0 +1,502 @@
+from concourse.mybir import dt, AluOpType, ActivationFunctionType
+
+FN = ActivationFunctionType
+COPY = FN.Copy
+ADD, SUB, MUL, MAX, MIN = AluOpType.add, AluOpType.subtract, AluOpType.mult, AluOpType.max, AluOpType.min
+BIG = 1048576.0
+C = 320
+STEP = [1, 2, 4]
+CH = [(0, 192), (192, 320)]
+
+SCRATCH = {}
+
+
+def _d(name, cols, dtype, where="sbuf"):
+    SCRATCH[name] = (where, [128, cols], dtype)
+
+
+ALIAS = {}
+
+
+def _share(buf, dtype, *parts):
+    at = 0
+    for n, c in parts:
+        ALIAS[n] = (buf, at, c)
+        at += c + c % 2
+    _d(buf, at, dtype)
+
+
+_share("iv", "int32", ("pint", 1), ("lanei", 1), ("hi", 1), ("xi", 1), ("sxi", 1), ("sx7", 1), ("upi", 16), ("mi", 24), ("pi0", 24), ("pi1", 24), ("pi2", 24))
+_share("iw", "int32", ("ogr", 20), ("og7", 20), ("ls0", 24), ("ls1", 24), ("ls2", 24))
+_share("fv", "float32", ("lanef", 1), ("hf", 1), ("h8", 1), ("h2", 1), ("ux", 1), ("xf", 1), ("lan16", 1), ("lanem", 1), ("ge20", 24), ("ge40", 24), ("ja", 48), ("jf", 48))
+_share("uv", "uint16", ("pgu", 20), ("ogu", 20), ("upu", 16), ("cl", 24), ("gw", 24))
+_share("wv", "float32", *[(n, 48) for n in ("x0", "y0", "y1", "X1", "Y1", "DX", "DY", "MA", "MB", "sa0", "sb0", "sa1", "sb1", "sa2", "sb2")])
+_d("pgi", 20, "int32")
+_d("ogi", 20, "int32")
+for _n, _c in (("i16", 384), ("i8", 320), ("w320", 8), ("wone", 8),
+               ("un", 384), ("ka", 384), ("msk", 384), ("r16", 384), ("r8", 320), ("lab", 320),
+               ("N", 384), ("K", 384), ("DN", 192), ("KA", 192), ("KB", 192), ("KC", 192), ("MN", 192), ("E", 192), ("CC", 192),
+               ("G", 48), ("SC", 48), ("G2", 48), ("SC2", 48), ("VV", 384), ("SV", 320), ("VF", 384), ("SF", 384), ("ST", 2560), ("BG", 320), ("BS", 320),
+               ("rb0", 320), ("rb1", 320), ("rb2", 320), ("rb3", 320), ("lm", 384), ("o1", 384), ("o2", 192), ("o3", 96), ("o4", 48),
+               ("olf", 320), ("yb", 320)):
+    _d(_n, _c, "float32")
+for _n, _c in (("off", 32), ("of2", 8), ("fl0", 26), ("fl1", 26), ("fl2", 26), ("ol40", 40), ("ow", 20)):
+    _d(_n, _c, "uint16")
+for _t in range(3):
+    _d("ml%d" % _t, 40, "uint16")
+    _d("ll%d" % _t, 40, "uint16")
+    _d("al%d" % _t, 20, "uint16")
+    _d("pl%d" % _t, 20, "uint16")
+    _d("bl%d" % _t, 20, "uint16")
+    _d("fo%d" % _t, 1280, "bfloat16")
+    _d("fp%d" % _t, 1280, "bfloat16")
+    _d("zt%d" % _t, 1280, "bfloat16")
+    _d("zc%d" % _t, 320, "float8_e4m3fn_x4")
+    _d("zs%d" % _t, 320, "uint8")
+    _d("lc%d" % _t, 320, "float8_e4m3fn_x4")
+    _d("lp%d" % _t, 320, "uint8")
+for _t in range(4):
+    _d("xt%d" % _t, 1280, "bfloat16")
+    _d("qc%d" % _t, 320, "float8_e4m3fn_x4")
+    _d("qs%d" % _t, 320, "uint8")
+for _n, _c in (("i320", 320), ("P", 2560), ("ones", 512), ("ec", 2048), ("ut", 512), ("vt", 512)):
+    _d(_n, _c, "bfloat16")
+for _n, _c in (("eq", 512), ("wq", 512), ("uq", 128), ("uw", 256), ("vq", 128)):
+    _d(_n, _c, "float8_e4m3fn_x4")
+    _d(_n + "s", _c, "uint8")
+for _k in range(8):
+    _d("ps%d" % _k, 512, "float32", "psum")
+
+DMA_SEMS = ["dpg", "dog", "du", "dxa", "dxb", "dw", "dv", "dp", "own0", "own1", "own2", "par0", "par1", "par2", "do1", "do2", "dout"]
+SEMAPHORES = ["cv", "cs", "ct", "cg", "left", "rq0", "rq1", "rq2", "rl0", "rl1", "rl2"] + DMA_SEMS
+
+
+def slot(k):
+    return k // 2 + (4 if k % 2 else 0)
+
+
+def rank_program(g, core, T, topo):
+    rank = T.rank_of(core)
+    if rank is None:
+        return
+    queue = {"v": g.vector, "s": g.scalar, "t": g.tensor, "g": g, "y": g.sync}
+    total = {s: 0 for s in SEMAPHORES}
+    clock = {q: {} for q in queue}
+    wrote, read = {}, {}
+
+    def O(name, lo=0, hi=None, step=1):
+        if name in ALIAS:
+            name, at, n = ALIAS[name]
+            lo, hi = at + lo, at + (n if hi is None else hi)
+        hi = SCRATCH[name][1][1] if hi is None else hi
+        ap = T[name][:, lo:hi] if step == 1 else T[name][:, lo:hi:step]
+        return (ap, [(name, lo, hi, step, lo % step)])
+
+    def codes(o):
+        return (o[0].bitcast(dt.uint8), o[1])
+
+    def words(o):
+        return (o[0].bitcast(dt.uint32), o[1])
+
+    def by(win, off):
+        return (win[0].indirect(off[0]), win[1] + off[1])
+
+    def meet(a, b):
+        return a[1] < b[2] and b[1] < a[2] and not (a[3] == b[3] > 1 and a[4] != b[4])
+
+    def order(q, reads, writes, dma=False):
+        evs = []
+        writes = writes + [r for r in reads if r[0][:2] == "ps"]
+        for r in reads:
+            evs += [e for w, e in wrote.get(r[0], []) if meet(r, w)]
+        for r in writes:
+            evs += [e for w, e in wrote.get(r[0], []) if meet(r, w)]
+            evs += [e for w, e in read.get(r[0], []) if meet(r, w) and (dma or e[3] != q)]
+        want = {}
+        for sem, val, snap, who in evs:
+            if clock[q].get(sem, 0) < val and want.get(sem, (0,))[0] < val:
+                want[sem] = (val, snap)
+        for sem in list(want):
+            if any(o != sem and want[o][1].get(sem, 0) >= want[sem][0] for o in want):
+                del want[sem]
+        for sem, (val, snap) in want.items():
+            queue[q].wait_ge(T.sem[sem], val)
+            for s2, v2 in list(snap.items()) + [(sem, val)]:
+                clock[q][s2] = max(clock[q].get(s2, 0), v2)
+
+    def note(reads, writes, ev):
+        for r in reads:
+            read.setdefault(r[0], []).append((r, ev))
+        for w in writes:
+            old = wrote.get(w[0], [])
+            wrote[w[0]] = [(o, e) for o, e in old if not (w[3] == 1 and w[1] <= o[1] and o[2] <= w[2])] + [(w, ev)]
+            if w[0] in read:
+                read[w[0]] = [(o, e) for o, e in read[w[0]] if not (w[3] == 1 and w[1] <= o[1] and o[2] <= w[2])]
+
+    def run(q, outs, ins, call):
+        reads = [r for o in ins for r in o[1]]
+        writes = [r for o in outs for r in o[1]]
+        order(q, reads, writes)
+        sem = "c" + q
+        total[sem] += 1
+        snap = dict(clock[q])
+        call().then_inc(T.sem[sem], 1)
+        note(reads, writes, (sem, total[sem], snap, q))
+
+    def dmas(sem, items):
+        snap, acc = {}, []
+        for q, out, in_, writes, reads in items:
+            order(q, reads, writes, True)
+            queue[q].dma_start(out, in_).then_inc(T.sem[sem], 16)
+            total[sem] += 16
+            for s2, v2 in clock[q].items():
+                snap[s2] = max(snap.get(s2, 0), v2)
+            acc.append((reads, writes))
+        for reads, writes in acc:
+            note(reads, writes, (sem, total[sem], snap, "dma"))
+
+    def arrives(sem, val, outs):
+        total[sem] += val
+        note([], [r for o in outs for r in o[1]], (sem, val, {}, "far"))
+
+    def copy(out, in_, q="v"):
+        if q == "v":
+            run(q, [out], [in_], lambda: g.vector.tensor_copy(out[0], in_[0]))
+        else:
+            run(q, [out], [in_], lambda: g.scalar.activation(out[0], in_[0], COPY))
+
+    def tt(out, a, b, op):
+        run("v", [out], [a, b], lambda: g.vector.tensor_tensor(out[0], a[0], b[0], op))
+
+    def ts(out, a, s1, s2, op0, op1=None):
+        ins = [a] + [s for s in (s1, s2) if isinstance(s, tuple)]
+        v1 = s1[0] if isinstance(s1, tuple) else s1
+        v2 = s2[0] if isinstance(s2, tuple) else s2
+        if op1 is None:
+            run("v", [out], ins, lambda: g.vector.tensor_scalar(out[0], a[0], v1, None, op0))
+        else:
+            run("v", [out], ins, lambda: g.vector.tensor_scalar(out[0], a[0], v1, v2, op0, op1))
+
+    def act(out, in_, func, scale, bias):
+        col = isinstance(bias, tuple)
+        run("s", [out], [in_] + [bias] * col, lambda: g.scalar.activation(out[0], in_[0], func, bias=bias[0] if col else bias, scale=scale))
+
+    def scan(out, reset, data):
+        run("v", [out], [reset, data], lambda: g.vector.tensor_tensor_scan(out[0], reset[0], data[0], -2.0 * BIG, MIN, MAX))
+
+    def iota(out, pattern, base, mul):
+        kw = {} if SCRATCH[out[1][0][0]][2] == "int32" else {"allow_small_or_imprecise_dtypes": True}
+        run("g", [out], [], lambda: g.iota(out[0], pattern, base, mul, **kw))
+
+    def quant(cn, sn, xn, lo, hi):
+        q, s, x = O(cn, lo, hi), O(sn, lo, hi), O(xn, 4 * lo, 4 * hi)
+        run("v", [q, s], [x], lambda: g.vector.quantize_mx(q[0], s[0], x[0]))
+
+    bank = [0]
+
+    def mx(an, alo, bn, lo, hi, bsn=None, asn=None):
+        k = bank[0] % 8
+        bank[0] += 1
+        out = O("ps%d" % k, 0, hi - lo)
+        full = (out[0], [("ps%d" % k, 0, 512, 1, 0)])
+        a, s = O(an, alo, alo + 128), O(asn or an + "s", alo, alo + 128)
+        b, p = O(bn, lo, hi), O(bsn, lo, hi)
+        run("t", [full], [a, s, b, p], lambda: g.tensor.matmul_mx(out[0], a[0], s[0], b[0], p[0], True, True))
+        return full
+
+    def load(q, name, src, lo, hi, fn=None):
+        o = O(name, lo, hi)
+        return (q, (fn(o) if fn else o)[0], src, o[1], [])
+
+    dmas("dpg", [load("y", "pgi", T.pg[:], 0, 20)])
+    dmas("dog", [("s" if d else "y", T.ogi[2 * k + d:128:16, 0:20], T.og[16 * k + d:16 * k + 16:2, 0:20], [("ogi", 0, 20, 1, 0)], [])
+                 for k in range(8) for d in range(2)])
+    dmas("du", [load("s", "ut", T.u[:], 0, 512)])
+    dmas("dxa", [load("y", "xt0", T.x[:, 0:768], 0, 768)])
+    dmas("dxb", [load("y", "xt0", T.x[:, 768:1280], 768, 1280)])
+
+    AND, SHR, EQ, NE, GE, LT = (AluOpType.bitwise_and, AluOpType.arith_shift_right, AluOpType.is_equal, AluOpType.not_equal,
+                                AluOpType.is_ge, AluOpType.is_lt)
+
+    def select(out, in_, pattern, fill, base=0, mul=0):
+        run("g", [out], [in_], lambda: g.affine_select(out[0], in_[0], pattern, EQ, fill, base, mul))
+
+    iota(O("pint"), [[1, 1]], 0, 1)
+    iota(O("mi"), [[0, 8], [16, 3]], 0, 0)
+    iota(O("pi0"), [[2, 2], [4, 4], [256, 3]], 0, 0)
+    iota(O("i320"), [[1, 320]], -160, 0)
+    iota(O("ja", 0, 40), [[1, 2], [16, 20]], 0, 0)
+    iota(O("ja", 40, 48), [[16, 8]], 0, 0)
+    iota(O("w320"), [[320, 8]], 160, 0)
+    iota(O("upi"), [[0, 2], [16, 8]], 0, 0)
+    iota(O("i16"), [[0, 24], [1, 16]], -2097152, 0)
+    select(O("r16"), O("i16"), [[0, 24], [1, 16]], 2.0 * BIG)
+    for b in range(4):
+        if b == 0:
+            run("v", [O("ones")], [], lambda: g.vector.memset(O("ones")[0], 1.0))
+        select(O("ec", 512 * b, 512 * b + 512), O("ones"), [[-1, 512]], 0.0, b, 4)
+
+    ts(O("lanei"), O("pint"), 15, None, AND)
+    ts(O("hi"), O("pint"), 4, None, SHR)
+    ts(O("xi"), O("pint"), 7, None, AND)
+    copy(O("lanef"), O("lanei"))
+    copy(O("hf"), O("hi"))
+    ts(O("h8"), O("hf"), 8.0, None, ADD)
+    ts(O("lan16"), O("lanef"), 16.0, None, MUL)
+    ts(O("pi1"), O("mi"), O("lanef"), None, ADD)
+    ts(O("ge20"), O("pi1"), 20.0, -319.0, GE, MUL)
+    ts(O("ge40"), O("pi1"), 40.0, -321.0, GE, MUL)
+    tt(O("ge20"), O("ge20"), O("ge40"), ADD)
+    ts(O("pi2"), O("pi0"), O("lan16"), None, ADD)
+    tt(O("pi2"), O("pi2"), O("ge20"), ADD)
+    copy(O("cl"), O("pi2"))
+    ts(O("h2"), O("hf"), 2.0, -160.0, MUL, ADD)
+    ts(O("jf"), O("ja"), O("h2"), None, ADD)
+    tt(O("sxi"), O("hi"), O("xi"), SUB)
+    ts(O("sx7"), O("sxi"), 7, None, AND)
+    ts(O("ux"), O("sx7"), -320.0, -160.0, MUL, ADD)
+    ts(O("lanem"), O("lanef"), -BIG, 2.0 * BIG * BIG, MUL, ADD)
+    act(O("msk"), O("i16"), FN.Abs, BIG, O("lanem"))
+    copy(O("pgu"), O("pgi"))
+    copy(O("P", 0, 320), by(O("i320"), O("pgu")))
+    items = []
+    for s in range(1, 8):
+        w = [("P", 320 * s, 320 * s + 320, 1, 0)]
+        r = [("P", 0, 320, 1, 0)]
+        q = "y" if s % 2 else "s"
+        items.append((q, T.P[16 * s:128, 320 * s:320 * s + 320], T.P[0:128 - 16 * s, 0:320], w, r))
+        items.append((q, T.P[0:16 * s, 320 * s:320 * s + 320], T.P[128 - 16 * s:128, 0:320], w, r))
+    dmas("dp", items)
+    dmas("dw", [("y", codes(O("wq"))[0], T.wc[:], O("wq")[1], []), ("y", O("wqs")[0], T.ws[:], O("wqs")[1], [])])
+    dmas("dv", [load("y", "vt", T.v[:], 0, 512)])
+
+    ts(O("ogr"), O("ogi"), -1.0, O("h8"), MUL, ADD)
+    ts(O("og7"), O("ogr"), 7, None, AND)
+    copy(O("ogu"), O("og7"))
+    copy(O("lab"), by(O("w320"), O("ogu")), "s")
+    tt(O("N"), by(O("lab"), O("cl")), O("msk"), SUB)
+    copy(O("un"), by(O("lab"), O("cl")), "s")
+    act(O("ka"), O("un"), FN.Abs, 1.0, O("ux"))
+    act(O("K"), O("ka"), FN.Relu, -1.0, 1.0)
+
+    def scores(t, piece):
+        lo, hi = CH[piece]
+        for s in range(8):
+            p = mx("uw", 16 * (8 - s), "qc%d" % t, lo, hi, "qs%d" % t)
+            q = "v" if t and piece and s % 2 else "s"
+            copy(O("ST", 320 * s + lo, 320 * s + hi), (p[0], p[1]), q)
+
+    partner = [T.cores[rank ^ s] for s in STEP]
+
+    def send(t, out, in_, sem):
+        rid, pid, _s = topo.addr(partner[t])
+        eng = topo.engines(core, partner[t])
+        order("g", in_[1], [])
+        g.remote_dma(out[0], in_[0], T.sem[sem], T.sem.left, pid=pid, routing_id=rid, dma_engine_mask=sum(1 << e for e in eng))
+        total["left"] += len(eng)
+        return len(eng)
+
+    def send_state(t):
+        n = send(t, codes(O("lc%d" % t)), codes(O("qc%d" % t)), "rq%d" % t)
+        n += send(t, O("lp%d" % t), O("qs%d" % t), "rq%d" % t)
+        arrives("rq%d" % t, n, [O("lc%d" % t), O("lp%d" % t)])
+
+    def P_by(k, name="off"):
+        return by(O("P"), O(name, 4 * k, 4 * k + 3))
+
+    def place(name, k):
+        return O(name, 48 * slot(k), 48 * slot(k) + 48)
+
+    def walk(start, k0, beside):
+        tt(O("G"), start, place("N", k0), ADD)
+        for call in beside[0]:
+            call()
+        for k in range(k0, 8):
+            scan(O("SC"), O("r16", 0, 48), O("G"))
+            copy(O("off", 4 * k, 4 * k + 3), O("SC", 15, 48, 16))
+            if k < 7:
+                tt(O("G"), P_by(k), place("N", k + 1), ADD)
+            for call in beside[k - k0 + 1]:
+                call()
+
+    first = [0, 1, 0]
+    FROM, NX, NY = ["jf", "sa0", "jf"], ["x0", "sb0", "sa0"], ["y0", "y1", "sa1"]
+
+    def ahead(t):
+        f = first[t]
+        return [lambda: tt(O("G2"), O(FROM[t]), place("N", f + 1), ADD),
+                lambda: scan(O("SC2"), O("r16", 0, 48), O("G2")),
+                lambda: copy(O("of2", 0, 3), O("SC2", 15, 48, 16)),
+                lambda: tt(O("G2"), P_by(0, "of2"), place("N", f), ADD),
+                lambda: copy(O("X1"), P_by(0, "of2"), "s"),
+                lambda: scan(O("SC2"), O("r16", 0, 48), O("G2")),
+                lambda: tt(O("DX"), O("X1"), O(NX[t]), SUB),
+                lambda: copy(O("of2", 4, 7), O("SC2", 15, 48, 16)),
+                lambda: copy(O("Y1"), P_by(1, "of2"), "s"),
+                lambda: tt(O("DY"), O("Y1"), O(NY[t]), SUB)]
+
+    def address(t, k):
+        if k in (first[t], first[t] + 1):
+            return O(("sa%d" if k == first[t] else "sb%d") % t)
+        return O("sa0") if k < first[t] else P_by(k)
+
+    def score_places(t, k):
+        tt(place("VF", k), P_by(k) if t < 0 else address(t, k), place("N", k), ADD)
+
+    def score_list(t):
+        scan(O("SF"), O("r16"), O("VF"))
+        if t == 1:
+            copy(O("fl1", 1, 13), O("SF", 15, 192, 16))
+            copy(O("fl1", 14, 26), O("SF", 207, 384, 16))
+        else:
+            copy(O("fl%d" % t, 0, 24), O("SF", 15, 384, 16))
+
+
+    def sides(t):
+        return ((192, 336), (48, 192)) if t == 1 else ((0, 192), (192, 384))
+
+    def differences(t):
+        a, b = sides(t)
+        n = a[1] - a[0]
+        return [lambda: tt(O("DN", 0, n), O("N", *b), O("N", *a), SUB),
+                lambda: act(O("KC", 0, n), O("K", *b), FN.Identity, 2.0, -1.0),
+                lambda: tt(O("KA", 0, n), O("KC", 0, n), O("K", *a), ADD),
+                lambda: act(O("KB", 0, n), O("KA", 0, n), FN.Identity, -1.0, 1.0)]
+
+    def exchange(t):
+        a, b = sides(t)
+        n = a[1] - a[0]
+        return [lambda: tt(O("MN", 0, n), O("DN", 0, n), O("CC", 0, n), MUL),
+                lambda: tt(O("N", *a), O("N", *a), O("MN", 0, n), ADD),
+                lambda: tt(O("N", *b), O("N", *b), O("MN", 0, n), SUB),
+                lambda: tt(O("K", *a), O("KA", 0, n), O("CC", 0, n), EQ),
+                lambda: tt(O("K", *b), O("KB", 0, n), O("CC", 0, n), EQ)]
+
+    def choose(t):
+        return [lambda: tt(O("MB"), O("DY"), O("CC", 0, 48), MUL),
+                lambda: tt(O("sb%d" % t), O(NY[t]), O("MB"), ADD),
+                lambda: tt(O("MA"), O("DX"), O("CC", 0, 48), MUL),
+                lambda: tt(O("sa%d" % t), O(NX[t]), O("MA"), ADD)]
+
+    def pick(t, k):
+        tt(O("VV", k, 384, 8), address(t, k), place("K", k), MUL)
+
+    def spread(sem, out, in_, qs):
+        dmas(sem, [(qs[i % len(qs)], T[out][16 * i:16 * i + 16, 0:20], T[in_][i:128:16, 0:40], [(out, 0, 20, 1, 0)], [(in_, 0, 40, 1, 0)])
+                   for i in range(8)])
+
+    def unpack(t, name, cn, sn):
+        for b in range(4):
+            p = mx("eq", 128 * b, cn, 0, 320, sn)
+            copy(O("%s%d" % (name, t), 320 * b, 320 * b + 320), p, "s")
+
+    sp, df, vf = ahead(0), differences(0), [lambda k=k: score_places(-1, k) for k in range(8)]
+    walk(O("jf"), 0, [
+        [lambda: copy(O("upu"), O("upi")), lambda: quant("uq", "uqs", "ut", 0, 128)],
+        [lambda: copy(words(O("uw")), by(words(O("uq")), O("upu"))), sp[0]],
+        [lambda: quant("qc0", "qs0", "xt0", *CH[0]), lambda: quant("qc0", "qs0", "xt0", *CH[1]), sp[1],
+         lambda: copy(O("uws"), by(O("uqs"), O("upu")), "s"), lambda: scores(0, 0)],
+        [lambda: copy(O("x0"), P_by(0), "s"), lambda: copy(O("y0"), P_by(1), "s"), df[1], sp[2], df[0]],
+        [sp[3], sp[4], lambda: scores(0, 1), vf[0], vf[1]],
+        [sp[5], vf[2], vf[3], sp[6]],
+        [sp[7], df[2], vf[4]],
+        [df[3], sp[8], vf[5]],
+        [vf[6], vf[7]]])
+    score_list(0)
+    sp[9]()
+    send_state(0)
+    quant("eq", "eqs", "ec", 0, 512)
+    iota(O("i8"), [[0, 40], [1, 8]], 0, 0)
+    select(O("r8"), O("i8"), [[0, 40], [1, 8]], 1.0)
+    iota(O("wone"), [[1, 8]], 0, 0)
+    iota(O("lm"), [[1, 2], [2, 4], [0, 48]], 0, 0)
+
+    for t in range(3):
+        n = sides(t)[0][1] - sides(t)[0][0]
+        unpack(t, "fo", "qc%d" % t, "qs%d" % t)
+        unpack(t, "fp", "lc%d" % t, "lp%d" % t)
+        one, two = ((14, 23), (4, 13)) if t == 1 else ((0, 12), (12, 24))
+        copy(O("E", 0, n), by(O("ST"), O("fl%d" % t, *one)))
+        tt(O("CC", 0, n), by(O("ST"), O("fl%d" % t, *two)), O("E", 0, n), LT)
+        ex, ch = exchange(t), choose(t)
+        for call in (ex[0], ch[0], ex[1], ch[1]):
+            call()
+        p = [lambda k=k: pick(t, k) for k in range(8)]
+        if t == 1:
+            walk(O("sb1"), 3, [ex[2:3], ex[3:4], ex[4:5] + ch[2:3], ch[3:4] + p[3:5], [p[0], p[1], p[2], p[5], p[6]], p[7:]])
+        else:
+            walk(O("sb%d" % t), 2, [ex[2:3], ex[3:4], ex[4:5] + ch[2:3], ch[3:4] + p[2:4], [p[0], p[1], p[4]], p[5:7], p[7:]])
+        run("v", [O("SV")], [O("r8"), O("VV", 0, 320)],
+            lambda: g.vector.tensor_tensor_scan(O("SV")[0], O("r8")[0], O("VV", 0, 320)[0], 0.0, MUL, ADD))
+        ts(O("ml%d" % t), O("SV", 7, 320, 8), 160.0, None, ADD)
+        k = send(t, O("ll%d" % t), O("ml%d" % t), "rl%d" % t)
+        arrives("rl%d" % t, k, [O("ll%d" % t)])
+        spread("own%d" % t, "al%d" % t, "ml%d" % t, "y")
+        if t < 2:
+            if t == 0:
+                copy(O("y1"), P_by(2), "s")
+            sp, df, vf = ahead(t + 1), differences(t + 1), [lambda k=k: score_places(t, k) for k in range(8)]
+            for call in (df[1:2] + sp[0:1] + vf[0:2] + sp[1:2] + vf[2:4] + sp[2:3] + df[2:3] + sp[3:5] + df[3:4] + vf[4:5] + sp[5:6] + vf[5:7]
+                         + sp[7:9] + vf[7:8] + sp[6:7] + df[0:1]):
+                call()
+            score_list(t + 1)
+            sp[9]()
+        else:
+            scan(O("SF"), O("r16"), O("N"))
+            ts(O("ls0"), O("SF", 15, 384, 16), -160.0, 1.0 / 320.0, ADD, MUL)
+            ts(O("ls1"), O("ls0"), -1.0, O("h8"), MUL, ADD)
+            ts(O("ls2"), O("ls1"), 7, None, AND)
+            copy(O("gw"), O("ls2"))
+            tt(O("o1"), by(O("wone"), O("gw")), O("lm"), MUL)
+            tt(O("o2"), O("o1", 0, 192), O("o1", 192, 384), ADD)
+            tt(O("o3"), O("o2", 0, 96), O("o2", 96, 192), ADD)
+            tt(O("o4"), O("o3", 0, 48), O("o3", 48, 96), ADD)
+            copy(O("ol40"), O("o4", 0, 40))
+        tt(O("BG"), by(O("P", 0, 320), O("al%d" % t)), O("msk", 0, 320), SUB)
+        scan(O("BS"), O("r16", 0, 320), O("BG"))
+        ts(O("bl%d" % t), O("BS", 15, 320, 16), 160.0, None, ADD)
+        spread("par%d" % t, "pl%d" % t, "ll%d" % t, "ys")
+        if t == 2:
+            spread("do1", "ow", "ol40", "y")
+        for lo, hi in CH:
+            off = O("pl%d" % t, lo // 16, hi // 16)
+            for b in range(4):
+                copy(O("zt%d" % t, 4 * lo + b, 4 * hi, 4), by(O("fp%d" % t, 320 * b, 320 * b + 320), off), "v" if b < 2 else "s")
+            quant("zc%d" % t, "zs%d" % t, "zt%d" % t, lo, hi)
+        if t == 0:
+            quant("vq", "vqs", "vt", 0, 128)
+            copy(O("xf"), O("xi"))
+            ts(O("lm"), O("lm"), O("xf"), None, EQ)
+        for lo, hi in CH:
+            for b in range(4):
+                p = mx("wq", 128 * b, "zc%d" % t, lo, hi, "zs%d" % t)
+                o = O("rb%d" % b, lo, hi)
+                run("s", [o], [p], lambda o=o, p=p: g.scalar.activation(o[0], p[0], COPY, scale=0.03125))
+        for i, (lo, hi) in enumerate(CH):
+            off = O("bl%d" % t, lo // 16, hi // 16)
+            for b in range(4):
+                tt(O("xt%d" % (t + 1), 4 * lo + b, 4 * hi, 4), by(O("rb%d" % b), off), O("fo%d" % t, 320 * b + lo, 320 * b + hi), ADD)
+            quant("qc%d" % (t + 1), "qs%d" % (t + 1), "xt%d" % (t + 1), lo, hi)
+            if t < 2 and i == 0:
+                scores(t + 1, 0)
+        if t < 2:
+            send_state(t + 1)
+            scores(t + 1, 1)
+        else:
+            copy(O("olf"), by(O("wone"), O("ow")))
+    outs = []
+    for lo, hi in CH:
+        o = O("qc3", lo, hi)
+        outs.append(("y", T.oc[:, 4 * lo:4 * hi], codes(o)[0], [], o[1]))
+    for k in range(4):
+        outs.append(("y", T.osc[4 * k:4 * k + 4, 0:320], T.qs3[32 * k:32 * k + 4, 0:320], [], O("qs3")[1]))
+    outs.append(("y", T.ol[:], T.olf[0:128:16, 0:320], [], O("olf")[1]))
+    for lo, hi in CH:
+        p = mx("vq", 0, "qc3", lo, hi, "qs3")
+        o = O("yb", lo, hi)
+        copy(o, p, "s")
+        outs.append(("s", T.y[:, lo:hi], o[0], [], o[1]))
+    dmas("dout", outs)
+    for s in SEMAPHORES:
+        if total[s]:
+            g.wait_ge(T.sem[s], total[s])

@@ -2,11 +2,17 @@ from concourse.mybir import dt, AluOpType, ActivationFunctionType
 
 FN = ActivationFunctionType
 COPY = FN.Copy
-ADD, SUB, MUL, MAX, MIN = AluOpType.add, AluOpType.subtract, AluOpType.mult, AluOpType.max, AluOpType.min
+A = AluOpType
+ADD, SUB, MUL, MAX, MIN = A.add, A.subtract, A.mult, A.max, A.min
+AND, SHR, NE, GE, LT, EQ = A.bitwise_and, A.arith_shift_right, A.not_equal, A.is_ge, A.is_lt, A.is_equal
 BIG = 1048576.0
-C = 320
+RISE = 8192.0
+FAR = 1e29
 STEP = [1, 2, 4]
-CH = [(0, 192), (192, 320)]
+SQ = ["s", "vvsvsvsv"]
+RQ = ["ssss", "vvss"]
+ZCH = [(0, 192), (192, 320)]
+CH = [(0, 128), (128, 320)]
 
 SCRATCH = {}
 
@@ -22,29 +28,29 @@ def _share(buf, dtype, *parts):
     at = 0
     for n, c in parts:
         ALIAS[n] = (buf, at, c)
-        at += c + c % 2
+        at += c + (-c) % 8
     _d(buf, at, dtype)
 
 
-_share("iv", "int32", ("pint", 1), ("lanei", 1), ("hi", 1), ("xi", 1), ("sxi", 1), ("sx7", 1), ("upi", 16), ("mi", 24), ("pi0", 24), ("pi1", 24), ("pi2", 24))
-_share("iw", "int32", ("ogr", 20), ("og7", 20), ("ls0", 24), ("ls1", 24), ("ls2", 24))
-_share("fv", "float32", ("lanef", 1), ("hf", 1), ("h8", 1), ("h2", 1), ("ux", 1), ("xf", 1), ("lan16", 1), ("lanem", 1), ("ge20", 24), ("ge40", 24), ("ja", 48), ("jf", 48))
-_share("uv", "uint16", ("pgu", 20), ("ogu", 20), ("upu", 16), ("cl", 24), ("gw", 24))
-_share("wv", "float32", *[(n, 48) for n in ("x0", "y0", "y1", "X1", "Y1", "DX", "DY", "MA", "MB", "sa0", "sb0", "sa1", "sb1", "sa2", "sb2")])
-_d("pgi", 20, "int32")
+_share("iv", "int32", ("pint", 1), ("lanei", 1), ("hi", 1), ("xi", 1), ("sxi", 1), ("sx7", 1), ("upi", 16), ("mi", 24), ("pi0", 24),
+       ("pi1", 24), ("pi2", 24), ("t8", 8), ("t8a", 8), ("t8b", 8))
+_share("fv", "float32", ("lanef", 1), ("hf", 1), ("h2", 1), ("ux", 1), ("kap", 1), ("lan16", 1), ("ge20", 24), ("ge40", 24), ("ja", 48),
+       ("jf", 48), ("i16", 16), ("z16", 16), ("t320", 8), ("tone", 8), ("wd", 16), ("r3", 9), ("z24", 24))
+_share("ov", "float32", ("W", 80), ("a2", 8), ("DF", 24), ("L", 24), ("M", 12), ("d0", 80), ("d1", 80), ("SS", 80),
+       ("a1", 6), ("e1", 3), ("e3", 3), ("k1", 3), ("k2", 3), ("dB", 3), ("xB", 3))
+_share("uv", "uint16", ("ogu", 20), ("upu", 16), ("cl", 24), ("ln", 24), ("rl", 24), ("sl", 12), ("lu", 24), ("ow", 20))
+_share("wv", "float32", ("SG", 48), ("SC", 48), ("G2", 96), ("T1", 96), ("T2", 96), ("T3", 96), ("T4", 96))
+_d("pgi", 40, "int32")
 _d("ogi", 20, "int32")
-for _n, _c in (("i16", 384), ("i8", 320), ("w320", 8), ("wone", 8),
-               ("un", 384), ("ka", 384), ("msk", 384), ("r16", 384), ("r8", 320), ("lab", 320),
-               ("N", 384), ("K", 384), ("DN", 192), ("KA", 192), ("KB", 192), ("KC", 192), ("MN", 192), ("E", 192), ("CC", 192),
-               ("G", 48), ("SC", 48), ("G2", 48), ("SC2", 48), ("VV", 384), ("SV", 320), ("VF", 384), ("SF", 384), ("ST", 2560), ("BG", 320), ("BS", 320),
-               ("rb0", 320), ("rb1", 320), ("rb2", 320), ("rb3", 320), ("lm", 384), ("o1", 384), ("o2", 192), ("o3", 96), ("o4", 48),
-               ("olf", 320), ("yb", 320)):
+for _n, _c in (("i320", 320), ("rise", 384), ("zero", 192), ("cap", 192), ("pats", 384), ("patx", 384), ("gpat", 192), ("c0", 192), ("cpat", 192),
+               ("lab", 320), ("NB", 384), ("ND", 384), ("E", 192), ("CC", 192), ("FL", 200), ("G", 64), ("VAL", 384), ("SF", 384), ("sel", 192), ("selx", 192),
+               ("PN", 192), ("PC", 192), ("PS", 2560), ("ST", 2560), ("BG", 320), ("BS", 320), ("one", 320),
+               ("rb0", 320), ("rb1", 320), ("rb2", 320), ("rb3", 320), ("olf", 320), ("yb", 320)):
     _d(_n, _c, "float32")
-for _n, _c in (("off", 32), ("of2", 8), ("fl0", 26), ("fl1", 26), ("fl2", 26), ("ol40", 40), ("ow", 20)):
+for _n, _c in (("pu", 160), ("off", 26), ("of2", 26), ("ndu", 24), ("pos", 24), ("fl0", 26), ("fl1", 26), ("fl2", 26)):
     _d(_n, _c, "uint16")
 for _t in range(3):
-    _d("ml%d" % _t, 40, "uint16")
-    _d("ll%d" % _t, 40, "uint16")
+    _d("ml%d" % _t, 384, "uint16")
     _d("al%d" % _t, 20, "uint16")
     _d("pl%d" % _t, 20, "uint16")
     _d("bl%d" % _t, 20, "uint16")
@@ -59,7 +65,7 @@ for _t in range(4):
     _d("xt%d" % _t, 1280, "bfloat16")
     _d("qc%d" % _t, 320, "float8_e4m3fn_x4")
     _d("qs%d" % _t, 320, "uint8")
-for _n, _c in (("i320", 320), ("P", 2560), ("ones", 512), ("ec", 2048), ("ut", 512), ("vt", 512)):
+for _n, _c in (("ones", 512), ("ec", 2048), ("ut", 512), ("vt", 512), ("OB", 384), ("owb", 20)):
     _d(_n, _c, "bfloat16")
 for _n, _c in (("eq", 512), ("wq", 512), ("uq", 128), ("uw", 256), ("vq", 128)):
     _d(_n, _c, "float8_e4m3fn_x4")
@@ -67,7 +73,7 @@ for _n, _c in (("eq", 512), ("wq", 512), ("uq", 128), ("uw", 256), ("vq", 128)):
 for _k in range(8):
     _d("ps%d" % _k, 512, "float32", "psum")
 
-DMA_SEMS = ["dpg", "dog", "du", "dxa", "dxb", "dw", "dv", "dp", "own0", "own1", "own2", "par0", "par1", "par2", "do1", "do2", "dout"]
+DMA_SEMS = ["dpg", "dog", "du", "dxa", "dxb", "dw", "dv", "own0", "own1", "own2", "do1", "dout"]
 SEMAPHORES = ["cv", "cs", "ct", "cg", "left", "rq0", "rq1", "rq2", "rl0", "rl1", "rl2"] + DMA_SEMS
 
 
@@ -84,13 +90,13 @@ def rank_program(g, core, T, topo):
     clock = {q: {} for q in queue}
     wrote, read = {}, {}
 
-    def O(name, lo=0, hi=None, step=1):
+    def O(name, lo=0, hi=None, step=1, rows=(0, 128)):
         if name in ALIAS:
             name, at, n = ALIAS[name]
             lo, hi = at + lo, at + (n if hi is None else hi)
         hi = SCRATCH[name][1][1] if hi is None else hi
-        ap = T[name][:, lo:hi] if step == 1 else T[name][:, lo:hi:step]
-        return (ap, [(name, lo, hi, step, lo % step)])
+        ap = T[name][rows[0]:rows[1], lo:hi] if step == 1 else T[name][rows[0]:rows[1], lo:hi:step]
+        return (ap, [(name, lo, hi, step, lo % step) + rows])
 
     def codes(o):
         return (o[0].bitcast(dt.uint8), o[1])
@@ -102,7 +108,10 @@ def rank_program(g, core, T, topo):
         return (win[0].indirect(off[0]), win[1] + off[1])
 
     def meet(a, b):
-        return a[1] < b[2] and b[1] < a[2] and not (a[3] == b[3] > 1 and a[4] != b[4])
+        return a[1] < b[2] and b[1] < a[2] and a[5] < b[6] and b[5] < a[6] and not (a[3] == b[3] > 1 and a[4] != b[4])
+
+    def covers(w, o):
+        return w[3] == 1 and w[1] <= o[1] and o[2] <= w[2] and w[5] <= o[5] and o[6] <= w[6]
 
     def order(q, reads, writes, dma=False):
         evs = []
@@ -128,10 +137,9 @@ def rank_program(g, core, T, topo):
         for r in reads:
             read.setdefault(r[0], []).append((r, ev))
         for w in writes:
-            old = wrote.get(w[0], [])
-            wrote[w[0]] = [(o, e) for o, e in old if not (w[3] == 1 and w[1] <= o[1] and o[2] <= w[2])] + [(w, ev)]
+            wrote[w[0]] = [(o, e) for o, e in wrote.get(w[0], []) if not covers(w, o)] + [(w, ev)]
             if w[0] in read:
-                read[w[0]] = [(o, e) for o, e in read[w[0]] if not (w[3] == 1 and w[1] <= o[1] and o[2] <= w[2])]
+                read[w[0]] = [(o, e) for o, e in read[w[0]] if not covers(w, o)]
 
     def run(q, outs, ins, call):
         reads = [r for o in ins for r in o[1]]
@@ -177,16 +185,21 @@ def rank_program(g, core, T, topo):
         else:
             run("v", [out], ins, lambda: g.vector.tensor_scalar(out[0], a[0], v1, v2, op0, op1))
 
-    def act(out, in_, func, scale, bias):
-        col = isinstance(bias, tuple)
-        run("s", [out], [in_] + [bias] * col, lambda: g.scalar.activation(out[0], in_[0], func, bias=bias[0] if col else bias, scale=scale))
+    def act(out, in_, scale, bias):
+        run("s", [out], [in_], lambda: g.scalar.activation(out[0], in_[0], FN.Identity, bias=bias, scale=scale))
 
-    def scan(out, reset, data):
-        run("v", [out], [reset, data], lambda: g.vector.tensor_tensor_scan(out[0], reset[0], data[0], -2.0 * BIG, MIN, MAX))
+    def scan(out, d0, d1, op0=ADD, op1=MAX, first=0.0):
+        run("v", [out], [d0, d1], lambda: g.vector.tensor_tensor_scan(out[0], d0[0], d1[0], first, op0, op1))
 
-    def iota(out, pattern, base, mul):
+    def fill(out, value):
+        run("v", [out], [], lambda: g.vector.memset(out[0], value))
+
+    def iota(out, pattern, base, mul=0):
         kw = {} if SCRATCH[out[1][0][0]][2] == "int32" else {"allow_small_or_imprecise_dtypes": True}
         run("g", [out], [], lambda: g.iota(out[0], pattern, base, mul, **kw))
+
+    def select(out, in_, pattern, fill_, base=0, mul=0, op=EQ):
+        run("g", [out], [in_], lambda: g.affine_select(out[0], in_[0], pattern, op, fill_, base, mul))
 
     def quant(cn, sn, xn, lo, hi):
         q, s, x = O(cn, lo, hi), O(sn, lo, hi), O(xn, 4 * lo, 4 * hi)
@@ -198,93 +211,116 @@ def rank_program(g, core, T, topo):
         k = bank[0] % 8
         bank[0] += 1
         out = O("ps%d" % k, 0, hi - lo)
-        full = (out[0], [("ps%d" % k, 0, 512, 1, 0)])
+        full = (out[0], O("ps%d" % k)[1])
         a, s = O(an, alo, alo + 128), O(asn or an + "s", alo, alo + 128)
         b, p = O(bn, lo, hi), O(bsn, lo, hi)
         run("t", [full], [a, s, b, p], lambda: g.tensor.matmul_mx(out[0], a[0], s[0], b[0], p[0], True, True))
         return full
 
-    def load(q, name, src, lo, hi, fn=None):
-        o = O(name, lo, hi)
-        return (q, (fn(o) if fn else o)[0], src, o[1], [])
+    def narrow(out, wide):
+        ts(out, wide, O("kap"), None, SUB)
 
-    dmas("dpg", [load("y", "pgi", T.pg[:], 0, 20)])
-    dmas("dog", [("s" if d else "y", T.ogi[2 * k + d:128:16, 0:20], T.og[16 * k + d:16 * k + 16:2, 0:20], [("ogi", 0, 20, 1, 0)], [])
-                 for k in range(8) for d in range(2)])
-    dmas("du", [load("s", "ut", T.u[:], 0, 512)])
+    def load(q, name, src, lo, hi, rows=(0, 128)):
+        o = O(name, lo, hi, 1, rows)
+        return (q, o[0], src, o[1], [])
+
+    dmas("dpg", [load("y", "pgi", T.pg[:], 0, 20), load("s", "pgi", T.pg[0:112, :], 20, 40, (16, 128)),
+                 load("y", "pgi", T.pg[112:128, :], 20, 40, (0, 16))])
+    dmas("dog", [("s" if k % 2 else "y", T.ogi[k:128:8, 0:20], T.og[16 * k:16 * k + 16, 0:20], O("ogi")[1] if k == 0 else [], [])
+                 for k in range(8)])
     dmas("dxa", [load("y", "xt0", T.x[:, 0:768], 0, 768)])
+    dmas("du", [load("s", "ut", T.u[:], 0, 512)])
     dmas("dxb", [load("y", "xt0", T.x[:, 768:1280], 768, 1280)])
-
-    AND, SHR, EQ, NE, GE, LT = (AluOpType.bitwise_and, AluOpType.arith_shift_right, AluOpType.is_equal, AluOpType.not_equal,
-                                AluOpType.is_ge, AluOpType.is_lt)
-
-    def select(out, in_, pattern, fill, base=0, mul=0):
-        run("g", [out], [in_], lambda: g.affine_select(out[0], in_[0], pattern, EQ, fill, base, mul))
+    dmas("dw", [("y", codes(O("wq"))[0], T.wc[:], O("wq")[1], []), ("y", O("wqs")[0], T.ws[:], O("wqs")[1], [])])
+    dmas("dv", [load("y", "vt", T.v[:], 0, 512)])
 
     iota(O("pint"), [[1, 1]], 0, 1)
-    iota(O("mi"), [[0, 8], [16, 3]], 0, 0)
-    iota(O("pi0"), [[2, 2], [4, 4], [256, 3]], 0, 0)
-    iota(O("i320"), [[1, 320]], -160, 0)
-    iota(O("ja", 0, 40), [[1, 2], [16, 20]], 0, 0)
-    iota(O("ja", 40, 48), [[16, 8]], 0, 0)
-    iota(O("w320"), [[320, 8]], 160, 0)
-    iota(O("upi"), [[0, 2], [16, 8]], 0, 0)
-    iota(O("i16"), [[0, 24], [1, 16]], -2097152, 0)
-    select(O("r16"), O("i16"), [[0, 24], [1, 16]], 2.0 * BIG)
-    for b in range(4):
-        if b == 0:
-            run("v", [O("ones")], [], lambda: g.vector.memset(O("ones")[0], 1.0))
-        select(O("ec", 512 * b, 512 * b + 512), O("ones"), [[-1, 512]], 0.0, b, 4)
+    iota(O("i16"), [[1, 16]], 0)
+    iota(O("t8"), [[-1, 8]], 8)
+    iota(O("mi"), [[0, 8], [16, 3]], 0)
+    iota(O("pi0"), [[1, 2], [2, 4], [256, 3]], 0)
+    fill(O("one"), 1.0)
+    fill(O("sel"), 193.0)
+    iota(O("pats", 0, 192), [[0, 8], [1, 3], [3, 8]], 0)
+    iota(O("pats", 192, 384), [[1, 8], [0, 24]], 0)
+    iota(O("upi"), [[0, 2], [16, 8]], 0)
+    iota(O("ja", 0, 40), [[1, 2], [16, 20]], 0)
+    iota(O("ja", 40, 48), [[16, 8]], 0)
+    iota(O("wd"), [[320, 16]], -2240)
+    iota(O("sel", 1, 75, 5), [[0, 5], [16, 3]], 15)
+    iota(O("sel", 2, 75, 5), [[0, 5], [16, 3]], 63)
+    iota(O("sel", 99, 171, 5), [[0, 5], [16, 3]], 15)
+    iota(O("sel", 100, 141, 5), [[48, 3], [16, 3]], 15)
+    iota(O("c0"), [[0, 8], [16, 3], [0, 8]], 336)
+    select(O("cpat"), O("c0"), [[0, 24], [1, 8]], -48.0, -7)
+    iota(O("ones"), [[0, 512]], 1)
 
     ts(O("lanei"), O("pint"), 15, None, AND)
     ts(O("hi"), O("pint"), 4, None, SHR)
     ts(O("xi"), O("pint"), 7, None, AND)
+    fill(O("off"), 0)
     copy(O("lanef"), O("lanei"))
     copy(O("hf"), O("hi"))
-    ts(O("h8"), O("hf"), 8.0, None, ADD)
+    tt(O("sxi"), O("hi"), O("xi"), SUB)
+    fill(O("sel", 0, 80, 5), 192.0)
+    ts(O("z16"), O("i16"), O("lanef"), None, NE)
+    ts(O("ln"), O("one", 0, 24), O("lanef"), None, MUL)
+    ts(O("t8a"), O("t8"), O("hf"), None, ADD)
     ts(O("lan16"), O("lanef"), 16.0, None, MUL)
     ts(O("pi1"), O("mi"), O("lanef"), None, ADD)
-    ts(O("ge20"), O("pi1"), 20.0, -319.0, GE, MUL)
-    ts(O("ge40"), O("pi1"), 40.0, -321.0, GE, MUL)
-    tt(O("ge20"), O("ge20"), O("ge40"), ADD)
-    ts(O("pi2"), O("pi0"), O("lan16"), None, ADD)
-    tt(O("pi2"), O("pi2"), O("ge20"), ADD)
-    copy(O("cl"), O("pi2"))
-    ts(O("h2"), O("hf"), 2.0, -160.0, MUL, ADD)
-    ts(O("jf"), O("ja"), O("h2"), None, ADD)
-    tt(O("sxi"), O("hi"), O("xi"), SUB)
+    scan(O("i320"), O("one"), O("one"), MUL, ADD, -1.0)
+    act(O("rise"), by(O("z16"), O("ln")), BIG + RISE, -BIG)
+    copy(O("zero"), by(O("z16"), O("ln", 0, 12)), "s")
+    act(O("cap"), by(O("z16"), O("ln", 0, 12)), -2 * FAR, FAR)
+    ts(O("t8b"), O("t8a"), 7, None, AND)
     ts(O("sx7"), O("sxi"), 7, None, AND)
-    ts(O("ux"), O("sx7"), -320.0, -160.0, MUL, ADD)
-    ts(O("lanem"), O("lanef"), -BIG, 2.0 * BIG * BIG, MUL, ADD)
-    act(O("msk"), O("i16"), FN.Abs, BIG, O("lanem"))
-    copy(O("pgu"), O("pgi"))
-    copy(O("P", 0, 320), by(O("i320"), O("pgu")))
-    items = []
-    for s in range(1, 8):
-        w = [("P", 320 * s, 320 * s + 320, 1, 0)]
-        r = [("P", 0, 320, 1, 0)]
-        q = "y" if s % 2 else "s"
-        items.append((q, T.P[16 * s:128, 320 * s:320 * s + 320], T.P[0:128 - 16 * s, 0:320], w, r))
-        items.append((q, T.P[0:16 * s, 320 * s:320 * s + 320], T.P[128 - 16 * s:128, 0:320], w, r))
-    dmas("dp", items)
-    dmas("dw", [("y", codes(O("wq"))[0], T.wc[:], O("wq")[1], []), ("y", O("wqs")[0], T.ws[:], O("wqs")[1], [])])
-    dmas("dv", [load("y", "vt", T.v[:], 0, 512)])
+    ts(O("ge20"), O("pi1"), 20.0, -312.0, GE, MUL)
+    ts(O("ge40"), O("pi1"), 40.0, -328.0, GE, MUL)
+    ts(O("pi2"), O("pi0"), O("lan16"), None, ADD)
+    ts(O("t320"), O("t8b"), 320.0, None, MUL)
+    ts(O("kap"), O("lanef"), -RISE, 15 * RISE, MUL, ADD)
+    tt(O("ge20"), O("ge20"), O("ge40"), ADD)
+    ts(O("h2"), O("hf"), 2.0, None, MUL)
+    ts(O("ux"), O("sx7"), 320.0, None, MUL)
+    copy(O("tone"), O("t8b"))
+    tt(O("pi2"), O("pi2"), O("ge20"), ADD)
+    fill(O("ov", 0, 112), 0.0)
+    scan(O("patx"), O("rise"), O("pats"))
+    copy(O("cl"), O("pi2"))
+    fill(O("FL", 192, 193), 0.0)
+    fill(O("FL", 193, 200), 1.0)
+    narrow(O("rl"), O("patx", 15, 384, 16))
+    for b in range(4):
+        select(O("ec", 512 * b, 512 * b + 512), O("ones"), [[-1, 512]], 0.0, b, 4)
 
-    ts(O("ogr"), O("ogi"), -1.0, O("h8"), MUL, ADD)
-    ts(O("og7"), O("ogr"), 7, None, AND)
-    copy(O("ogu"), O("og7"))
-    copy(O("lab"), by(O("w320"), O("ogu")), "s")
-    tt(O("N"), by(O("lab"), O("cl")), O("msk"), SUB)
-    copy(O("un"), by(O("lab"), O("cl")), "s")
-    act(O("ka"), O("un"), FN.Abs, 1.0, O("ux"))
-    act(O("K"), O("ka"), FN.Relu, -1.0, 1.0)
+    copy(O("pu", 0, 40), O("pgi"))
+    for q in range(4):
+        copy(O("pu", 40, 80, 1, (32 * q, 32 * q + 32)), O("pgi", 0, 40, 1, (32 * ((q - 1) % 4), 32 * ((q - 1) % 4) + 32)))
+    copy(O("ogu"), O("ogi"))
+    copy(O("upu"), O("upi"))
+    for q in range(2):
+        copy(O("pu", 80, 160, 1, (64 * q, 64 * q + 64)), O("pu", 0, 80, 1, (64 - 64 * q, 128 - 64 * q)))
 
-    def scores(t, piece):
+    def table(s, q):
+        o, i = O("PS", 320 * s, 320 * s + 320), by(O("i320"), O("pu", 20 * s, 20 * s + 20))
+        if q == "v":
+            ts(o, i, 320.0 * s, None, ADD)
+        else:
+            act(o, i, 1.0, 320.0 * s)
+
+    copy(O("lab"), by(O("t320"), O("ogu")), "s")
+    copy(O("NB"), by(O("lab"), O("cl")), "s")
+    for s in range(0, 4):
+        table(s, "v")
+    for s in (4, 6, 7):
+        table(s, "s")
+    ts(O("jf"), O("ja"), O("h2"), None, ADD)
+
+    def scores(t, piece, qs):
         lo, hi = CH[piece]
         for s in range(8):
             p = mx("uw", 16 * (8 - s), "qc%d" % t, lo, hi, "qs%d" % t)
-            q = "v" if t and piece and s % 2 else "s"
-            copy(O("ST", 320 * s + lo, 320 * s + hi), (p[0], p[1]), q)
+            copy(O("ST", 320 * s + lo, 320 * s + hi), p, qs[s % len(qs)])
 
     partner = [T.cores[rank ^ s] for s in STEP]
 
@@ -301,202 +337,214 @@ def rank_program(g, core, T, topo):
         n += send(t, O("lp%d" % t), O("qs%d" % t), "rq%d" % t)
         arrives("rq%d" % t, n, [O("lc%d" % t), O("lp%d" % t)])
 
-    def P_by(k, name="off"):
-        return by(O("P"), O(name, 4 * k, 4 * k + 3))
+    def col(k):
+        return 22 if k == 7 else 3 * slot(k)
 
-    def place(name, k):
-        return O(name, 48 * slot(k), 48 * slot(k) + 48)
+    def off(k):
+        return O("off", col(k), col(k) + 3)
 
-    def walk(start, k0, beside):
-        tt(O("G"), start, place("N", k0), ADD)
-        for call in beside[0]:
+    def place(name, k, before=0):
+        return O(name, 48 * slot(k) - before, 48 * slot(k) + 48)
+
+    def kept(name, lo=0, hi=1):
+        return O(name, 48 * lo + 15, 48 * hi, 16)
+
+    def step(k, add=None):
+        odd = col(k) % 2
+        gk = O("G", 16 - 16 * odd, 64)
+        nk = place("ND", k + 1, 16 * odd) if add is None else add
+        return [lambda: tt(gk, by(O("PS"), O("off", col(k) - odd, col(k) + 3)), nk, ADD),
+                lambda: scan(O("SC"), O("rise", 0, 48), O("G", 16, 64)),
+                lambda: narrow(off(k + 1), kept("SC"))]
+
+    def weave(chain, beside):
+        beside = list(beside)
+        for i, call in enumerate(chain):
             call()
-        for k in range(k0, 8):
-            scan(O("SC"), O("r16", 0, 48), O("G"))
-            copy(O("off", 4 * k, 4 * k + 3), O("SC", 15, 48, 16))
-            if k < 7:
-                tt(O("G"), P_by(k), place("N", k + 1), ADD)
-            for call in beside[k - k0 + 1]:
-                call()
+            for c in (beside[i] if i < len(beside) else []):
+                c()
 
     first = [0, 1, 0]
-    FROM, NX, NY = ["jf", "sa0", "jf"], ["x0", "sb0", "sa0"], ["y0", "y1", "sa1"]
+
+    def sides(t):
+        return ((12, 21), (3, 12)) if t == 1 else ((0, 12), (12, 24))
+
+    def steps_between(k, n=1):
+        return O("DF", 3 * slot(k), 3 * (slot(k) + n))
 
     def ahead(t):
         f = first[t]
-        return [lambda: tt(O("G2"), O(FROM[t]), place("N", f + 1), ADD),
-                lambda: scan(O("SC2"), O("r16", 0, 48), O("G2")),
-                lambda: copy(O("of2", 0, 3), O("SC2", 15, 48, 16)),
-                lambda: tt(O("G2"), P_by(0, "of2"), place("N", f), ADD),
-                lambda: copy(O("X1"), P_by(0, "of2"), "s"),
-                lambda: scan(O("SC2"), O("r16", 0, 48), O("G2")),
-                lambda: tt(O("DX"), O("X1"), O(NX[t]), SUB),
-                lambda: copy(O("of2", 4, 7), O("SC2", 15, 48, 16)),
-                lambda: copy(O("Y1"), P_by(1, "of2"), "s"),
-                lambda: tt(O("DY"), O("Y1"), O(NY[t]), SUB)]
+        w = lambda q, r, n=1: O("W", 15 * q + r, 15 * (q + n), 5)
+        rise = O("rise", 0, 96)
+        ps = lambda lo, hi: by(O("PS"), O("of2", lo, hi))
+        early = [lambda: ts(w(0, 2, 2), O("off", col(f), col(f) + 6), O("kap"), None, ADD),
+                 lambda: copy(w(0, 4, 3), steps_between(f + 1, 3)),
+                 lambda: tt(O("e1"), steps_between(f + 1), steps_between(f + 2), ADD)]
+        chain = [lambda: tt(O("a1"), w(0, 2, 2), steps_between(f + 1, 2), ADD),
+                 lambda: narrow(O("of2", 0, 6), O("a1")),
+                 lambda: tt(O("G2"), ps(0, 6), O("ND", 48 * slot(f + 1), 48 * slot(f + 1) + 96), SUB),
+                 lambda: scan(O("T1"), rise, O("G2")),
+                 lambda: narrow(O("of2", 6, 12), kept("T1", 0, 2)),
+                 lambda: copy(O("G2"), ps(6, 12)),
+                 lambda: scan(O("T2"), rise, O("G2")),
+                 lambda: (tt(O("a2", 0, 3), kept("T2"), O("e1"), ADD), tt(O("a2", 4, 7), kept("T2"), O("e3"), ADD)),
+                 lambda: narrow(O("of2", 12, 19), O("a2", 0, 7)),
+                 lambda: (tt(O("G2", 0, 48), ps(12, 15), place("ND", f + 3), ADD), tt(O("G2", 48, 96), ps(16, 19), place("ND", f + 3), SUB)),
+                 lambda: scan(O("T3"), rise, O("G2")),
+                 lambda: narrow(O("of2", 20, 26), kept("T3", 0, 2)),
+                 lambda: copy(O("G2"), ps(20, 26)),
+                 lambda: scan(O("T4"), rise, O("G2")),
+                 lambda: (tt(w(2, 3), kept("T4"), O("k1"), ADD), tt(O("dB"), kept("T4", 1, 2), kept("T2", 1, 2), SUB)),
+                 lambda: tt(w(2, 0), O("dB"), w(2, 3), SUB)]
+        beside = [[lambda: tt(O("e3"), O("e1"), steps_between(f + 3), ADD)], [], [],
+                  [lambda: ts(w(3, 2, 2), O("off", col(f + 1), col(f + 1) + 6), O("kap"), None, ADD)],
+                  [lambda: tt(w(3, 3), kept("T1"), w(3, 2), SUB)],
+                  [lambda: tt(w(4, 1), kept("T1", 1, 2), w(4, 2), SUB)],
+                  [lambda: ts(w(2, 2), off(f + 4), O("kap"), None, ADD)], [],
+                  [lambda: tt(w(1, 3), O("a2", 0, 3), w(1, 2), SUB)],
+                  [lambda: tt(O("k1"), steps_between(f + 4), w(2, 2), SUB)], [],
+                  [lambda: tt(w(4, 3), kept("T3"), w(4, 2), SUB), lambda: tt(O("xB"), kept("T3", 1, 2), kept("T1", 1, 2), SUB)],
+                  [lambda: tt(O("k2"), O("k1"), steps_between(f + 3), ADD)],
+                  [lambda: tt(w(4, 0), O("xB"), w(4, 3), SUB), lambda: tt(w(2, 1), kept("T2", 1, 2), O("k2"), ADD)], [], []]
+        return early, [[c] + b for c, b in zip(chain, beside)]
 
-    def address(t, k):
-        if k in (first[t], first[t] + 1):
-            return O(("sa%d" if k == first[t] else "sb%d") % t)
-        return O("sa0") if k < first[t] else P_by(k)
+    def label_steps():
+        return [lambda: tt(O("DF", 12, 24), O("L", 12, 24), O("L", 0, 12), SUB), lambda: tt(O("DF", 3, 12), O("L", 3, 12), O("L", 12, 21), SUB)]
 
-    def score_places(t, k):
-        tt(place("VF", k), P_by(k) if t < 0 else address(t, k), place("N", k), ADD)
+    def values(lo, hi, q):
+        c = 22 if lo == 7 else 3 * lo
+        copy(O("VAL", 48 * lo, 48 * hi), by(O("PS"), O("off", c, c + 3 * (hi - lo))), q)
 
     def score_list(t):
-        scan(O("SF"), O("r16"), O("VF"))
+        scan(O("SF"), O("rise"), O("VAL"))
         if t == 1:
-            copy(O("fl1", 1, 13), O("SF", 15, 192, 16))
-            copy(O("fl1", 14, 26), O("SF", 207, 384, 16))
+            narrow(O("fl1", 1, 13), O("SF", 15, 192, 16))
+            narrow(O("fl1", 14, 26), O("SF", 207, 384, 16))
         else:
-            copy(O("fl%d" % t, 0, 24), O("SF", 15, 384, 16))
-
-
-    def sides(t):
-        return ((192, 336), (48, 192)) if t == 1 else ((0, 192), (192, 384))
-
-    def differences(t):
-        a, b = sides(t)
-        n = a[1] - a[0]
-        return [lambda: tt(O("DN", 0, n), O("N", *b), O("N", *a), SUB),
-                lambda: act(O("KC", 0, n), O("K", *b), FN.Identity, 2.0, -1.0),
-                lambda: tt(O("KA", 0, n), O("KC", 0, n), O("K", *a), ADD),
-                lambda: act(O("KB", 0, n), O("KA", 0, n), FN.Identity, -1.0, 1.0)]
-
-    def exchange(t):
-        a, b = sides(t)
-        n = a[1] - a[0]
-        return [lambda: tt(O("MN", 0, n), O("DN", 0, n), O("CC", 0, n), MUL),
-                lambda: tt(O("N", *a), O("N", *a), O("MN", 0, n), ADD),
-                lambda: tt(O("N", *b), O("N", *b), O("MN", 0, n), SUB),
-                lambda: tt(O("K", *a), O("KA", 0, n), O("CC", 0, n), EQ),
-                lambda: tt(O("K", *b), O("KB", 0, n), O("CC", 0, n), EQ)]
-
-    def choose(t):
-        return [lambda: tt(O("MB"), O("DY"), O("CC", 0, 48), MUL),
-                lambda: tt(O("sb%d" % t), O(NY[t]), O("MB"), ADD),
-                lambda: tt(O("MA"), O("DX"), O("CC", 0, 48), MUL),
-                lambda: tt(O("sa%d" % t), O(NX[t]), O("MA"), ADD)]
-
-    def pick(t, k):
-        tt(O("VV", k, 384, 8), address(t, k), place("K", k), MUL)
-
-    def spread(sem, out, in_, qs):
-        dmas(sem, [(qs[i % len(qs)], T[out][16 * i:16 * i + 16, 0:20], T[in_][i:128:16, 0:40], [(out, 0, 20, 1, 0)], [(in_, 0, 40, 1, 0)])
-                   for i in range(8)])
+            narrow(O("fl%d" % t, 0, 24), O("SF", 15, 384, 16))
 
     def unpack(t, name, cn, sn):
         for b in range(4):
             p = mx("eq", 128 * b, cn, 0, 320, sn)
             copy(O("%s%d" % (name, t), 320 * b, 320 * b + 320), p, "s")
 
-    sp, df, vf = ahead(0), differences(0), [lambda k=k: score_places(-1, k) for k in range(8)]
-    walk(O("jf"), 0, [
-        [lambda: copy(O("upu"), O("upi")), lambda: quant("uq", "uqs", "ut", 0, 128)],
-        [lambda: copy(words(O("uw")), by(words(O("uq")), O("upu"))), sp[0]],
-        [lambda: quant("qc0", "qs0", "xt0", *CH[0]), lambda: quant("qc0", "qs0", "xt0", *CH[1]), sp[1],
-         lambda: copy(O("uws"), by(O("uqs"), O("upu")), "s"), lambda: scores(0, 0)],
-        [lambda: copy(O("x0"), P_by(0), "s"), lambda: copy(O("y0"), P_by(1), "s"), df[1], sp[2], df[0]],
-        [sp[3], sp[4], lambda: scores(0, 1), vf[0], vf[1]],
-        [sp[5], vf[2], vf[3], sp[6]],
-        [sp[7], df[2], vf[4]],
-        [df[3], sp[8], vf[5]],
-        [vf[6], vf[7]]])
+    def spread(sem, out, in_, at, lane, qs):
+        dmas(sem, [(qs[i % len(qs)], T[out][16 * i:16 * i + 16, 0:20], T[in_][lane(i):128:16, at(i):at(i) + 40], O(out, 0, 20, 1, (16 * i, 16 * i + 16))[1],
+                    O(in_)[1]) for i in range(8)])
+
+    def wide_steps(pieces, anew=True):
+        if anew:
+            ts(O("ndu"), O("DF"), 1.0 / 320.0, 7.25, MUL, ADD)
+        for lo, hi in pieces:
+            copy(O("ND", 16 * lo, 16 * hi), by(O("wd"), O("ndu", lo, hi)), "s")
+
+    tt(O("G", 16, 64), O("jf"), place("NB", 0), ADD)
+    scan(O("SF"), O("rise"), O("NB"))
+    scan(O("SC"), O("rise", 0, 48), O("G", 16, 64))
+    narrow(O("L"), O("SF", 15, 384, 16))
+    tt(place("ND", 1), place("NB", 1), place("NB", 0), SUB)
+    narrow(off(0), kept("SC"))
+    for call in label_steps():
+        call()
+    table(5, "v")
+    wide_steps([])
+    chain = [c for k in range(7) for c in step(k)]
+    early, sp = ahead(0)
+    more = {14: [lambda: values(4, 7, "s")], 17: [lambda: values(0, 4, "s")]}
+    weave(chain, [
+        [lambda: wide_steps([(2, 6), (14, 24), (6, 12)], False), lambda: quant("uq", "uqs", "ut", 0, 128)],
+        [lambda: quant("qc0", "qs0", "xt0", *CH[0]), lambda: copy(O("uws"), by(O("uqs"), O("upu")), "s")],
+        [lambda: copy(words(O("uw")), by(words(O("uq")), O("upu")))],
+        [lambda: quant("qc0", "qs0", "xt0", *CH[1]), lambda: scores(0, 0, "s"), lambda: scores(0, 1, "s"), lambda: send_state(0)],
+        [lambda: scan(O("selx"), O("rise", 0, 192), O("sel"))], early] + [sp[i - 6] + more.get(i, []) for i in range(6, 21)])
+    values(7, 8, "v")
+    sp[15][0]()
+    narrow(O("sl"), O("selx", 15, 192, 16))
     score_list(0)
-    sp[9]()
-    send_state(0)
-    quant("eq", "eqs", "ec", 0, 512)
-    iota(O("i8"), [[0, 40], [1, 8]], 0, 0)
-    select(O("r8"), O("i8"), [[0, 40], [1, 8]], 1.0)
-    iota(O("wone"), [[1, 8]], 0, 0)
-    iota(O("lm"), [[1, 2], [2, 4], [0, 48]], 0, 0)
+    copy(O("gpat"), by(O("t320"), O("rl", 12, 24)), "s")
 
     for t in range(3):
-        n = sides(t)[0][1] - sides(t)[0][0]
-        unpack(t, "fo", "qc%d" % t, "qs%d" % t)
-        unpack(t, "fp", "lc%d" % t, "lp%d" % t)
+        f = first[t]
+        a, b = sides(t)
+        n = a[1] - a[0]
         one, two = ((14, 23), (4, 13)) if t == 1 else ((0, 12), (12, 24))
-        copy(O("E", 0, n), by(O("ST"), O("fl%d" % t, *one)))
-        tt(O("CC", 0, n), by(O("ST"), O("fl%d" % t, *two)), O("E", 0, n), LT)
-        ex, ch = exchange(t), choose(t)
-        for call in (ex[0], ch[0], ex[1], ch[1]):
-            call()
-        p = [lambda k=k: pick(t, k) for k in range(8)]
-        if t == 1:
-            walk(O("sb1"), 3, [ex[2:3], ex[3:4], ex[4:5] + ch[2:3], ch[3:4] + p[3:5], [p[0], p[1], p[2], p[5], p[6]], p[7:]])
-        else:
-            walk(O("sb%d" % t), 2, [ex[2:3], ex[3:4], ex[4:5] + ch[2:3], ch[3:4] + p[2:4], [p[0], p[1], p[4]], p[5:7], p[7:]])
-        run("v", [O("SV")], [O("r8"), O("VV", 0, 320)],
-            lambda: g.vector.tensor_tensor_scan(O("SV")[0], O("r8")[0], O("VV", 0, 320)[0], 0.0, MUL, ADD))
-        ts(O("ml%d" % t), O("SV", 7, 320, 8), 160.0, None, ADD)
-        k = send(t, O("ll%d" % t), O("ml%d" % t), "rl%d" % t)
-        arrives("rl%d" % t, k, [O("ll%d" % t)])
-        spread("own%d" % t, "al%d" % t, "ml%d" % t, "y")
+        tt(O("E", 0, 16 * n), by(O("ST"), O("fl%d" % t, *one)), O("cap", 0, 16 * n), MIN)
+        tt(O("CC", 0, 16 * n), by(O("ST"), O("fl%d" % t, *two)), O("E", 0, 16 * n), LT)
+        act(O("SG"), O("CC", 96, 144), -2.0, 1.0)
+        scan(O("FL", 0, 16 * n), O("zero", 0, 16 * n), O("CC", 0, 16 * n), MUL, ADD)
+        copy(O("d0"), by(O("FL"), O("sl", 0, 5)))
+        tt(O("d1"), by(O("FL"), O("sl", 6, 11)), O("W"), MUL)
+        tt(O("M", 0, n), O("FL", 15, 16 * n, 16), steps_between(f + 1, n // 3), MUL)
+        entry = [lambda: scan(O("SS"), O("d0"), O("d1"), MUL, ADD), lambda: narrow(O("off", col(f), col(f) + 9), O("SS", 4, 45, 5))]
+        chain = entry + step(f + 4, O("NB", 16, 64)) + [c for k in range(f + 5, 7) for c in step(k)] + [lambda: values(7, 8, "v")]
+        pieces = [[(8, 12), (20, 24), (2, 8)], [(20, 24), (12, 20)], [(8, 12), (20, 24)]][t]
         if t < 2:
-            if t == 0:
-                copy(O("y1"), P_by(2), "s")
-            sp, df, vf = ahead(t + 1), differences(t + 1), [lambda k=k: score_places(t, k) for k in range(8)]
-            for call in (df[1:2] + sp[0:1] + vf[0:2] + sp[1:2] + vf[2:4] + sp[2:3] + df[2:3] + sp[3:5] + df[3:4] + vf[4:5] + sp[5:6] + vf[5:7]
-                         + sp[7:9] + vf[7:8] + sp[6:7] + df[0:1]):
-                call()
-            score_list(t + 1)
-            sp[9]()
+            early, sp = ahead(t + 1)
         else:
-            scan(O("SF"), O("r16"), O("N"))
-            ts(O("ls0"), O("SF", 15, 384, 16), -160.0, 1.0 / 320.0, ADD, MUL)
-            ts(O("ls1"), O("ls0"), -1.0, O("h8"), MUL, ADD)
-            ts(O("ls2"), O("ls1"), 7, None, AND)
-            copy(O("gw"), O("ls2"))
-            tt(O("o1"), by(O("wone"), O("gw")), O("lm"), MUL)
-            tt(O("o2"), O("o1", 0, 192), O("o1", 192, 384), ADD)
-            tt(O("o3"), O("o2", 0, 96), O("o2", 96, 192), ADD)
-            tt(O("o4"), O("o3", 0, 48), O("o3", 48, 96), ADD)
-            copy(O("ol40"), O("o4", 0, 40))
-        tt(O("BG"), by(O("P", 0, 320), O("al%d" % t)), O("msk", 0, 320), SUB)
-        scan(O("BS"), O("r16", 0, 320), O("BG"))
-        ts(O("bl%d" % t), O("BS", 15, 320, 16), 160.0, None, ADD)
-        spread("par%d" % t, "pl%d" % t, "ll%d" % t, "ys")
-        if t == 2:
-            spread("do1", "ow", "ol40", "y")
-        for lo, hi in CH:
-            off = O("pl%d" % t, lo // 16, hi // 16)
-            for b in range(4):
-                copy(O("zt%d" % t, 4 * lo + b, 4 * hi, 4), by(O("fp%d" % t, 320 * b, 320 * b + 320), off), "v" if b < 2 else "s")
-            quant("zc%d" % t, "zs%d" % t, "zt%d" % t, lo, hi)
+            early = [lambda: ts(O("lu"), O("L"), 1.0 / 320.0, 0.25, MUL, ADD), lambda: copy(O("OB"), by(O("tone"), O("lu")), "s"),
+                     lambda: spread("do1", "owb", "OB", lambda i: 48 * slot(i), lambda i: 0, "y")]
+            sp = [[]] * 16
+        position = [[lambda: tt(O("PN"), by(O("L"), O("rl", 0, 12)), O("gpat"), NE)],
+                    [lambda: scan(O("PC"), O("PN"), O("cpat"), MUL, ADD)],
+                    [lambda: ts(O("pos"), O("PC", 7, 192, 8), O("lanef"), None, ADD)]]
+        odd, even = [lambda: values(4, 7, "s")], [lambda: values(0, 4, "s")]
+        beside = [[lambda: tt(O("L", *a), O("L", *a), O("M", 0, n), ADD), lambda: tt(O("L", *b), O("L", *b), O("M", 0, n), SUB),
+                   lambda: tt(O("NB", 16, 64), place("ND", f + 5), O("SG"), MUL)],
+                  label_steps(),
+                  [lambda: wide_steps(pieces), lambda: narrow(O("off", col(f + 1), col(f + 1) + 6), O("SS", 49, 75, 5))]]
+        if t == 1:
+            beside += [position[0], odd + even + position[1], position[2], early, sp[0], sp[1]]
+            done = 2
+        else:
+            beside += [early, odd + sp[0], position[0], sp[1], even + position[1], sp[2], position[2], sp[3], sp[4]]
+            done = 5
+        weave(chain, beside)
+        ts(O("ml%d" % t), by(O("VAL"), O("pos")), O("ux"), None, SUB)
+        spread("own%d" % t, "al%d" % t, "ml%d" % t, lambda i: 48 * i, lambda i: i, "ys")
+        k = send(t, O("pl%d" % t), O("al%d" % t), "rl%d" % t)
+        arrives("rl%d" % t, k, [O("pl%d" % t)])
         if t == 0:
-            quant("vq", "vqs", "vt", 0, 128)
-            copy(O("xf"), O("xi"))
-            ts(O("lm"), O("lm"), O("xf"), None, EQ)
-        for lo, hi in CH:
+            quant("eq", "eqs", "ec", 0, 512)
+        unpack(t, "fp", "lc%d" % t, "lp%d" % t)
+        copy(O("BG"), by(O("PS", 0, 320), O("al%d" % t)), "s")
+        unpack(t, "fo", "qc%d" % t, "qs%d" % t)
+        list_b = [lambda: scan(O("BS"), O("rise", 0, 320), O("BG")), lambda: narrow(O("bl%d" % t), O("BS", 15, 320, 16))]
+        extra = {done: [lambda: score_list(t + 1)] if t < 2 else [], 12: list_b[:1], 13: list_b[1:]}
+        if t == 0:
+            extra[8] = [lambda: quant("vq", "vqs", "vt", 0, 128)]
+        if t == 2:
+            extra[11] = [lambda: copy(O("ow"), O("owb")), lambda: copy(O("olf"), by(O("i320"), O("ow"))),
+                         lambda: dmas("dout", [("y", T.ol[:], T.olf[0:128:16, 0:320], [], O("olf")[1])])]
+        for i in range(done, 16):
+            for call in sp[i] + extra.get(i, []):
+                call()
+        for lo, hi in ZCH:
+            o = O("pl%d" % t, lo // 16, hi // 16)
+            for b in range(4):
+                copy(O("zt%d" % t, 4 * lo + b, 4 * hi, 4), by(O("fp%d" % t, 320 * b, 320 * b + 320), o), "v" if b < 2 else "s")
+            quant("zc%d" % t, "zs%d" % t, "zt%d" % t, lo, hi)
+        for i, (lo, hi) in enumerate(ZCH):
             for b in range(4):
                 p = mx("wq", 128 * b, "zc%d" % t, lo, hi, "zs%d" % t)
                 o = O("rb%d" % b, lo, hi)
-                run("s", [o], [p], lambda o=o, p=p: g.scalar.activation(o[0], p[0], COPY, scale=0.03125))
+                if RQ[i][b] == "v":
+                    ts(o, p, 0.03125, None, MUL)
+                else:
+                    run("s", [o], [p], lambda o=o, p=p: g.scalar.activation(o[0], p[0], COPY, scale=0.03125))
         for i, (lo, hi) in enumerate(CH):
-            off = O("bl%d" % t, lo // 16, hi // 16)
+            o = O("bl%d" % t, lo // 16, hi // 16)
             for b in range(4):
-                tt(O("xt%d" % (t + 1), 4 * lo + b, 4 * hi, 4), by(O("rb%d" % b), off), O("fo%d" % t, 320 * b + lo, 320 * b + hi), ADD)
+                tt(O("xt%d" % (t + 1), 4 * lo + b, 4 * hi, 4), by(O("rb%d" % b), o), O("fo%d" % t, 320 * b + lo, 320 * b + hi), ADD)
             quant("qc%d" % (t + 1), "qs%d" % (t + 1), "xt%d" % (t + 1), lo, hi)
-            if t < 2 and i == 0:
-                scores(t + 1, 0)
+            if t < 2:
+                scores(t + 1, i, SQ[i])
+            else:
+                o, y = O("qc3", lo, hi), O("yb", lo, hi)
+                copy(y, mx("vq", 0, "qc3", lo, hi, "qs3"), "s")
+                dmas("dout", [("y", T.oc[:, 4 * lo:4 * hi], codes(o)[0], [], o[1]), ("s", T.y[:, lo:hi], y[0], [], y[1])])
         if t < 2:
             send_state(t + 1)
-            scores(t + 1, 1)
-        else:
-            copy(O("olf"), by(O("wone"), O("ow")))
-    outs = []
-    for lo, hi in CH:
-        o = O("qc3", lo, hi)
-        outs.append(("y", T.oc[:, 4 * lo:4 * hi], codes(o)[0], [], o[1]))
-    for k in range(4):
-        outs.append(("y", T.osc[4 * k:4 * k + 4, 0:320], T.qs3[32 * k:32 * k + 4, 0:320], [], O("qs3")[1]))
-    outs.append(("y", T.ol[:], T.olf[0:128:16, 0:320], [], O("olf")[1]))
-    for lo, hi in CH:
-        p = mx("vq", 0, "qc3", lo, hi, "qs3")
-        o = O("yb", lo, hi)
-        copy(o, p, "s")
-        outs.append(("s", T.y[:, lo:hi], o[0], [], o[1]))
-    dmas("dout", outs)
+    dmas("dout", [("y", T.osc[4 * k:4 * k + 4, 0:320], T.qs3[32 * k:32 * k + 4, 0:320], [], O("qs3")[1]) for k in range(4)])
     for s in SEMAPHORES:
         if total[s]:
             g.wait_ge(T.sem[s], total[s])

@@ -11,8 +11,12 @@ FAR = 1e29
 STEP = [1, 2, 4]
 SQ = ["s", "vvsvsvsv"]
 RQ = ["ssss", "vvss"]
+TQ = "v"
+CUT = [16, 16, 16]
+ZQ = ["vvss", "vsss"]
+FO = 2
 ZCH = [(0, 192), (192, 320)]
-CH = [(0, 128), (128, 320)]
+CH = [(0, 160), (160, 320)]
 
 SCRATCH = {}
 
@@ -34,20 +38,20 @@ def _share(buf, dtype, *parts):
 
 _share("iv", "int32", ("pint", 1), ("lanei", 1), ("hi", 1), ("xi", 1), ("sxi", 1), ("sx7", 1), ("upi", 16), ("mi", 24), ("pi0", 24),
        ("pi1", 24), ("pi2", 24), ("t8", 8), ("t8a", 8), ("t8b", 8))
-_share("fv", "float32", ("lanef", 1), ("hf", 1), ("h2", 1), ("ux", 1), ("kap", 1), ("lan16", 1), ("ge20", 24), ("ge40", 24), ("ja", 48),
-       ("jf", 48), ("i16", 16), ("z16", 16), ("t320", 8), ("tone", 8), ("wd", 16), ("r3", 9), ("z24", 24))
-_share("ov", "float32", ("W", 80), ("a2", 8), ("DF", 24), ("L", 24), ("M", 12), ("d0", 80), ("d1", 80), ("SS", 80),
+_share("fv", "float32", ("lanef", 1), ("hf", 1), ("h2", 1), ("kap2", 1), ("kap", 1), ("lan16", 1), ("ge20", 24), ("ge40", 24), ("ja", 48),
+       ("jf", 48), ("i16", 16), ("z16", 16), ("t320", 8), ("tone", 8), ("wd", 8), ("r3", 9), ("z24", 24))
+_share("ov", "float32", ("W", 80), ("a2", 8), ("D", 12), ("fs", 24), ("L", 24), ("M", 12), ("d0", 80), ("d1", 80), ("SS", 80),
        ("a1", 6), ("e1", 3), ("e3", 3), ("k1", 3), ("k2", 3), ("dB", 3), ("xB", 3))
 _share("uv", "uint16", ("ogu", 20), ("upu", 16), ("cl", 24), ("ln", 24), ("rl", 24), ("sl", 12), ("lu", 24), ("ow", 20))
 _share("wv", "float32", ("SG", 48), ("SC", 48), ("G2", 96), ("T1", 96), ("T2", 96), ("T3", 96), ("T4", 96))
 _d("pgi", 40, "int32")
 _d("ogi", 20, "int32")
-for _n, _c in (("i320", 320), ("rise", 384), ("zero", 192), ("cap", 192), ("pats", 384), ("patx", 384), ("gpat", 192), ("c0", 192), ("cpat", 192),
-               ("lab", 320), ("NB", 384), ("ND", 384), ("E", 192), ("CC", 192), ("FL", 200), ("G", 64), ("VAL", 384), ("SF", 384), ("sel", 192), ("selx", 192),
-               ("PN", 192), ("PC", 192), ("PS", 2560), ("ST", 2560), ("BG", 320), ("BS", 320), ("one", 320),
+for _n, _c in (("rise", 384), ("zero", 192), ("cap", 192), ("pats", 384), ("patx", 384), ("gpat", 192), ("c0", 192), ("cpat", 192),
+               ("lab", 320), ("N", 384), ("E", 192), ("CC", 192), ("FL", 200), ("G", 64), ("VAL", 384), ("SF", 384), ("sel", 192), ("selx", 192),
+               ("PN", 192), ("PC", 192), ("ST", 2560), ("BG", 320), ("BS", 320),
                ("rb0", 320), ("rb1", 320), ("rb2", 320), ("rb3", 320), ("olf", 320), ("yb", 320)):
     _d(_n, _c, "float32")
-for _n, _c in (("pu", 160), ("off", 26), ("of2", 26), ("ndu", 24), ("pos", 24), ("fl0", 26), ("fl1", 26), ("fl2", 26)):
+for _n, _c in (("pu", 40), ("off", 26), ("of2", 26), ("pos", 24), ("fl0", 26), ("fl1", 26), ("fl2", 26)):
     _d(_n, _c, "uint16")
 for _t in range(3):
     _d("ml%d" % _t, 384, "uint16")
@@ -65,7 +69,7 @@ for _t in range(4):
     _d("xt%d" % _t, 1280, "bfloat16")
     _d("qc%d" % _t, 320, "float8_e4m3fn_x4")
     _d("qs%d" % _t, 320, "uint8")
-for _n, _c in (("ones", 512), ("ec", 2048), ("ut", 512), ("vt", 512), ("OB", 384), ("owb", 20)):
+for _n, _c in (("ones", 516), ("ec", 516), ("i320", 320), ("P", 2560), ("ut", 512), ("vt", 512), ("OB", 384), ("owb", 20)):
     _d(_n, _c, "bfloat16")
 for _n, _c in (("eq", 512), ("wq", 512), ("uq", 128), ("uw", 256), ("vq", 128)):
     _d(_n, _c, "float8_e4m3fn_x4")
@@ -73,7 +77,7 @@ for _n, _c in (("eq", 512), ("wq", 512), ("uq", 128), ("uw", 256), ("vq", 128)):
 for _k in range(8):
     _d("ps%d" % _k, 512, "float32", "psum")
 
-DMA_SEMS = ["dpg", "dog", "du", "dxa", "dxb", "dw", "dv", "own0", "own1", "own2", "do1", "dout"]
+DMA_SEMS = ["dpg", "dog", "du", "dxa", "dxb", "dw", "dv", "dp", "own00", "own01", "own10", "own11", "own20", "own21", "do1", "dout"]
 SEMAPHORES = ["cv", "cs", "ct", "cg", "left", "rq0", "rq1", "rq2", "rl0", "rl1", "rl2"] + DMA_SEMS
 
 
@@ -217,8 +221,8 @@ def rank_program(g, core, T, topo):
         run("t", [full], [a, s, b, p], lambda: g.tensor.matmul_mx(out[0], a[0], s[0], b[0], p[0], True, True))
         return full
 
-    def narrow(out, wide):
-        ts(out, wide, O("kap"), None, SUB)
+    def narrow(out, wide, climb="kap2"):
+        ts(out, wide, O(climb), None, SUB)
 
     def load(q, name, src, lo, hi, rows=(0, 128)):
         o = O(name, lo, hi, 1, rows)
@@ -231,93 +235,75 @@ def rank_program(g, core, T, topo):
     dmas("dxa", [load("y", "xt0", T.x[:, 0:768], 0, 768)])
     dmas("du", [load("s", "ut", T.u[:], 0, 512)])
     dmas("dxb", [load("y", "xt0", T.x[:, 768:1280], 768, 1280)])
-    dmas("dw", [("y", codes(O("wq"))[0], T.wc[:], O("wq")[1], []), ("y", O("wqs")[0], T.ws[:], O("wqs")[1], [])])
-    dmas("dv", [load("y", "vt", T.v[:], 0, 512)])
 
+    fill(O("ones"), 1.0)
+    fill(O("sel"), 193.0)
     iota(O("pint"), [[1, 1]], 0, 1)
     iota(O("i16"), [[1, 16]], 0)
     iota(O("t8"), [[-1, 8]], 8)
     iota(O("mi"), [[0, 8], [16, 3]], 0)
     iota(O("pi0"), [[1, 2], [2, 4], [256, 3]], 0)
-    fill(O("one"), 1.0)
-    fill(O("sel"), 193.0)
+    iota(O("i320"), [[1, 320]], -160)
+    iota(O("upi"), [[0, 2], [16, 8]], 0)
+    iota(O("ja", 0, 40), [[1, 2], [16, 20]], -160)
+    iota(O("ja", 40, 48), [[16, 8]], -160)
+    select(O("ec"), O("ones"), [[-1, 516]], 0.0, 3, 4)
     iota(O("pats", 0, 192), [[0, 8], [1, 3], [3, 8]], 0)
     iota(O("pats", 192, 384), [[1, 8], [0, 24]], 0)
-    iota(O("upi"), [[0, 2], [16, 8]], 0)
-    iota(O("ja", 0, 40), [[1, 2], [16, 20]], 0)
-    iota(O("ja", 40, 48), [[16, 8]], 0)
-    iota(O("wd"), [[320, 16]], -2240)
+    iota(O("wd"), [[320, 8]], 0)
     iota(O("sel", 1, 75, 5), [[0, 5], [16, 3]], 15)
     iota(O("sel", 2, 75, 5), [[0, 5], [16, 3]], 63)
     iota(O("sel", 99, 171, 5), [[0, 5], [16, 3]], 15)
     iota(O("sel", 100, 141, 5), [[48, 3], [16, 3]], 15)
     iota(O("c0"), [[0, 8], [16, 3], [0, 8]], 336)
     select(O("cpat"), O("c0"), [[0, 24], [1, 8]], -48.0, -7)
-    iota(O("ones"), [[0, 512]], 1)
 
     ts(O("lanei"), O("pint"), 15, None, AND)
     ts(O("hi"), O("pint"), 4, None, SHR)
-    ts(O("xi"), O("pint"), 7, None, AND)
     fill(O("off"), 0)
     copy(O("lanef"), O("lanei"))
     copy(O("hf"), O("hi"))
-    tt(O("sxi"), O("hi"), O("xi"), SUB)
     fill(O("sel", 0, 80, 5), 192.0)
     ts(O("z16"), O("i16"), O("lanef"), None, NE)
-    ts(O("ln"), O("one", 0, 24), O("lanef"), None, MUL)
+    ts(O("ln"), O("ones", 0, 24), O("lanef"), None, MUL)
     ts(O("t8a"), O("t8"), O("hf"), None, ADD)
     ts(O("lan16"), O("lanef"), 16.0, None, MUL)
     ts(O("pi1"), O("mi"), O("lanef"), None, ADD)
-    scan(O("i320"), O("one"), O("one"), MUL, ADD, -1.0)
     act(O("rise"), by(O("z16"), O("ln")), BIG + RISE, -BIG)
-    copy(O("zero"), by(O("z16"), O("ln", 0, 12)), "s")
-    act(O("cap"), by(O("z16"), O("ln", 0, 12)), -2 * FAR, FAR)
     ts(O("t8b"), O("t8a"), 7, None, AND)
-    ts(O("sx7"), O("sxi"), 7, None, AND)
     ts(O("ge20"), O("pi1"), 20.0, -312.0, GE, MUL)
     ts(O("ge40"), O("pi1"), 40.0, -328.0, GE, MUL)
     ts(O("pi2"), O("pi0"), O("lan16"), None, ADD)
     ts(O("t320"), O("t8b"), 320.0, None, MUL)
     ts(O("kap"), O("lanef"), -RISE, 15 * RISE, MUL, ADD)
     tt(O("ge20"), O("ge20"), O("ge40"), ADD)
+    ts(O("kap2"), O("lanef"), -RISE, 15 * RISE - 160.0, MUL, ADD)
     ts(O("h2"), O("hf"), 2.0, None, MUL)
-    ts(O("ux"), O("sx7"), 320.0, None, MUL)
-    copy(O("tone"), O("t8b"))
     tt(O("pi2"), O("pi2"), O("ge20"), ADD)
-    fill(O("ov", 0, 112), 0.0)
-    scan(O("patx"), O("rise"), O("pats"))
+    fill(O("ov", 0, 88), 0.0)
     copy(O("cl"), O("pi2"))
+
+    copy(O("pu"), O("pgi"))
+    copy(O("P", 0, 320), by(O("i320"), O("pu", 0, 20)))
+    copy(O("P", 320, 640), by(O("i320"), O("pu", 20, 40)), "s")
+    copy(O("ogu"), O("ogi"))
+    items = []
+    for s in range(1, 4):
+        for q, to, fro in (("y", (32 * s, 128), (0, 128 - 32 * s)), ("s", (0, 32 * s), (128 - 32 * s, 128))):
+            o, i = O("P", 640 * s, 640 * s + 640, 1, to), O("P", 0, 640, 1, fro)
+            items.append((q, o[0], i[0], o[1], i[1]))
+    dmas("dp", items)
+    dmas("dw", [("y", codes(O("wq"))[0], T.wc[:], O("wq")[1], []), ("y", O("wqs")[0], T.ws[:], O("wqs")[1], [])])
+    dmas("dv", [load("y", "vt", T.v[:], 0, 512)])
+    copy(O("lab"), by(O("t320"), O("ogu")))
+    copy(O("upu"), O("upi"))
+    copy(O("N"), by(O("lab"), O("cl")), "s")
+    ts(O("jf"), O("ja"), O("h2"), None, ADD)
+    copy(O("tone"), O("t8b"))
     fill(O("FL", 192, 193), 0.0)
     fill(O("FL", 193, 200), 1.0)
-    narrow(O("rl"), O("patx", 15, 384, 16))
-    for b in range(4):
-        select(O("ec", 512 * b, 512 * b + 512), O("ones"), [[-1, 512]], 0.0, b, 4)
 
-    copy(O("pu", 0, 40), O("pgi"))
-    for q in range(4):
-        copy(O("pu", 40, 80, 1, (32 * q, 32 * q + 32)), O("pgi", 0, 40, 1, (32 * ((q - 1) % 4), 32 * ((q - 1) % 4) + 32)))
-    copy(O("ogu"), O("ogi"))
-    copy(O("upu"), O("upi"))
-    for q in range(2):
-        copy(O("pu", 80, 160, 1, (64 * q, 64 * q + 64)), O("pu", 0, 80, 1, (64 - 64 * q, 128 - 64 * q)))
-
-    def table(s, q):
-        o, i = O("PS", 320 * s, 320 * s + 320), by(O("i320"), O("pu", 20 * s, 20 * s + 20))
-        if q == "v":
-            ts(o, i, 320.0 * s, None, ADD)
-        else:
-            act(o, i, 1.0, 320.0 * s)
-
-    copy(O("lab"), by(O("t320"), O("ogu")), "s")
-    copy(O("NB"), by(O("lab"), O("cl")), "s")
-    for s in range(0, 4):
-        table(s, "v")
-    for s in (4, 6, 7):
-        table(s, "s")
-    ts(O("jf"), O("ja"), O("h2"), None, ADD)
-
-    def scores(t, piece, qs):
-        lo, hi = CH[piece]
+    def scores(t, lo, hi, qs):
         for s in range(8):
             p = mx("uw", 16 * (8 - s), "qc%d" % t, lo, hi, "qs%d" % t)
             copy(O("ST", 320 * s + lo, 320 * s + hi), p, qs[s % len(qs)])
@@ -352,10 +338,13 @@ def rank_program(g, core, T, topo):
     def step(k, add=None):
         odd = col(k) % 2
         gk = O("G", 16 - 16 * odd, 64)
-        nk = place("ND", k + 1, 16 * odd) if add is None else add
-        return [lambda: tt(gk, by(O("PS"), O("off", col(k) - odd, col(k) + 3)), nk, ADD),
-                lambda: scan(O("SC"), O("rise", 0, 48), O("G", 16, 64)),
-                lambda: narrow(off(k + 1), kept("SC"))]
+        pk = by(O("P"), O("off", col(k) - odd, col(k) + 3))
+        if add is None:
+            return [lambda: tt(gk, pk, place("N", k + 1, 16 * odd), ADD),
+                    lambda: scan(O("SC"), O("rise", 0, 48), O("G", 16, 64)),
+                    lambda: narrow(off(k + 1), kept("SC"))]
+        return [lambda: copy(gk, pk), lambda: scan(O("SC"), O("rise", 0, 48), O("G", 16, 64)),
+                lambda: tt(O("e1"), kept("SC"), add, ADD), lambda: narrow(off(k + 1), O("e1"))]
 
     def weave(chain, beside):
         beside = list(beside)
@@ -369,99 +358,95 @@ def rank_program(g, core, T, topo):
     def sides(t):
         return ((12, 21), (3, 12)) if t == 1 else ((0, 12), (12, 24))
 
-    def steps_between(k, n=1):
-        return O("DF", 3 * slot(k), 3 * (slot(k) + n))
+    def label(k):
+        return O("L", 3 * slot(k), 3 * slot(k) + 3)
 
     def ahead(t):
         f = first[t]
         w = lambda q, r, n=1: O("W", 15 * q + r, 15 * (q + n), 5)
         rise = O("rise", 0, 96)
-        ps = lambda lo, hi: by(O("PS"), O("of2", lo, hi))
-        early = [lambda: ts(w(0, 2, 2), O("off", col(f), col(f) + 6), O("kap"), None, ADD),
-                 lambda: copy(w(0, 4, 3), steps_between(f + 1, 3)),
-                 lambda: tt(O("e1"), steps_between(f + 1), steps_between(f + 2), ADD)]
-        chain = [lambda: tt(O("a1"), w(0, 2, 2), steps_between(f + 1, 2), ADD),
+        ps = lambda lo, hi: by(O("P"), O("of2", lo, hi))
+        a, b = sides(t)
+        early = [lambda: ts(w(0, 2, 2), O("off", col(f), col(f) + 6), O("kap2"), None, ADD),
+                 lambda: tt(O("D", 0, a[1] - a[0]), O("L", *b), O("L", *a), SUB)]
+        chain = [lambda: tt(O("a1"), w(0, 2, 2), O("D", 0, 6), ADD),
                  lambda: narrow(O("of2", 0, 6), O("a1")),
-                 lambda: tt(O("G2"), ps(0, 6), O("ND", 48 * slot(f + 1), 48 * slot(f + 1) + 96), SUB),
+                 lambda: tt(O("G2"), ps(0, 6), O("N", 48 * slot(f), 48 * slot(f) + 96), ADD),
                  lambda: scan(O("T1"), rise, O("G2")),
                  lambda: narrow(O("of2", 6, 12), kept("T1", 0, 2)),
-                 lambda: copy(O("G2"), ps(6, 12)),
+                 lambda: copy(O("G2"), ps(6, 12), TQ),
                  lambda: scan(O("T2"), rise, O("G2")),
-                 lambda: (tt(O("a2", 0, 3), kept("T2"), O("e1"), ADD), tt(O("a2", 4, 7), kept("T2"), O("e3"), ADD)),
+                 lambda: (tt(O("a2", 0, 3), kept("T2"), label(f + 2), ADD), tt(O("a2", 4, 7), kept("T2"), label(f + 3), ADD)),
                  lambda: narrow(O("of2", 12, 19), O("a2", 0, 7)),
-                 lambda: (tt(O("G2", 0, 48), ps(12, 15), place("ND", f + 3), ADD), tt(O("G2", 48, 96), ps(16, 19), place("ND", f + 3), SUB)),
+                 lambda: (tt(O("G2", 0, 48), ps(12, 15), place("N", f + 3), ADD), tt(O("G2", 48, 96), ps(16, 19), place("N", f + 2), ADD)),
                  lambda: scan(O("T3"), rise, O("G2")),
                  lambda: narrow(O("of2", 20, 26), kept("T3", 0, 2)),
-                 lambda: copy(O("G2"), ps(20, 26)),
+                 lambda: copy(O("G2"), ps(20, 26), TQ),
                  lambda: scan(O("T4"), rise, O("G2")),
                  lambda: (tt(w(2, 3), kept("T4"), O("k1"), ADD), tt(O("dB"), kept("T4", 1, 2), kept("T2", 1, 2), SUB)),
                  lambda: tt(w(2, 0), O("dB"), w(2, 3), SUB)]
-        beside = [[lambda: tt(O("e3"), O("e1"), steps_between(f + 3), ADD)], [], [],
-                  [lambda: ts(w(3, 2, 2), O("off", col(f + 1), col(f + 1) + 6), O("kap"), None, ADD)],
+        beside = [[lambda: copy(w(0, 4, 3), O("D", 0, 9))], [], [],
+                  [lambda: ts(w(3, 2, 2), O("off", col(f + 1), col(f + 1) + 6), O("kap2"), None, ADD)],
                   [lambda: tt(w(3, 3), kept("T1"), w(3, 2), SUB)],
                   [lambda: tt(w(4, 1), kept("T1", 1, 2), w(4, 2), SUB)],
-                  [lambda: ts(w(2, 2), off(f + 4), O("kap"), None, ADD)], [],
+                  [lambda: ts(w(2, 2), off(f + 4), O("kap2"), None, ADD)], [],
                   [lambda: tt(w(1, 3), O("a2", 0, 3), w(1, 2), SUB)],
-                  [lambda: tt(O("k1"), steps_between(f + 4), w(2, 2), SUB)], [],
+                  [lambda: tt(O("k1"), label(f + 4), w(2, 2), SUB)], [],
                   [lambda: tt(w(4, 3), kept("T3"), w(4, 2), SUB), lambda: tt(O("xB"), kept("T3", 1, 2), kept("T1", 1, 2), SUB)],
-                  [lambda: tt(O("k2"), O("k1"), steps_between(f + 3), ADD)],
-                  [lambda: tt(w(4, 0), O("xB"), w(4, 3), SUB), lambda: tt(w(2, 1), kept("T2", 1, 2), O("k2"), ADD)], [], []]
+                  [lambda: tt(w(2, 1), kept("T2", 1, 2), O("k1"), ADD)],
+                  [lambda: tt(w(4, 0), O("xB"), w(4, 3), SUB)], [], []]
         return early, [[c] + b for c, b in zip(chain, beside)]
-
-    def label_steps():
-        return [lambda: tt(O("DF", 12, 24), O("L", 12, 24), O("L", 0, 12), SUB), lambda: tt(O("DF", 3, 12), O("L", 3, 12), O("L", 12, 21), SUB)]
 
     def values(lo, hi, q):
         c = 22 if lo == 7 else 3 * lo
-        copy(O("VAL", 48 * lo, 48 * hi), by(O("PS"), O("off", c, c + 3 * (hi - lo))), q)
+        copy(O("VAL", 48 * lo, 48 * hi), by(O("P"), O("off", c, c + 3 * (hi - lo))), q)
 
     def score_list(t):
-        scan(O("SF"), O("rise"), O("VAL"))
         if t == 1:
-            narrow(O("fl1", 1, 13), O("SF", 15, 192, 16))
-            narrow(O("fl1", 14, 26), O("SF", 207, 384, 16))
+            ends = [lambda: narrow(O("fl1", 1, 13), O("fs", 0, 12)), lambda: narrow(O("fl1", 14, 26), O("fs", 12, 24))]
         else:
-            narrow(O("fl%d" % t, 0, 24), O("SF", 15, 384, 16))
+            ends = [lambda: narrow(O("fl%d" % t, 0, 24), O("fs"))]
+        return [[lambda: scan(O("SF"), O("rise"), O("VAL"))], [lambda: tt(O("fs"), O("SF", 15, 384, 16), O("L"), ADD)], ends]
 
-    def unpack(t, name, cn, sn):
-        for b in range(4):
+    def unpack(t, name, cn, sn, planes=range(4)):
+        for b in planes:
             p = mx("eq", 128 * b, cn, 0, 320, sn)
             copy(O("%s%d" % (name, t), 320 * b, 320 * b + 320), p, "s")
 
-    def spread(sem, out, in_, at, lane, qs):
-        dmas(sem, [(qs[i % len(qs)], T[out][16 * i:16 * i + 16, 0:20], T[in_][lane(i):128:16, at(i):at(i) + 40], O(out, 0, 20, 1, (16 * i, 16 * i + 16))[1],
-                    O(in_)[1]) for i in range(8)])
+    def spread(sem, out, in_, at, groups, qs):
+        dmas(sem, [(qs[i % len(qs)], T[out][16 * i:16 * i + 16, 0:20], T[in_][i:128:16, at(i):at(i) + 40], O(out, 0, 20, 1, (16 * i, 16 * i + 16))[1],
+                    O(in_, at(i), at(i) + 40)[1]) for i in groups])
 
-    def wide_steps(pieces, anew=True):
-        if anew:
-            ts(O("ndu"), O("DF"), 1.0 / 320.0, 7.25, MUL, ADD)
+    def wide_labels(pieces):
         for lo, hi in pieces:
-            copy(O("ND", 16 * lo, 16 * hi), by(O("wd"), O("ndu", lo, hi)), "s")
+            copy(O("N", 16 * lo, 16 * hi), by(O("wd"), O("lu", lo, hi)), "s")
 
-    tt(O("G", 16, 64), O("jf"), place("NB", 0), ADD)
-    scan(O("SF"), O("rise"), O("NB"))
+    quant("uq", "uqs", "ut", 0, 128)
+    copy(O("uws"), by(O("uqs"), O("upu")), "s")
+    copy(words(O("uw")), by(words(O("uq")), O("upu")))
+    quant("qc0", "qs0", "xt0", 0, 320)
+    tt(O("G", 16, 64), O("jf"), place("N", 0), ADD)
+    scan(O("SF"), O("rise"), O("N"))
     scan(O("SC"), O("rise", 0, 48), O("G", 16, 64))
-    narrow(O("L"), O("SF", 15, 384, 16))
-    tt(place("ND", 1), place("NB", 1), place("NB", 0), SUB)
+    narrow(O("L"), O("SF", 15, 384, 16), "kap")
     narrow(off(0), kept("SC"))
-    for call in label_steps():
-        call()
-    table(5, "v")
-    wide_steps([])
-    chain = [c for k in range(7) for c in step(k)]
+    scores(0, 0, 320, "s")
+    for b in range(4):
+        q, s, x = O("eq", 128 * b, 128 * b + 128), O("eqs", 128 * b, 128 * b + 128), O("ec", 3 - b, 515 - b)
+        run("v", [q, s], [x], lambda: g.vector.quantize_mx(q[0], s[0], x[0]))
+    send_state(0)
+    copy(O("zero"), by(O("z16"), O("ln", 0, 12)), "s")
+    act(O("cap"), by(O("z16"), O("ln", 0, 12)), -2 * FAR, FAR)
+    chain = [c for k in range(7) for c in step(k)] + [lambda: values(7, 8, "v")]
     early, sp = ahead(0)
     more = {14: [lambda: values(4, 7, "s")], 17: [lambda: values(0, 4, "s")]}
     weave(chain, [
-        [lambda: wide_steps([(2, 6), (14, 24), (6, 12)], False), lambda: quant("uq", "uqs", "ut", 0, 128)],
-        [lambda: quant("qc0", "qs0", "xt0", *CH[0]), lambda: copy(O("uws"), by(O("uqs"), O("upu")), "s")],
-        [lambda: copy(words(O("uw")), by(words(O("uq")), O("upu")))],
-        [lambda: quant("qc0", "qs0", "xt0", *CH[1]), lambda: scores(0, 0, "s"), lambda: scores(0, 1, "s"), lambda: send_state(0)],
-        [lambda: scan(O("selx"), O("rise", 0, 192), O("sel"))], early] + [sp[i - 6] + more.get(i, []) for i in range(6, 21)])
-    values(7, 8, "v")
-    sp[15][0]()
-    narrow(O("sl"), O("selx", 15, 192, 16))
-    score_list(0)
-    copy(O("gpat"), by(O("t320"), O("rl", 12, 24)), "s")
+        [lambda: scan(O("patx"), O("rise"), O("pats"))], [lambda: narrow(O("rl"), O("patx", 15, 384, 16), "kap")],
+        [lambda: scan(O("selx"), O("rise", 0, 192), O("sel")), lambda: copy(O("gpat"), by(O("t320"), O("rl", 12, 24)), "s")],
+        [lambda: narrow(O("sl"), O("selx", 15, 192, 16), "kap"), lambda: unpack(0, "fo", "qc0", "qs0")],
+        [], early] + [sp[i - 6] + more.get(i, []) for i in range(6, 22)])
+    for calls in score_list(0):
+        calls[0]()
 
     for t in range(3):
         f = first[t]
@@ -470,59 +455,67 @@ def rank_program(g, core, T, topo):
         one, two = ((14, 23), (4, 13)) if t == 1 else ((0, 12), (12, 24))
         tt(O("E", 0, 16 * n), by(O("ST"), O("fl%d" % t, *one)), O("cap", 0, 16 * n), MIN)
         tt(O("CC", 0, 16 * n), by(O("ST"), O("fl%d" % t, *two)), O("E", 0, 16 * n), LT)
-        act(O("SG"), O("CC", 96, 144), -2.0, 1.0)
+        if t:
+            unpack(t, "fo", "qc%d" % t, "qs%d" % t, range(FO))
         scan(O("FL", 0, 16 * n), O("zero", 0, 16 * n), O("CC", 0, 16 * n), MUL, ADD)
         copy(O("d0"), by(O("FL"), O("sl", 0, 5)))
         tt(O("d1"), by(O("FL"), O("sl", 6, 11)), O("W"), MUL)
-        tt(O("M", 0, n), O("FL", 15, 16 * n, 16), steps_between(f + 1, n // 3), MUL)
+        tt(O("M", 0, n), O("FL", 15, 16 * n, 16), O("D", 0, n), MUL)
         entry = [lambda: scan(O("SS"), O("d0"), O("d1"), MUL, ADD), lambda: narrow(O("off", col(f), col(f) + 9), O("SS", 4, 45, 5))]
-        chain = entry + step(f + 4, O("NB", 16, 64)) + [c for k in range(f + 5, 7) for c in step(k)] + [lambda: values(7, 8, "v")]
-        pieces = [[(8, 12), (20, 24), (2, 8)], [(20, 24), (12, 20)], [(8, 12), (20, 24)]][t]
+        chain = entry + step(f + 4, label(f + 5)) + [c for k in range(f + 5, 7) for c in step(k)] + [lambda: values(7, 8, "v")]
+        pieces = [[(8, 12), (20, 24), (12, 18), (6, 8)], [(20, 24), (0, 6), (14, 18)], [(8, 12), (20, 24)]][t]
         if t < 2:
             early, sp = ahead(t + 1)
         else:
-            early = [lambda: ts(O("lu"), O("L"), 1.0 / 320.0, 0.25, MUL, ADD), lambda: copy(O("OB"), by(O("tone"), O("lu")), "s"),
-                     lambda: spread("do1", "owb", "OB", lambda i: 48 * slot(i), lambda i: 0, "y")]
+            early = [lambda: copy(O("OB"), by(O("tone"), O("lu")), "s"),
+                     lambda: spread("do1", "owb", "OB", lambda i: 48 * slot(i), range(8), "y")]
             sp = [[]] * 16
         position = [[lambda: tt(O("PN"), by(O("L"), O("rl", 0, 12)), O("gpat"), NE)],
                     [lambda: scan(O("PC"), O("PN"), O("cpat"), MUL, ADD)],
                     [lambda: ts(O("pos"), O("PC", 7, 192, 8), O("lanef"), None, ADD)]]
         odd, even = [lambda: values(4, 7, "s")], [lambda: values(0, 4, "s")]
-        beside = [[lambda: tt(O("L", *a), O("L", *a), O("M", 0, n), ADD), lambda: tt(O("L", *b), O("L", *b), O("M", 0, n), SUB),
-                   lambda: tt(O("NB", 16, 64), place("ND", f + 5), O("SG"), MUL)],
-                  label_steps(),
-                  [lambda: wide_steps(pieces), lambda: narrow(O("off", col(f + 1), col(f + 1) + 6), O("SS", 49, 75, 5))]]
+        beside = [[lambda: tt(O("L", *a), O("L", *a), O("M", 0, n), ADD), lambda: tt(O("L", *b), O("L", *b), O("M", 0, n), SUB)],
+                  [lambda: ts(O("lu"), O("L"), 1.0 / 320.0, 0.25, MUL, ADD), lambda: wide_labels(pieces)],
+                  [lambda: narrow(O("off", col(f + 1), col(f + 1) + 6), O("SS", 49, 75, 5))]]
         if t == 1:
-            beside += [position[0], odd + even + position[1], position[2], early, sp[0], sp[1]]
+            beside += [position[0], [], odd + even + position[1], position[2], early, sp[0], sp[1]]
             done = 2
         else:
-            beside += [early, odd + sp[0], position[0], sp[1], even + position[1], sp[2], position[2], sp[3], sp[4]]
-            done = 5
+            beside += [position[0], early, odd + sp[0], position[1], sp[1], even + position[2], sp[2], sp[3], sp[4], sp[5]]
+            done = 6
         weave(chain, beside)
-        ts(O("ml%d" % t), by(O("VAL"), O("pos")), O("ux"), None, SUB)
-        spread("own%d" % t, "al%d" % t, "ml%d" % t, lambda i: 48 * i, lambda i: i, "ys")
+        for i in range(2):
+            ts(O("ml%d" % t, 192 * i, 192 * i + 192), by(O("VAL"), O("pos", 12 * i, 12 * i + 12)), 160.0, None, ADD)
+            spread("own%d%d" % (t, i), "al%d" % t, "ml%d" % t, lambda i: 48 * i, range(4 * i, 4 * i + 4), "ys")
         k = send(t, O("pl%d" % t), O("al%d" % t), "rl%d" % t)
         arrives("rl%d" % t, k, [O("pl%d" % t)])
-        if t == 0:
-            quant("eq", "eqs", "ec", 0, 512)
         unpack(t, "fp", "lc%d" % t, "lp%d" % t)
-        copy(O("BG"), by(O("PS", 0, 320), O("al%d" % t)), "s")
-        unpack(t, "fo", "qc%d" % t, "qs%d" % t)
-        list_b = [lambda: scan(O("BS"), O("rise", 0, 320), O("BG")), lambda: narrow(O("bl%d" % t), O("BS", 15, 320, 16))]
-        extra = {done: [lambda: score_list(t + 1)] if t < 2 else [], 12: list_b[:1], 13: list_b[1:]}
+        copy(O("BG"), by(O("P", 0, 320), O("al%d" % t)), "s")
+        if t:
+            unpack(t, "fo", "qc%d" % t, "qs%d" % t, range(FO, 4))
+        extra = {}
+        if t < 2:
+            extra.update(zip((done, done + 1, done + 2), score_list(t + 1)))
         if t == 0:
-            extra[8] = [lambda: quant("vq", "vqs", "vt", 0, 128)]
+            extra[10] = [lambda: quant("vq", "vqs", "vt", 0, 128)]
         if t == 2:
-            extra[11] = [lambda: copy(O("ow"), O("owb")), lambda: copy(O("olf"), by(O("i320"), O("ow"))),
+            extra[11] = [lambda: copy(O("ow"), O("owb")), lambda: ts(O("olf"), by(O("i320"), O("ow")), 160.0, None, ADD),
                          lambda: dmas("dout", [("y", T.ol[:], T.olf[0:128:16, 0:320], [], O("olf")[1])])]
-        for i in range(done, 16):
+        list_b = [lambda: scan(O("BS"), O("rise", 0, 320), O("BG")), lambda: narrow(O("bl%d" % t), O("BS", 15, 320, 16))]
+        cut = CUT[t]
+        if t != 1:
+            extra[cut - 2], extra[cut - 1], list_b = list_b[:1], list_b[1:], []
+        for i in range(done, cut):
             for call in sp[i] + extra.get(i, []):
                 call()
-        for lo, hi in ZCH:
+        for i, (lo, hi) in enumerate(ZCH):
             o = O("pl%d" % t, lo // 16, hi // 16)
             for b in range(4):
-                copy(O("zt%d" % t, 4 * lo + b, 4 * hi, 4), by(O("fp%d" % t, 320 * b, 320 * b + 320), o), "v" if b < 2 else "s")
+                copy(O("zt%d" % t, 4 * lo + b, 4 * hi, 4), by(O("fp%d" % t, 320 * b, 320 * b + 320), o), ZQ[i][b])
             quant("zc%d" % t, "zs%d" % t, "zt%d" % t, lo, hi)
+        for call in list_b:
+            call()
+        rest = [c for cs in sp[cut:] for c in cs]
         for i, (lo, hi) in enumerate(ZCH):
             for b in range(4):
                 p = mx("wq", 128 * b, "zc%d" % t, lo, hi, "zs%d" % t)
@@ -537,7 +530,9 @@ def rank_program(g, core, T, topo):
                 tt(O("xt%d" % (t + 1), 4 * lo + b, 4 * hi, 4), by(O("rb%d" % b), o), O("fo%d" % t, 320 * b + lo, 320 * b + hi), ADD)
             quant("qc%d" % (t + 1), "qs%d" % (t + 1), "xt%d" % (t + 1), lo, hi)
             if t < 2:
-                scores(t + 1, i, SQ[i])
+                for call in rest[:1] if i == 0 else rest[1:]:
+                    call()
+                scores(t + 1, lo, hi, SQ[i])
             else:
                 o, y = O("qc3", lo, hi), O("yb", lo, hi)
                 copy(y, mx("vq", 0, "qc3", lo, hi, "qs3"), "s")

@@ -9,14 +9,13 @@ BIG = 1048576.0
 RISE = 8192.0
 FAR = 1e29
 STEP = [1, 2, 4]
-SQ = ["s", "vvsvsvsv"]
 RQ = ["ssss", "vvss"]
-TQ = "v"
-CUT = [16, 16, 16]
-ZQ = ["vvss", "vsss"]
-FO = 2
+ZQ = ["vvss", "vvss"]
+PQ = "s"
+WH = [[4, 7, 9], [2, 4, 6], [4, 7, 9]]
+TAKE = [[[0, 0, 0, 2, 0, 1, 1, 0, 1, 1, 0, 1], [1, 0, 1], 6, 0, 0, 2], [[0, 0, 0, 2, 0, 1, 0, 1, 1], [1, 0, 1], 6, 0, 0, 2], [[0, 0, 0, 1, 0, 1, 1, 0, 1, 0, 1, 0], [0, 0, 0], 0, 0, 0, 0]]
 ZCH = [(0, 192), (192, 320)]
-CH = [(0, 160), (160, 320)]
+CH = [(0, 192), (192, 320)]
 
 SCRATCH = {}
 
@@ -36,29 +35,30 @@ def _share(buf, dtype, *parts):
     _d(buf, at, dtype)
 
 
-_share("iv", "int32", ("pint", 1), ("lanei", 1), ("hi", 1), ("xi", 1), ("sxi", 1), ("sx7", 1), ("upi", 16), ("mi", 24), ("pi0", 24),
-       ("pi1", 24), ("pi2", 24), ("t8", 8), ("t8a", 8), ("t8b", 8))
-_share("fv", "float32", ("lanef", 1), ("hf", 1), ("h2", 1), ("kap2", 1), ("kap", 1), ("lan16", 1), ("ge20", 24), ("ge40", 24), ("ja", 48),
-       ("jf", 48), ("i16", 16), ("z16", 16), ("t320", 8), ("tone", 8), ("wd", 8), ("r3", 9), ("z24", 24))
-_share("ov", "float32", ("W", 80), ("a2", 8), ("D", 12), ("fs", 24), ("L", 24), ("M", 12), ("d0", 80), ("d1", 80), ("SS", 80),
-       ("a1", 6), ("e1", 3), ("e3", 3), ("k1", 3), ("k2", 3), ("dB", 3), ("xB", 3))
-_share("uv", "uint16", ("ogu", 20), ("upu", 16), ("cl", 24), ("ln", 24), ("rl", 24), ("sl", 12), ("lu", 24), ("ow", 20))
-_share("wv", "float32", ("SG", 48), ("SC", 48), ("G2", 96), ("T1", 96), ("T2", 96), ("T3", 96), ("T4", 96))
+_share("iv", "int32", ("pint", 1), ("lanei", 1), ("xi", 1), ("hi", 1), ("ei", 1), ("quadi", 1), ("upi", 1), ("kk", 24), ("k1i", 24), ("k2i", 24),
+       ("t8", 8), ("t8a", 8), ("t8b", 8), ("t8c", 8), ("t8d", 8), ("o32", 32), ("f0", 2), ("f1", 2), ("f2", 2))
+_share("fv", "float32", ("lanef", 1), ("xf", 1), ("hf", 1), ("ef", 1), ("quadf", 1), ("upf", 1), ("h8", 1), ("q8", 1), ("x3", 1), ("c5", 1),
+       ("kap2", 1), ("kap", 1), ("bb", 24), ("cb", 24), ("k20", 24), ("j16", 3), ("oa", 32), ("ob", 32), ("b12", 12), ("d12", 12), ("c2", 2),
+       ("f3", 2), ("f4", 2), ("f5", 2), ("f6", 2), ("q24", 24), ("p24", 24),
+       ("i16", 16), ("z16", 16), ("t320", 8), ("tone", 8), ("wd", 8), ("c8", 8), ("cap8", 8))
+_share("ov", "float32", ("W", 80), ("a2", 8), ("FL", 16), ("D", 12), ("L", 24), ("M", 12), ("d0", 80), ("d1", 80), ("SS", 80),
+       ("a1", 6), ("e1", 3), ("k1", 3), ("dB", 3), ("xB", 3))
+_share("uv", "uint16", ("ogl", 2), ("upu", 8), ("gl", 24), ("fl", 24), ("fin", 2), ("ln", 24), ("rl", 24), ("sl", 12), ("lu", 24), ("ow", 32),
+       ("pol", 24))
+_share("wv", "float32", ("SC", 48), ("G2", 96), ("T1", 96), ("T2", 96), ("T3", 96), ("T4", 96))
 _d("pgi", 40, "int32")
-_d("ogi", 20, "int32")
-for _n, _c in (("rise", 384), ("zero", 192), ("cap", 192), ("pats", 384), ("patx", 384), ("gpat", 192), ("c0", 192), ("cpat", 192),
-               ("lab", 320), ("N", 384), ("E", 192), ("CC", 192), ("FL", 200), ("G", 64), ("VAL", 384), ("SF", 384), ("sel", 192), ("selx", 192),
-               ("PN", 192), ("PC", 192), ("ST", 2560), ("BG", 320), ("BS", 320),
+_d("OG", 160, "int32")
+for _n, _c in (("rise", 384), ("gpat", 192), ("c0", 192), ("cpat", 192), ("N", 384), ("G", 64), ("sel", 192), ("selx", 192), ("MK", 384), ("GS", 384), ("TS", 384), ("SE", 384),
+               ("PN", 192), ("PC", 192), ("ST", 320), ("BG", 320), ("BS", 320), ("tb2", 320), ("tb3", 320),
                ("rb0", 320), ("rb1", 320), ("rb2", 320), ("rb3", 320), ("olf", 320), ("yb", 320)):
     _d(_n, _c, "float32")
-for _n, _c in (("pu", 40), ("off", 26), ("of2", 26), ("pos", 24), ("fl0", 26), ("fl1", 26), ("fl2", 26)):
+for _n, _c in (("pu", 80), ("off", 26), ("of2", 26), ("pos", 24)):
     _d(_n, _c, "uint16")
 for _t in range(3):
-    _d("ml%d" % _t, 384, "uint16")
-    _d("al%d" % _t, 20, "uint16")
+    _d("al%d" % _t, 32, "uint16")
     _d("pl%d" % _t, 20, "uint16")
     _d("bl%d" % _t, 20, "uint16")
-    _d("fo%d" % _t, 1280, "bfloat16")
+    _d("fo%d" % _t, 640, "bfloat16")
     _d("fp%d" % _t, 1280, "bfloat16")
     _d("zt%d" % _t, 1280, "bfloat16")
     _d("zc%d" % _t, 320, "float8_e4m3fn_x4")
@@ -69,15 +69,16 @@ for _t in range(4):
     _d("xt%d" % _t, 1280, "bfloat16")
     _d("qc%d" % _t, 320, "float8_e4m3fn_x4")
     _d("qs%d" % _t, 320, "uint8")
-for _n, _c in (("ones", 516), ("ec", 516), ("i320", 320), ("P", 2560), ("ut", 512), ("vt", 512), ("OB", 384), ("owb", 20)):
+for _n, _c in (("ones", 516), ("ec", 516), ("i320", 320), ("P", 2560), ("ut", 512), ("vt", 512), ("OB", 384), ("PK", 384), ("PT", 384), ("TM", 32),
+               ("OT", 384), ("VAL", 384), ("VT", 384), ("far", 384), ("r16", 384)):
     _d(_n, _c, "bfloat16")
-for _n, _c in (("eq", 512), ("wq", 512), ("uq", 128), ("uw", 256), ("vq", 128)):
+for _n, _c in (("eq", 512), ("wq", 512), ("uq", 128), ("uw", 128), ("vq", 128)):
     _d(_n, _c, "float8_e4m3fn_x4")
     _d(_n + "s", _c, "uint8")
 for _k in range(8):
     _d("ps%d" % _k, 512, "float32", "psum")
 
-DMA_SEMS = ["dpg", "dog", "du", "dxa", "dxb", "dw", "dv", "dp", "own00", "own01", "own10", "own11", "own20", "own21", "do1", "dout"]
+DMA_SEMS = ["dpg", "dog", "du", "dx", "dw", "dp", "dout"]
 SEMAPHORES = ["cv", "cs", "ct", "cg", "left", "rq0", "rq1", "rq2", "rl0", "rl1", "rl2"] + DMA_SEMS
 
 
@@ -156,20 +157,15 @@ def rank_program(g, core, T, topo):
         note(reads, writes, (sem, total[sem], snap, q))
 
     def dmas(sem, items):
-        snap, acc = {}, []
+        snap = {}
         for q, out, in_, writes, reads in items:
             order(q, reads, writes, True)
             queue[q].dma_start(out, in_).then_inc(T.sem[sem], 16)
             total[sem] += 16
             for s2, v2 in clock[q].items():
                 snap[s2] = max(snap.get(s2, 0), v2)
-            acc.append((reads, writes))
-        for reads, writes in acc:
+        for q, out, in_, writes, reads in items:
             note(reads, writes, (sem, total[sem], snap, "dma"))
-
-    def arrives(sem, val, outs):
-        total[sem] += val
-        note([], [r for o in outs for r in o[1]], (sem, val, {}, "far"))
 
     def copy(out, in_, q="v"):
         if q == "v":
@@ -192,8 +188,11 @@ def rank_program(g, core, T, topo):
     def act(out, in_, scale, bias):
         run("s", [out], [in_], lambda: g.scalar.activation(out[0], in_[0], FN.Identity, bias=bias, scale=scale))
 
-    def scan(out, d0, d1, op0=ADD, op1=MAX, first=0.0):
-        run("v", [out], [d0, d1], lambda: g.vector.tensor_tensor_scan(out[0], d0[0], d1[0], first, op0, op1))
+    def scan(out, d0, d1, op0=ADD, op1=MAX):
+        run("v", [out], [d0, d1], lambda: g.vector.tensor_tensor_scan(out[0], d0[0], d1[0], 0.0, op0, op1))
+
+    def turn(out, in_):
+        run("v", [out], [in_], lambda: g.vector.transpose(out[0], in_[0]))
 
     def fill(out, value):
         run("v", [out], [], lambda: g.vector.memset(out[0], value))
@@ -202,21 +201,23 @@ def rank_program(g, core, T, topo):
         kw = {} if SCRATCH[out[1][0][0]][2] == "int32" else {"allow_small_or_imprecise_dtypes": True}
         run("g", [out], [], lambda: g.iota(out[0], pattern, base, mul, **kw))
 
-    def select(out, in_, pattern, fill_, base=0, mul=0, op=EQ):
+    def select(out, in_, pattern, op, fill_, base=0, mul=0):
         run("g", [out], [in_], lambda: g.affine_select(out[0], in_[0], pattern, op, fill_, base, mul))
 
-    def quant(cn, sn, xn, lo, hi):
-        q, s, x = O(cn, lo, hi), O(sn, lo, hi), O(xn, 4 * lo, 4 * hi)
+    def pack(q, s, x):
         run("v", [q, s], [x], lambda: g.vector.quantize_mx(q[0], s[0], x[0]))
+
+    def quant(cn, sn, xn, lo, hi):
+        pack(O(cn, lo, hi), O(sn, lo, hi), O(xn, 4 * lo, 4 * hi))
 
     bank = [0]
 
-    def mx(an, alo, bn, lo, hi, bsn=None, asn=None):
+    def mx(an, alo, bn, lo, hi, bsn):
         k = bank[0] % 8
         bank[0] += 1
         out = O("ps%d" % k, 0, hi - lo)
         full = (out[0], O("ps%d" % k)[1])
-        a, s = O(an, alo, alo + 128), O(asn or an + "s", alo, alo + 128)
+        a, s = O(an, alo, alo + 128), O(an + "s", alo, alo + 128)
         b, p = O(bn, lo, hi), O(bsn, lo, hi)
         run("t", [full], [a, s, b, p], lambda: g.tensor.matmul_mx(out[0], a[0], s[0], b[0], p[0], True, True))
         return full
@@ -224,104 +225,137 @@ def rank_program(g, core, T, topo):
     def narrow(out, wide, climb="kap2"):
         ts(out, wide, O(climb), None, SUB)
 
+    def later(f, *args):
+        return lambda: f(*args)
+
+    def weave(chain, beside):
+        for i in range(max(len(chain), len(beside))):
+            for call in chain[i:i + 1] + (beside[i] if i < len(beside) else []):
+                call()
+
     def load(q, name, src, lo, hi, rows=(0, 128)):
         o = O(name, lo, hi, 1, rows)
         return (q, o[0], src, o[1], [])
 
     dmas("dpg", [load("y", "pgi", T.pg[:], 0, 20), load("s", "pgi", T.pg[0:112, :], 20, 40, (16, 128)),
                  load("y", "pgi", T.pg[112:128, :], 20, 40, (0, 16))])
-    dmas("dog", [("s" if k % 2 else "y", T.ogi[k:128:8, 0:20], T.og[16 * k:16 * k + 16, 0:20], O("ogi")[1] if k == 0 else [], [])
-                 for k in range(8)])
-    dmas("dxa", [load("y", "xt0", T.x[:, 0:768], 0, 768)])
+    dmas("dog", [load("s", "OG", T.og[0:112, :], 20, 40, (16, 128)), load("y", "OG", T.og[:], 0, 20),
+                 load("s", "OG", T.og[112:128, :], 20, 40, (0, 16))])
+    dmas("dx", [load("y", "xt0", T.x[:], 0, 1280)])
     dmas("du", [load("s", "ut", T.u[:], 0, 512)])
-    dmas("dxb", [load("y", "xt0", T.x[:, 768:1280], 768, 1280)])
+    dmas("dw", [("y", codes(O("wq"))[0], T.wc[:], O("wq")[1], []), ("y", O("wqs")[0], T.ws[:], O("wqs")[1], []),
+                load("y", "vt", T.v[:], 0, 512)])
 
     fill(O("ones"), 1.0)
-    fill(O("sel"), 193.0)
+    fill(O("sel"), 13.0)
     iota(O("pint"), [[1, 1]], 0, 1)
     iota(O("i16"), [[1, 16]], 0)
-    iota(O("t8"), [[-1, 8]], 8)
-    iota(O("mi"), [[0, 8], [16, 3]], 0)
-    iota(O("pi0"), [[1, 2], [2, 4], [256, 3]], 0)
+    iota(O("kk"), [[-1, 2], [-2, 4], [0, 3]], 8)
+    iota(O("bb"), [[0, 8], [2, 3]], 0)
     iota(O("i320"), [[1, 320]], -160)
-    iota(O("upi"), [[0, 2], [16, 8]], 0)
-    iota(O("ja", 0, 40), [[1, 2], [16, 20]], -160)
-    iota(O("ja", 40, 48), [[16, 8]], -160)
-    select(O("ec"), O("ones"), [[-1, 516]], 0.0, 3, 4)
-    iota(O("pats", 0, 192), [[0, 8], [1, 3], [3, 8]], 0)
-    iota(O("pats", 192, 384), [[1, 8], [0, 24]], 0)
+    iota(O("t8"), [[-1, 8]], 8)
     iota(O("wd"), [[320, 8]], 0)
-    iota(O("sel", 1, 75, 5), [[0, 5], [16, 3]], 15)
-    iota(O("sel", 2, 75, 5), [[0, 5], [16, 3]], 63)
-    iota(O("sel", 99, 171, 5), [[0, 5], [16, 3]], 15)
-    iota(O("sel", 100, 141, 5), [[48, 3], [16, 3]], 15)
-    iota(O("c0"), [[0, 8], [16, 3], [0, 8]], 336)
-    select(O("cpat"), O("c0"), [[0, 24], [1, 8]], -48.0, -7)
 
-    ts(O("lanei"), O("pint"), 15, None, AND)
-    ts(O("hi"), O("pint"), 4, None, SHR)
-    fill(O("off"), 0)
-    copy(O("lanef"), O("lanei"))
-    copy(O("hf"), O("hi"))
-    fill(O("sel", 0, 80, 5), 192.0)
+    for name, shift, mask in (("lane", 0, 15), ("x", 0, 7), ("h", 4, 7), ("e", 4, 1), ("quad", 5, 3), ("up", 3, 1)):
+        ts(O(name + "i"), O("pint"), shift, mask, SHR, AND)
+    copy(O("fv", 0, 48, 8), O("iv", 8, 56, 8))
+    fill(O("sel", 0, 80, 5), 12.0)
+    fill(O("oa"), 0.0)
     ts(O("z16"), O("i16"), O("lanef"), None, NE)
     ts(O("ln"), O("ones", 0, 24), O("lanef"), None, MUL)
-    ts(O("t8a"), O("t8"), O("hf"), None, ADD)
-    ts(O("lan16"), O("lanef"), 16.0, None, MUL)
-    ts(O("pi1"), O("mi"), O("lanef"), None, ADD)
+    ts(O("c5"), O("quadf"), 5.0, O("ef"), MUL, ADD)
+    ts(O("k1i"), O("kk"), O("hf"), None, ADD)
     act(O("rise"), by(O("z16"), O("ln")), BIG + RISE, -BIG)
-    ts(O("t8b"), O("t8a"), 7, None, AND)
-    ts(O("ge20"), O("pi1"), 20.0, -312.0, GE, MUL)
-    ts(O("ge40"), O("pi1"), 40.0, -328.0, GE, MUL)
-    ts(O("pi2"), O("pi0"), O("lan16"), None, ADD)
-    ts(O("t320"), O("t8b"), 320.0, None, MUL)
     ts(O("kap"), O("lanef"), -RISE, 15 * RISE, MUL, ADD)
-    tt(O("ge20"), O("ge20"), O("ge40"), ADD)
     ts(O("kap2"), O("lanef"), -RISE, 15 * RISE - 160.0, MUL, ADD)
-    ts(O("h2"), O("hf"), 2.0, None, MUL)
-    tt(O("pi2"), O("pi2"), O("ge20"), ADD)
-    fill(O("ov", 0, 88), 0.0)
-    copy(O("cl"), O("pi2"))
+    ts(O("cb"), O("bb"), O("c5"), 19.0, ADD, MIN)
+    ts(O("k2i"), O("k1i"), 7, None, AND)
+    ts(O("h8"), O("hf"), 8.0, None, ADD)
+    ts(O("j16"), O("cb", 0, 3), 16.0, O("lanef"), MUL, ADD)
+    ts(O("k20"), O("k2i"), 20.0, None, MUL)
+    fill(O("off"), 0)
+    ts(O("upu"), O("ones", 0, 8), O("xf"), 16.0, MUL, MUL)
+    tt(O("oa", 0, 24), O("k20"), O("cb"), ADD)
 
-    copy(O("pu"), O("pgi"))
-    copy(O("P", 0, 320), by(O("i320"), O("pu", 0, 20)))
-    copy(O("P", 320, 640), by(O("i320"), O("pu", 20, 40)), "s")
-    copy(O("ogu"), O("ogi"))
-    items = []
-    for s in range(1, 4):
-        for q, to, fro in (("y", (32 * s, 128), (0, 128 - 32 * s)), ("s", (0, 32 * s), (128 - 32 * s, 128))):
-            o, i = O("P", 640 * s, 640 * s + 640, 1, to), O("P", 0, 640, 1, fro)
-            items.append((q, o[0], i[0], o[1], i[1]))
-    dmas("dp", items)
-    dmas("dw", [("y", codes(O("wq"))[0], T.wc[:], O("wq")[1], []), ("y", O("wqs")[0], T.ws[:], O("wqs")[1], [])])
-    dmas("dv", [load("y", "vt", T.v[:], 0, 512)])
-    copy(O("lab"), by(O("t320"), O("ogu")))
-    copy(O("upu"), O("upi"))
-    copy(O("N"), by(O("lab"), O("cl")), "s")
-    ts(O("jf"), O("ja"), O("h2"), None, ADD)
+    iota(O("sel", 1, 75, 5), [[0, 5], [1, 3]], 0)
+    iota(O("sel", 2, 75, 5), [[0, 5], [1, 3]], 3)
+    iota(O("sel", 99, 171, 5), [[0, 5], [1, 3]], 0)
+    iota(O("sel", 100, 141, 5), [[1, 9]], 0)
+    iota(O("b12"), [[0, 4], [1, 3]], 0)
+    iota(O("d12"), [[2, 4], [0, 3]], 0)
+    iota(O("c2"), [[16, 2]], -2)
+
+    def quarters(name, width, to, fro, shift, qs, step=1):
+        size = [128, 32, 64, 32][shift]
+        for n, p in enumerate(range(0, 128, size)):
+            at = (p + 32 * shift) % 128
+            copy(O(name, to, to + width, 1, (at, at + size)), O(fro[0], fro[1], fro[1] + width * step, step, (p, p + size)), qs[n % len(qs)])
+
+    def table(s, q):
+        copy(O("P", 320 * s, 320 * s + 320), by(O("i320"), O("pu", 20 * s, 20 * s + 20)), q)
+
+    copy(O("pu", 0, 40), O("pgi"))
+    quarters("pu", 40, 40, ("pgi", 0), 1, "v")
+    table(0, "s")
+    table(1, "s")
+    scan(O("ob"), O("rise", 0, 32), O("oa"))
+    table(2, "v")
+    quarters("OG", 40, 40, ("OG", 0), 1, "v")
+    narrow(O("ogl"), O("ob", 15, 32, 16), "kap")
+    table(3, "v")
+    quarters("OG", 80, 80, ("OG", 0), 2, "v")
+    ts(O("t8a"), O("t8"), O("hf"), None, ADD)
+    copy(O("P", 1280, 2560, 1, (0, 64)), O("P", 0, 1280, 1, (64, 128)), PQ)
+    copy(O("o32"), by(O("OG"), O("ogl")))
+    ts(O("t8b"), O("t8a"), 7, None, AND)
+    fill(O("ov", 0, 101), 0.0)
+    ts(O("k1i"), O("o32", 0, 24), -1.0, O("h8"), MUL, ADD)
     copy(O("tone"), O("t8b"))
-    fill(O("FL", 192, 193), 0.0)
-    fill(O("FL", 193, 200), 1.0)
+    fill(O("FL", 13, 16), 1.0)
+    ts(O("c8"), O("i16", 0, 8), O("xf"), 2 * FAR, EQ, MUL)
+    ts(O("k2i"), O("k1i"), 7, None, AND)
+    fill(O("far"), FAR)
+    copy(O("lu"), O("k2i"))
+    ts(O("L"), O("k2i"), 320.0, None, MUL)
+    copy(O("N", 192, 384), by(O("wd"), O("lu", 12, 24)), "s")
+    copy(O("N", 0, 192), by(O("wd"), O("lu", 0, 12)), "s")
+    for c in range(3):
+        ts(O("off", c, c + 1), O("k2i", c, c + 1), 320.0, O("j16", c, c + 1), MUL, ADD)
+    copy(O("P", 1280, 2560, 1, (64, 128)), O("P", 0, 1280, 1, (0, 64)))
+    ts(O("cap8"), O("c8"), FAR, None, SUB)
+    quant("uq", "uqs", "ut", 0, 128)
+    select(O("ec"), O("ones"), [[-1, 516]], EQ, 0.0, 3, 4)
+    select(O("r16"), O("far"), [[0, 24], [1, 16]], NE, -FAR)
 
-    def scores(t, lo, hi, qs):
-        for s in range(8):
-            p = mx("uw", 16 * (8 - s), "qc%d" % t, lo, hi, "qs%d" % t)
-            copy(O("ST", 320 * s + lo, 320 * s + hi), p, qs[s % len(qs)])
+    lists = [later(ts, O("x3"), O("xf"), 3.0, None, MUL), later(ts, O("t8c"), O("t8"), O("ef"), None, ADD),
+             later(ts, O("rl", 0, 12), O("b12"), O("x3"), None, ADD), later(ts, O("t8d"), O("t8c"), 7, None, AND),
+             later(ts, O("rl", 12, 24), O("d12"), O("upf"), None, ADD), later(ts, O("t320"), O("t8d"), 320.0, None, MUL),
+             later(ts, O("f0"), O("c2"), O("lanef"), 0.2, ADD, MUL), later(copy, O("gpat"), by(O("t320"), O("rl", 12, 24)), "s"),
+             later(ts, O("q8"), O("quadf"), 8.0, None, ADD), later(ts, O("f3"), O("f0"), -5.0, O("lanef"), MUL, ADD),
+             later(ts, O("f1"), O("f0"), -1.0, O("q8"), MUL, ADD), later(tt, O("f4"), O("f3"), O("c2"), ADD),
+             later(ts, O("f2"), O("f1"), 3, None, AND), later(ts, O("f5"), O("f2"), 6.0, 2.0, MUL, ADD),
+             later(tt, O("f6"), O("f5"), O("f4"), ADD), later(copy, O("fin"), O("f6"))]
+    by_position = [later(ts, O("k1i"), O("q24"), O("quadf"), None, ADD), later(ts, O("k2i"), O("k1i"), 3, None, AND),
+                   later(ts, O("k20"), O("k2i"), 48.0, O("lanef"), MUL, ADD), later(tt, O("cb"), O("k20"), O("p24"), ADD),
+                   later(copy, O("pol"), O("cb"))]
 
     partner = [T.cores[rank ^ s] for s in STEP]
 
-    def send(t, out, in_, sem):
+    def send(t, pairs, sem):
         rid, pid, _s = topo.addr(partner[t])
         eng = topo.engines(core, partner[t])
-        order("g", in_[1], [])
-        g.remote_dma(out[0], in_[0], T.sem[sem], T.sem.left, pid=pid, routing_id=rid, dma_engine_mask=sum(1 << e for e in eng))
-        total["left"] += len(eng)
-        return len(eng)
+        for out, in_ in pairs:
+            order("g", in_[1], [])
+            g.remote_dma(out[0], in_[0], T.sem[sem], T.sem.left, pid=pid, routing_id=rid, dma_engine_mask=sum(1 << e for e in eng))
+            total["left"] += len(eng)
+            total[sem] += len(eng)
+        note([], [r for out, in_ in pairs for r in out[1]], (sem, total[sem], {}, "far"))
 
     def send_state(t):
-        n = send(t, codes(O("lc%d" % t)), codes(O("qc%d" % t)), "rq%d" % t)
-        n += send(t, O("lp%d" % t), O("qs%d" % t), "rq%d" % t)
-        arrives("rq%d" % t, n, [O("lc%d" % t), O("lp%d" % t)])
+        send(t, [(codes(O("lc%d" % t)), codes(O("qc%d" % t))), (O("lp%d" % t), O("qs%d" % t))], "rq%d" % t)
+
+    def scores(t, lo, hi, q):
+        copy(O("ST", lo, hi), mx("uw", 0, "qc%d" % t, lo, hi, "qs%d" % t), q)
 
     def col(k):
         return 22 if k == 7 else 3 * slot(k)
@@ -335,187 +369,165 @@ def rank_program(g, core, T, topo):
     def kept(name, lo=0, hi=1):
         return O(name, 48 * lo + 15, 48 * hi, 16)
 
-    def step(k, add=None):
+    def label(k):
+        return O("L", 3 * slot(k), 3 * slot(k) + 3)
+
+    def step(k, wide=True):
         odd = col(k) % 2
         gk = O("G", 16 - 16 * odd, 64)
         pk = by(O("P"), O("off", col(k) - odd, col(k) + 3))
-        if add is None:
-            return [lambda: tt(gk, pk, place("N", k + 1, 16 * odd), ADD),
-                    lambda: scan(O("SC"), O("rise", 0, 48), O("G", 16, 64)),
-                    lambda: narrow(off(k + 1), kept("SC"))]
-        return [lambda: copy(gk, pk), lambda: scan(O("SC"), O("rise", 0, 48), O("G", 16, 64)),
-                lambda: tt(O("e1"), kept("SC"), add, ADD), lambda: narrow(off(k + 1), O("e1"))]
-
-    def weave(chain, beside):
-        beside = list(beside)
-        for i, call in enumerate(chain):
-            call()
-            for c in (beside[i] if i < len(beside) else []):
-                c()
+        keep = later(scan, O("SC"), O("rise", 0, 48), O("G", 16, 64))
+        if wide:
+            return [later(tt, gk, pk, place("N", k + 1, 16 * odd), ADD), keep, later(narrow, off(k + 1), kept("SC"))]
+        return [later(copy, gk, pk), keep,
+                lambda: [ts(O("off", col(k + 1) + c, col(k + 1) + c + 1), O("SC", 16 * c + 15, 16 * c + 16), O("e1", c, c + 1), None, ADD) for c in range(3)]]
 
     first = [0, 1, 0]
 
     def sides(t):
         return ((12, 21), (3, 12)) if t == 1 else ((0, 12), (12, 24))
 
-    def label(k):
-        return O("L", 3 * slot(k), 3 * slot(k) + 3)
-
-    def ahead(t):
+    def ahead(t, q="v"):
         f = first[t]
         w = lambda q, r, n=1: O("W", 15 * q + r, 15 * (q + n), 5)
         rise = O("rise", 0, 96)
         ps = lambda lo, hi: by(O("P"), O("of2", lo, hi))
         a, b = sides(t)
-        early = [lambda: ts(w(0, 2, 2), O("off", col(f), col(f) + 6), O("kap2"), None, ADD),
-                 lambda: tt(O("D", 0, a[1] - a[0]), O("L", *b), O("L", *a), SUB)]
-        chain = [lambda: tt(O("a1"), w(0, 2, 2), O("D", 0, 6), ADD),
-                 lambda: narrow(O("of2", 0, 6), O("a1")),
-                 lambda: tt(O("G2"), ps(0, 6), O("N", 48 * slot(f), 48 * slot(f) + 96), ADD),
-                 lambda: scan(O("T1"), rise, O("G2")),
-                 lambda: narrow(O("of2", 6, 12), kept("T1", 0, 2)),
-                 lambda: copy(O("G2"), ps(6, 12), TQ),
-                 lambda: scan(O("T2"), rise, O("G2")),
-                 lambda: (tt(O("a2", 0, 3), kept("T2"), label(f + 2), ADD), tt(O("a2", 4, 7), kept("T2"), label(f + 3), ADD)),
-                 lambda: narrow(O("of2", 12, 19), O("a2", 0, 7)),
-                 lambda: (tt(O("G2", 0, 48), ps(12, 15), place("N", f + 3), ADD), tt(O("G2", 48, 96), ps(16, 19), place("N", f + 2), ADD)),
-                 lambda: scan(O("T3"), rise, O("G2")),
-                 lambda: narrow(O("of2", 20, 26), kept("T3", 0, 2)),
-                 lambda: copy(O("G2"), ps(20, 26), TQ),
-                 lambda: scan(O("T4"), rise, O("G2")),
-                 lambda: (tt(w(2, 3), kept("T4"), O("k1"), ADD), tt(O("dB"), kept("T4", 1, 2), kept("T2", 1, 2), SUB)),
-                 lambda: tt(w(2, 0), O("dB"), w(2, 3), SUB)]
-        beside = [[lambda: copy(w(0, 4, 3), O("D", 0, 9))], [], [],
-                  [lambda: ts(w(3, 2, 2), O("off", col(f + 1), col(f + 1) + 6), O("kap2"), None, ADD)],
-                  [lambda: tt(w(3, 3), kept("T1"), w(3, 2), SUB)],
-                  [lambda: tt(w(4, 1), kept("T1", 1, 2), w(4, 2), SUB)],
-                  [lambda: ts(w(2, 2), off(f + 4), O("kap2"), None, ADD)], [],
-                  [lambda: tt(w(1, 3), O("a2", 0, 3), w(1, 2), SUB)],
-                  [lambda: tt(O("k1"), label(f + 4), w(2, 2), SUB)], [],
-                  [lambda: tt(w(4, 3), kept("T3"), w(4, 2), SUB), lambda: tt(O("xB"), kept("T3", 1, 2), kept("T1", 1, 2), SUB)],
-                  [lambda: tt(w(2, 1), kept("T2", 1, 2), O("k1"), ADD)],
-                  [lambda: tt(w(4, 0), O("xB"), w(4, 3), SUB)], [], []]
-        return early, [[c] + b for c, b in zip(chain, beside)]
+        return [[later(ts, w(0, 2, 2), O("off", col(f), col(f) + 6), O("kap2"), None, ADD)],
+                [later(tt, O("D", 0, a[1] - a[0]), O("L", *b), O("L", *a), SUB)],
+                [later(tt, O("a1"), w(0, 2, 2), O("D", 0, 6), ADD), later(copy, w(0, 4, 3), O("D", 0, 9))],
+                [later(narrow, O("of2", 0, 6), O("a1"))],
+                [later(tt, O("G2"), ps(0, 6), O("N", 48 * slot(f), 48 * slot(f) + 96), ADD)],
+                [later(scan, O("T1"), rise, O("G2")), later(ts, w(3, 2, 2), O("off", col(f + 1), col(f + 1) + 6), O("kap2"), None, ADD)],
+                [later(narrow, O("of2", 6, 12), kept("T1", 0, 2)), later(tt, w(3, 3), kept("T1"), w(3, 2), SUB)],
+                [later(copy, O("G2"), ps(6, 12), q), later(tt, w(4, 1), kept("T1", 1, 2), w(4, 2), SUB)],
+                [later(scan, O("T2"), rise, O("G2")), later(ts, w(2, 2), off(f + 4), O("kap2"), None, ADD)],
+                [later(tt, O("a2", 0, 3), kept("T2"), label(f + 2), ADD), later(tt, O("a2", 4, 7), kept("T2"), label(f + 3), ADD)],
+                [later(narrow, O("of2", 12, 19), O("a2", 0, 7)), later(tt, w(1, 3), O("a2", 0, 3), w(1, 2), SUB)],
+                [later(tt, O("G2", 0, 48), ps(12, 15), place("N", f + 3), ADD), later(tt, O("G2", 48, 96), ps(16, 19), place("N", f + 2), ADD),
+                 later(tt, O("k1"), label(f + 4), w(2, 2), SUB)],
+                [later(scan, O("T3"), rise, O("G2")), later(tt, w(2, 1), kept("T2", 1, 2), O("k1"), ADD)],
+                [later(narrow, O("of2", 20, 26), kept("T3", 0, 2)), later(tt, w(4, 3), kept("T3"), w(4, 2), SUB)],
+                [later(copy, O("G2"), ps(20, 26), q), later(tt, O("xB"), kept("T3", 1, 2), kept("T1", 1, 2), SUB)],
+                [later(scan, O("T4"), rise, O("G2")), later(tt, w(4, 0), O("xB"), w(4, 3), SUB)],
+                [later(tt, w(2, 3), kept("T4"), O("k1"), ADD), later(tt, O("dB"), kept("T4", 1, 2), kept("T2", 1, 2), SUB)],
+                [later(tt, w(2, 0), O("dB"), w(2, 3), SUB)]]
 
     def values(lo, hi, q):
         c = 22 if lo == 7 else 3 * lo
         copy(O("VAL", 48 * lo, 48 * hi), by(O("P"), O("off", c, c + 3 * (hi - lo))), q)
 
-    def score_list(t):
-        if t == 1:
-            ends = [lambda: narrow(O("fl1", 1, 13), O("fs", 0, 12)), lambda: narrow(O("fl1", 14, 26), O("fs", 12, 24))]
-        else:
-            ends = [lambda: narrow(O("fl%d" % t, 0, 24), O("fs"))]
-        return [[lambda: scan(O("SF"), O("rise"), O("VAL"))], [lambda: tt(O("fs"), O("SF", 15, 384, 16), O("L"), ADD)], ends]
-
-    def unpack(t, name, cn, sn, planes=range(4)):
+    def unpack(t, name, cn, sn, planes):
         for b in planes:
-            p = mx("eq", 128 * b, cn, 0, 320, sn)
-            copy(O("%s%d" % (name, t), 320 * b, 320 * b + 320), p, "s")
+            copy(O("%s%d" % (name, t), 320 * b, 320 * b + 320), mx("eq", 128 * b, cn + str(t), 0, 320, sn + str(t)), "s")
 
-    def spread(sem, out, in_, at, groups, qs):
-        dmas(sem, [(qs[i % len(qs)], T[out][16 * i:16 * i + 16, 0:20], T[in_][i:128:16, at(i):at(i) + 40], O(out, 0, 20, 1, (16 * i, 16 * i + 16))[1],
-                    O(in_, at(i), at(i) + 40)[1]) for i in groups])
+    def spread(out, win, where, add, other, between=lambda i: []):
+        for i, q in enumerate(other + "v"):
+            copy(O("PK", 192 * i, 192 * i + 192), by(O(win), O(where, 12 * i, 12 * i + 12)), q)
+        weave(between(0), [])
+        for i in (1, 0):
+            turn(O("PT", 192 * i, 192 * i + 192), O("PK", 192 * i, 192 * i + 192))
+        weave(between(1), [])
+        for s in (3, 2, 0, 1):
+            quarters("TM", 6, 6 * s, ("PT", 96 * s), s, other if s == 3 else "v", 16)
+        weave(between(2), [])
+        ts(O(out), by(O("TM", 0, 24), O("fin")), add, None, ADD)
 
-    def wide_labels(pieces):
-        for lo, hi in pieces:
-            copy(O("N", 16 * lo, 16 * hi), by(O("wd"), O("lu", lo, hi)), "s")
+    units = later(ts, O("lu"), O("L"), 1.0 / 320.0, 0.25, MUL, ADD)
+    groups = later(copy, O("OB"), by(O("tone"), O("lu")), "s")
 
-    quant("uq", "uqs", "ut", 0, 128)
-    copy(O("uws"), by(O("uqs"), O("upu")), "s")
-    copy(words(O("uw")), by(words(O("uq")), O("upu")))
-    quant("qc0", "qs0", "xt0", 0, 320)
-    tt(O("G", 16, 64), O("jf"), place("N", 0), ADD)
-    scan(O("SF"), O("rise"), O("N"))
-    scan(O("SC"), O("rise", 0, 48), O("G", 16, 64))
-    narrow(O("L"), O("SF", 15, 384, 16), "kap")
-    narrow(off(0), kept("SC"))
-    scores(0, 0, 320, "s")
-    for b in range(4):
-        q, s, x = O("eq", 128 * b, 128 * b + 128), O("eqs", 128 * b, 128 * b + 128), O("ec", 3 - b, 515 - b)
-        run("v", [q, s], [x], lambda: g.vector.quantize_mx(q[0], s[0], x[0]))
-    send_state(0)
-    copy(O("zero"), by(O("z16"), O("ln", 0, 12)), "s")
-    act(O("cap"), by(O("z16"), O("ln", 0, 12)), -2 * FAR, FAR)
-    chain = [c for k in range(7) for c in step(k)] + [lambda: values(7, 8, "v")]
-    early, sp = ahead(0)
-    more = {14: [lambda: values(4, 7, "s")], 17: [lambda: values(0, 4, "s")]}
-    weave(chain, [
-        [lambda: scan(O("patx"), O("rise"), O("pats"))], [lambda: narrow(O("rl"), O("patx", 15, 384, 16), "kap")],
-        [lambda: scan(O("selx"), O("rise", 0, 192), O("sel")), lambda: copy(O("gpat"), by(O("t320"), O("rl", 12, 24)), "s")],
-        [lambda: narrow(O("sl"), O("selx", 15, 192, 16), "kap"), lambda: unpack(0, "fo", "qc0", "qs0")],
-        [], early] + [sp[i - 6] + more.get(i, []) for i in range(6, 22)])
-    for calls in score_list(0):
-        calls[0]()
+    caps = [later(turn, O("OT"), O("OB")), later(copy, O("gl"), O("OT", 0, 384, 16)),
+            later(copy, O("MK"), by(O("cap8"), O("gl")), "s")]
+
+    def score_list(lo, hi):
+        return [later(turn, O("VT", 16 * lo, 16 * hi), O("VAL", 16 * lo, 16 * hi)),
+                later(ts, O("fl", lo, hi), O("VT", 16 * lo, 16 * hi, 16), 160.0, None, ADD)]
+
+    def scored(lo, hi):
+        w = (16 * lo, 16 * hi)
+        return [later(tt, O("GS", *w), by(O("ST"), O("fl", lo, hi)), O("MK", *w), MIN), later(turn, O("TS", *w), O("GS", *w)),
+                later(scan, O("SE", *w), O("r16", *w), O("TS", *w), MIN, MAX)]
+
+    iota(O("c0"), [[0, 4], [16, 3], [0, 16]], 336)
+    select(O("cpat"), O("c0"), [[0, 24], [1, 8]], EQ, -48.0, -7)
+    groups()
+    unit = [later(pack, O("eq", 128 * b, 128 * b + 128), O("eqs", 128 * b, 128 * b + 128), O("ec", 3 - b, 515 - b)) for b in range(4)]
+    sp = ahead(0)
+    (la, sa), (lb, sb), (lc, sc) = [(score_list(*p), scored(*p)) for p in ((12, 20), (0, 12), (20, 24))]
+    chain = [c for k in range(7) for c in step(k)] + [later(values, 7, 8, "v")] + lc + sc
+    more = {0: [later(copy, words(O("uw")), by(words(O("uq")), O("upu"))), later(copy, O("uws"), by(O("uqs"), O("upu")), "s")],
+            1: [later(scan, O("selx"), O("rise", 0, 192), O("sel"))],
+            2: [later(quant, "qc0", "qs0", "xt0", 0, 320), later(scores, 0, 0, 320, "s"), later(send_state, 0)],
+            3: caps[:1], 4: sp[1] + [later(narrow, O("sl"), O("selx", 15, 192, 16), "kap")] + lists[:2], 5: sp[0] + caps[1:] + lists[2:3],
+            6: lists[3:4], 7: lists[4:7], 8: [], 10: lists[7:9], 13: lists[9:10], 14: [later(values, 4, 7, "s")] + lists[10:11], 16: la[:1],
+            17: [later(values, 0, 4, "s")] + la[1:], 18: sa[:1], 19: lb[:1], 20: sa[1:2] + lb[1:], 21: sb[:1], 22: sa[2:], 23: sb[1:2], 24: sb[2:],
+            25: unit[:1] + lists[11:13], 26: unit[1:2] + lists[13:14]}
+    weave(chain, [(sp[i - 4] if 6 <= i < 22 else []) + more.get(i, []) for i in range(27)])
+    iota(O("q24"), [[1, 4], [0, 6]], 0)
+    iota(O("p24"), [[0, 4], [16, 3], [192, 2]], 0)
 
     for t in range(3):
         f = first[t]
         a, b = sides(t)
         n = a[1] - a[0]
-        one, two = ((14, 23), (4, 13)) if t == 1 else ((0, 12), (12, 24))
-        tt(O("E", 0, 16 * n), by(O("ST"), O("fl%d" % t, *one)), O("cap", 0, 16 * n), MIN)
-        tt(O("CC", 0, 16 * n), by(O("ST"), O("fl%d" % t, *two)), O("E", 0, 16 * n), LT)
-        if t:
-            unpack(t, "fo", "qc%d" % t, "qs%d" % t, range(FO))
-        scan(O("FL", 0, 16 * n), O("zero", 0, 16 * n), O("CC", 0, 16 * n), MUL, ADD)
+        sp = ahead(t + 1) if t < 2 else [[]] * 18
+        tt(O("FL", 0, n), O("SE", 16 * b[0] + 15, 16 * b[1], 16), O("SE", 16 * a[0] + 15, 16 * a[1], 16), LT)
+        if t == 0:
+            weave(unit[2:3] + lists[14:15], [])
         copy(O("d0"), by(O("FL"), O("sl", 0, 5)))
         tt(O("d1"), by(O("FL"), O("sl", 6, 11)), O("W"), MUL)
-        tt(O("M", 0, n), O("FL", 15, 16 * n, 16), O("D", 0, n), MUL)
-        entry = [lambda: scan(O("SS"), O("d0"), O("d1"), MUL, ADD), lambda: narrow(O("off", col(f), col(f) + 9), O("SS", 4, 45, 5))]
-        chain = entry + step(f + 4, label(f + 5)) + [c for k in range(f + 5, 7) for c in step(k)] + [lambda: values(7, 8, "v")]
-        pieces = [[(8, 12), (20, 24), (12, 18), (6, 8)], [(20, 24), (0, 6), (14, 18)], [(8, 12), (20, 24)]][t]
-        if t < 2:
-            early, sp = ahead(t + 1)
-        else:
-            early = [lambda: copy(O("OB"), by(O("tone"), O("lu")), "s"),
-                     lambda: spread("do1", "owb", "OB", lambda i: 48 * slot(i), range(8), "y")]
-            sp = [[]] * 16
-        position = [[lambda: tt(O("PN"), by(O("L"), O("rl", 0, 12)), O("gpat"), NE)],
-                    [lambda: scan(O("PC"), O("PN"), O("cpat"), MUL, ADD)],
-                    [lambda: ts(O("pos"), O("PC", 7, 192, 8), O("lanef"), None, ADD)]]
-        odd, even = [lambda: values(4, 7, "s")], [lambda: values(0, 4, "s")]
-        beside = [[lambda: tt(O("L", *a), O("L", *a), O("M", 0, n), ADD), lambda: tt(O("L", *b), O("L", *b), O("M", 0, n), SUB)],
-                  [lambda: ts(O("lu"), O("L"), 1.0 / 320.0, 0.25, MUL, ADD), lambda: wide_labels(pieces)],
-                  [lambda: narrow(O("off", col(f + 1), col(f + 1) + 6), O("SS", 49, 75, 5))]]
-        if t == 1:
-            beside += [position[0], [], odd + even + position[1], position[2], early, sp[0], sp[1]]
-            done = 2
-        else:
-            beside += [position[0], early, odd + sp[0], position[1], sp[1], even + position[2], sp[2], sp[3], sp[4], sp[5]]
-            done = 6
-        weave(chain, beside)
-        for i in range(2):
-            ts(O("ml%d" % t, 192 * i, 192 * i + 192), by(O("VAL"), O("pos", 12 * i, 12 * i + 12)), 160.0, None, ADD)
-            spread("own%d%d" % (t, i), "al%d" % t, "ml%d" % t, lambda i: 48 * i, range(4 * i, 4 * i + 4), "ys")
-        k = send(t, O("pl%d" % t), O("al%d" % t), "rl%d" % t)
-        arrives("rl%d" % t, k, [O("pl%d" % t)])
-        unpack(t, "fp", "lc%d" % t, "lp%d" % t)
-        copy(O("BG"), by(O("P", 0, 320), O("al%d" % t)), "s")
-        if t:
-            unpack(t, "fo", "qc%d" % t, "qs%d" % t, range(FO, 4))
-        extra = {}
-        if t < 2:
-            extra.update(zip((done, done + 1, done + 2), score_list(t + 1)))
+        tt(O("M", 0, n), O("FL", 0, n), O("D", 0, n), MUL)
         if t == 0:
-            extra[10] = [lambda: quant("vq", "vqs", "vt", 0, 128)]
-        if t == 2:
-            extra[11] = [lambda: copy(O("ow"), O("owb")), lambda: ts(O("olf"), by(O("i320"), O("ow")), 160.0, None, ADD),
-                         lambda: dmas("dout", [("y", T.ol[:], T.olf[0:128:16, 0:320], [], O("olf")[1])])]
-        list_b = [lambda: scan(O("BS"), O("rise", 0, 320), O("BG")), lambda: narrow(O("bl%d" % t), O("BS", 15, 320, 16))]
-        cut = CUT[t]
-        if t != 1:
-            extra[cut - 2], extra[cut - 1], list_b = list_b[:1], list_b[1:], []
-        for i in range(done, cut):
-            for call in sp[i] + extra.get(i, []):
-                call()
+            weave(unit[3:] + lists[15:], [])
+
+        def labels(pieces):
+            for lo, hi in pieces:
+                copy(O("N", 16 * lo, 16 * hi), by(O("wd"), O("lu", lo, hi)), "s")
+
+        now, then = [([(8, 12), (20, 24)], [(12, 18), (6, 8)]), ([(20, 24)], [(0, 6), (14, 18)]), ([(8, 12), (20, 24)], [])][t]
+        chain = ([later(scan, O("SS"), O("d0"), O("d1"), MUL, ADD), later(narrow, O("off", col(f), col(f) + 9), O("SS", 4, 45, 5))]
+                 + step(f + 4, False) + [c for k in range(f + 5, 7) for c in step(k)] + [later(values, 7, 8, "v")])
+        where = [later(tt, O("PN"), by(O("L"), O("rl", 0, 12)), O("gpat"), NE), later(scan, O("PC"), O("PN"), O("cpat"), MUL, ADD),
+                 later(ts, O("pos"), O("PC", 7, 192, 8), O("lanef"), None, ADD)]
+        odd, even, rest = later(values, 4, 7, "s"), later(values, 0, 4, "s"), later(labels, then)
+        fp = lambda *planes: later(unpack, t, "fp", "lc", "lp", planes)
+        beside = [[fp(0, 1), later(tt, O("L", *a), O("L", *a), O("M", 0, n), ADD), later(tt, O("L", *b), O("L", *b), O("M", 0, n), SUB)],
+                  [units, later(labels, now), later(narrow, O("e1"), label(f + 5))],
+                  [later(narrow, O("off", col(f + 1), col(f + 1) + 6), O("SS", 49, 75, 5))], []]
+        spare = list(sp) if t < 2 else [[c] for c in by_position]
+        take = lambda n: [c for _ in range(min(n, len(spare))) for c in spare.pop(0)]
+        if t == 1:
+            beside[2] += [odd, rest]
+            beside += [[even]]
+        else:
+            beside[2] += [rest, groups]
+            beside += [[odd], [], [], [even]]
+        beside += [[] for _ in range(len(chain) - len(beside))]
+        for i, call in zip(WH[t], where):
+            beside[i] = beside[i] + [call]
+        weave(chain, [beside[i] + take(TAKE[t][0][i]) for i in range(len(chain))])
+        spread("al%d" % t, "VAL", "pos", 160.0, "s", lambda i: take(TAKE[t][1][i]))
+        send(t, [(O("pl%d" % t), O("al%d" % t, 0, 20))], "rl%d" % t)
+        copy(O("BG"), by(O("P", 0, 320), O("al%d" % t, 0, 20)), "s")
+        unpack(t, "fp", "lc", "lp", range(2, 4))
+        if t == 0:
+            unpack(0, "fo", "qc", "qs", range(2))
+        if t == 1:
+            groups()
+        list_b = [later(scan, O("BS"), O("rise", 0, 320), O("BG")), later(narrow, O("bl%d" % t), O("BS", 15, 320, 16))]
+        if t < 2:
+            la = score_list(*((2, 22) if t == 0 else (0, 24)))
+            fillers = la + list_b + (caps[:2] if t == 0 else [])
+            weave([], [take(1) + fillers[i:i + 1] for i in range(TAKE[t][2])])
+        else:
+            spread("ow", "OB", "pol", 0.0, "v", lambda i: list_b[i - 1:i])
         for i, (lo, hi) in enumerate(ZCH):
             o = O("pl%d" % t, lo // 16, hi // 16)
             for b in range(4):
                 copy(O("zt%d" % t, 4 * lo + b, 4 * hi, 4), by(O("fp%d" % t, 320 * b, 320 * b + 320), o), ZQ[i][b])
+            weave(take(1), [])
             quant("zc%d" % t, "zs%d" % t, "zt%d" % t, lo, hi)
-        for call in list_b:
-            call()
-        rest = [c for cs in sp[cut:] for c in cs]
+        weave(take(TAKE[t][3]) + (caps[:1] if t == 1 else []) + take(1) + (caps[1:2] if t == 1 else []), [])
         for i, (lo, hi) in enumerate(ZCH):
             for b in range(4):
                 p = mx("wq", 128 * b, "zc%d" % t, lo, hi, "zs%d" % t)
@@ -523,23 +535,43 @@ def rank_program(g, core, T, topo):
                 if RQ[i][b] == "v":
                     ts(o, p, 0.03125, None, MUL)
                 else:
-                    run("s", [o], [p], lambda o=o, p=p: g.scalar.activation(o[0], p[0], COPY, scale=0.03125))
-        for i, (lo, hi) in enumerate(CH):
-            o = O("bl%d" % t, lo // 16, hi // 16)
-            for b in range(4):
-                tt(O("xt%d" % (t + 1), 4 * lo + b, 4 * hi, 4), by(O("rb%d" % b), o), O("fo%d" % t, 320 * b + lo, 320 * b + hi), ADD)
-            quant("qc%d" % (t + 1), "qs%d" % (t + 1), "xt%d" % (t + 1), lo, hi)
-            if t < 2:
-                for call in rest[:1] if i == 0 else rest[1:]:
-                    call()
-                scores(t + 1, lo, hi, SQ[i])
-            else:
-                o, y = O("qc3", lo, hi), O("yb", lo, hi)
-                copy(y, mx("vq", 0, "qc3", lo, hi, "qs3"), "s")
-                dmas("dout", [("y", T.oc[:, 4 * lo:4 * hi], codes(o)[0], [], o[1]), ("s", T.y[:, lo:hi], y[0], [], y[1])])
+                    run("s", [o], [p], lambda: g.scalar.activation(o[0], p[0], COPY, scale=0.03125))
+        x = lambda lo, hi, b: O("xt%d" % (t + 1), 4 * lo + b, 4 * hi, 4)
+        o = O("bl%d" % t)
+        own = {b: mx("eq", 128 * b, "qc%d" % t, 0, 320, "qs%d" % t) for b in (2, 3)}
+        for b in range(2):
+            tt(x(0, 320, b), by(O("rb%d" % b), o), O("fo%d" % t, 320 * b, 320 * b + 320), ADD)
+            copy(O("tb%d" % (b + 2)), by(O("rb%d" % (b + 2)), o), "s")
         if t < 2:
-            send_state(t + 1)
-    dmas("dout", [("y", T.osc[4 * k:4 * k + 4, 0:320], T.qs3[32 * k:32 * k + 4, 0:320], [], O("qs3")[1]) for k in range(4)])
+            caps[2]()
+        else:
+            act(O("olf"), by(O("i320"), O("ow", 0, 20)), 1.0, 160.0)
+            dmas("dout", [("y", T.ol[:], T.olf[0:128:16, 0:320], [], O("olf")[1])])
+        tt(x(0, 320, 2), O("tb2"), own[2], ADD)
+        weave(take(TAKE[t][4]), [])
+        for lo, hi in CH:
+            tt(x(lo, hi, 3), O("tb3", lo, hi), (T[own[3][1][0][0]][:, lo:hi], own[3][1]), ADD)
+        if t == 2:
+            break
+        for lo, hi in CH:
+            quant("qc%d" % (t + 1), "qs%d" % (t + 1), "xt%d" % (t + 1), lo, hi)
+        if t == 0:
+            quant("vq", "vqs", "vt", 0, 128)
+        weave(take(TAKE[t][5]), [])
+        for i, (lo, hi) in enumerate(CH):
+            scores(t + 1, lo, hi, "sv"[i])
+        send_state(t + 1)
+        unpack(t + 1, "fo", "qc", "qs", range(2))
+        sa, sb = [scored(*p) for p in (((2, 12), (12, 22)) if t == 0 else ((0, 12), (12, 24)))]
+        weave(sa, [sb[:1], sb[1:2], sb[2:] + take(9)])
+    scales = lambda q, k: (q, T.osc[4 * k:4 * k + 4, 0:320], T.qs3[32 * k:32 * k + 4, 0:320], [], O("qs3")[1])
+    for lo, hi in CH:
+        quant("qc3", "qs3", "xt3", lo, hi)
+    for i, (lo, hi) in enumerate(CH):
+        o, y = O("qc3", lo, hi), O("yb", lo, hi)
+        dmas("dout", [("y", T.oc[:, 4 * lo:4 * hi], codes(o)[0], [], o[1])] + [scales("y", k) for k in range(3 * i)])
+        copy(y, mx("vq", 0, "qc3", lo, hi, "qs3"), "sv"[i])
+        dmas("dout", [scales("s", 3)] * (1 - i) + [("s", T.y[:, lo:hi], y[0], [], y[1])])
     for s in SEMAPHORES:
         if total[s]:
             g.wait_ge(T.sem[s], total[s])

@@ -9,11 +9,13 @@ BIG = 1048576.0
 RISE = 8192.0
 FAR = 1e29
 STEP = [1, 2, 4]
-RQ = ["ssss", "vvss"]
+RQ = ["vsss", "vvss"]
 ZQ = ["vvss", "vvss"]
-PQ = "s"
-WH = [[4, 7, 9], [2, 4, 6], [4, 7, 9]]
-TAKE = [[[0, 0, 0, 2, 0, 1, 1, 0, 1, 1, 0, 1], [1, 0, 1], 6, 0, 0, 2], [[0, 0, 0, 2, 0, 1, 0, 1, 1], [1, 0, 1], 6, 0, 0, 2], [[0, 0, 0, 1, 0, 1, 1, 0, 1, 0, 1, 0], [0, 0, 0], 0, 0, 0, 0]]
+TQ = "s"
+AT = [6, 7, 8, 9, 10, 11, 13, 14, 15, 16, 17, 18, 19, 21, 22, 23]
+RO = [[2, 3, 0, 1], [0, 2, 1, 3]]
+WH = [[2, 4, 7, 9], [0, 2, 3, 4], [1, 2, 4, 6]]
+TAKE = [[[0, 0, 0, 2, 0, 1, 1, 0, 1, 0, 1, 1], [1, 1, 1], 5, 1, 0, 1], [[0, 0, 0, 2, 0, 1], [1, 1, 1], 6, 1, 1, 2], [[0, 0, 0, 1, 0, 1, 1, 0, 1, 1, 0, 1], [0, 0, 0], 0, 0, 0, 0]]
 ZCH = [(0, 192), (192, 320)]
 CH = [(0, 192), (192, 320)]
 
@@ -41,14 +43,15 @@ _share("fv", "float32", ("lanef", 1), ("xf", 1), ("hf", 1), ("ef", 1), ("quadf",
        ("kap2", 1), ("kap", 1), ("bb", 24), ("cb", 24), ("k20", 24), ("j16", 3), ("oa", 32), ("ob", 32), ("b12", 12), ("d12", 12), ("c2", 2),
        ("f3", 2), ("f4", 2), ("f5", 2), ("f6", 2), ("q24", 24), ("p24", 24),
        ("i16", 16), ("z16", 16), ("t320", 8), ("tone", 8), ("wd", 8), ("c8", 8), ("cap8", 8))
-_share("ov", "float32", ("W", 80), ("a2", 8), ("FL", 16), ("D", 12), ("L", 24), ("M", 12), ("d0", 80), ("d1", 80), ("SS", 80),
+_share("ov", "float32", ("W", 112), ("a2", 8), ("FL", 24), ("D", 12), ("L", 24), ("M", 12), ("d0", 112), ("d1", 112), ("SS", 112),
+       ("LK", 6), ("e3", 3), ("e6", 6),
        ("a1", 6), ("e1", 3), ("k1", 3), ("dB", 3), ("xB", 3))
-_share("uv", "uint16", ("ogl", 2), ("upu", 8), ("gl", 24), ("fl", 24), ("fin", 2), ("ln", 24), ("rl", 24), ("sl", 12), ("lu", 24), ("ow", 32),
+_share("uv", "uint16", ("ogl", 2), ("upu", 8), ("gl", 24), ("fl", 24), ("fin", 2), ("ln", 24), ("rl", 24), ("sl", 16), ("of3", 24), ("lu", 24), ("ow", 32),
        ("pol", 24))
-_share("wv", "float32", ("SC", 48), ("G2", 96), ("T1", 96), ("T2", 96), ("T3", 96), ("T4", 96))
+_share("wv", "float32", ("SC", 48), ("G2", 96), ("T1", 96), ("T2", 96), ("T4", 96), ("T3", 96))
 _d("pgi", 40, "int32")
 _d("OG", 160, "int32")
-for _n, _c in (("rise", 384), ("gpat", 192), ("c0", 192), ("cpat", 192), ("N", 384), ("G", 64), ("sel", 192), ("selx", 192), ("MK", 384), ("GS", 384), ("TS", 384), ("SE", 384),
+for _n, _c in (("rise", 384), ("gpat", 192), ("c0", 192), ("cpat", 192), ("N", 384), ("G", 64), ("sel", 256), ("selx", 256), ("G5", 384), ("T5", 384), ("MK", 384), ("GS", 384), ("TS", 384), ("SE", 384),
                ("PN", 192), ("PC", 192), ("ST", 320), ("BG", 320), ("BS", 320), ("tb2", 320), ("tb3", 320),
                ("rb0", 320), ("rb1", 320), ("rb2", 320), ("rb3", 320), ("olf", 320), ("yb", 320)):
     _d(_n, _c, "float32")
@@ -125,7 +128,7 @@ def rank_program(g, core, T, topo):
             evs += [e for w, e in wrote.get(r[0], []) if meet(r, w)]
         for r in writes:
             evs += [e for w, e in wrote.get(r[0], []) if meet(r, w)]
-            evs += [e for w, e in read.get(r[0], []) if meet(r, w) and (dma or e[3] != q)]
+            evs += [e for w, e in read.get(r[0], []) if meet(r, w) and (dma or e[3] != q or SCRATCH[r[0]][2] == "uint16")]
         want = {}
         for sem, val, snap, who in evs:
             if clock[q].get(sem, 0) < val and want.get(sem, (0,))[0] < val:
@@ -247,7 +250,6 @@ def rank_program(g, core, T, topo):
                 load("y", "vt", T.v[:], 0, 512)])
 
     fill(O("ones"), 1.0)
-    fill(O("sel"), 13.0)
     iota(O("pint"), [[1, 1]], 0, 1)
     iota(O("i16"), [[1, 16]], 0)
     iota(O("kk"), [[-1, 2], [-2, 4], [0, 3]], 8)
@@ -258,14 +260,16 @@ def rank_program(g, core, T, topo):
 
     for name, shift, mask in (("lane", 0, 15), ("x", 0, 7), ("h", 4, 7), ("e", 4, 1), ("quad", 5, 3), ("up", 3, 1)):
         ts(O(name + "i"), O("pint"), shift, mask, SHR, AND)
+    fill(O("far"), FAR)
     copy(O("fv", 0, 48, 8), O("iv", 8, 56, 8))
-    fill(O("sel", 0, 80, 5), 12.0)
-    fill(O("oa"), 0.0)
+    fill(O("sel"), 13.0)
     ts(O("z16"), O("i16"), O("lanef"), None, NE)
     ts(O("ln"), O("ones", 0, 24), O("lanef"), None, MUL)
     ts(O("c5"), O("quadf"), 5.0, O("ef"), MUL, ADD)
     ts(O("k1i"), O("kk"), O("hf"), None, ADD)
     act(O("rise"), by(O("z16"), O("ln")), BIG + RISE, -BIG)
+    fill(O("sel", 0, 110, 5), 12.0)
+    fill(O("oa"), 0.0)
     ts(O("kap"), O("lanef"), -RISE, 15 * RISE, MUL, ADD)
     ts(O("kap2"), O("lanef"), -RISE, 15 * RISE - 160.0, MUL, ADD)
     ts(O("cb"), O("bb"), O("c5"), 19.0, ADD, MIN)
@@ -274,13 +278,16 @@ def rank_program(g, core, T, topo):
     ts(O("j16"), O("cb", 0, 3), 16.0, O("lanef"), MUL, ADD)
     ts(O("k20"), O("k2i"), 20.0, None, MUL)
     fill(O("off"), 0)
+    ts(O("c8"), O("i16", 0, 8), O("xf"), 2 * FAR, EQ, MUL)
     ts(O("upu"), O("ones", 0, 8), O("xf"), 16.0, MUL, MUL)
     tt(O("oa", 0, 24), O("k20"), O("cb"), ADD)
+    fill(O("ov", 0, 133), 0.0)
 
-    iota(O("sel", 1, 75, 5), [[0, 5], [1, 3]], 0)
-    iota(O("sel", 2, 75, 5), [[0, 5], [1, 3]], 3)
-    iota(O("sel", 99, 171, 5), [[0, 5], [1, 3]], 0)
-    iota(O("sel", 100, 141, 5), [[1, 9]], 0)
+    iota(O("sel", 1, 105, 5), [[0, 7], [1, 3]], 0)
+    iota(O("sel", 2, 105, 5), [[0, 7], [1, 3]], 3)
+    iota(O("sel", 79, 105, 5), [[-10, 2], [1, 3]], 16)
+    iota(O("sel", 131, 233, 5), [[0, 7], [1, 3]], 0)
+    iota(O("sel", 132, 173, 5), [[1, 9]], 0)
     iota(O("b12"), [[0, 4], [1, 3]], 0)
     iota(O("d12"), [[2, 4], [0, 3]], 0)
     iota(O("c2"), [[16, 2]], -2)
@@ -299,33 +306,29 @@ def rank_program(g, core, T, topo):
     table(0, "s")
     table(1, "s")
     scan(O("ob"), O("rise", 0, 32), O("oa"))
-    table(2, "v")
     quarters("OG", 40, 40, ("OG", 0), 1, "v")
+    quarters("P", 640, 1280, ("P", 0), 2, "s")
+    table(2, "v")
     narrow(O("ogl"), O("ob", 15, 32, 16), "kap")
-    table(3, "v")
     quarters("OG", 80, 80, ("OG", 0), 2, "v")
-    ts(O("t8a"), O("t8"), O("hf"), None, ADD)
-    copy(O("P", 1280, 2560, 1, (0, 64)), O("P", 0, 1280, 1, (64, 128)), PQ)
+    table(3, "v")
     copy(O("o32"), by(O("OG"), O("ogl")))
-    ts(O("t8b"), O("t8a"), 7, None, AND)
-    fill(O("ov", 0, 101), 0.0)
+    ts(O("t8a"), O("t8"), O("hf"), None, ADD)
+    copy(O("P", 1920, 2560, 1, (0, 64)), O("P", 640, 1280, 1, (64, 128)))
     ts(O("k1i"), O("o32", 0, 24), -1.0, O("h8"), MUL, ADD)
-    copy(O("tone"), O("t8b"))
-    fill(O("FL", 13, 16), 1.0)
-    ts(O("c8"), O("i16", 0, 8), O("xf"), 2 * FAR, EQ, MUL)
+    copy(O("P", 1920, 2560, 1, (64, 128)), O("P", 640, 1280, 1, (0, 64)))
     ts(O("k2i"), O("k1i"), 7, None, AND)
-    fill(O("far"), FAR)
-    copy(O("lu"), O("k2i"))
-    ts(O("L"), O("k2i"), 320.0, None, MUL)
-    copy(O("N", 192, 384), by(O("wd"), O("lu", 12, 24)), "s")
-    copy(O("N", 0, 192), by(O("wd"), O("lu", 0, 12)), "s")
+    ts(O("t8b"), O("t8a"), 7, None, AND)
+    quant("uq", "uqs", "ut", 0, 128)
     for c in range(3):
         ts(O("off", c, c + 1), O("k2i", c, c + 1), 320.0, O("j16", c, c + 1), MUL, ADD)
-    copy(O("P", 1280, 2560, 1, (64, 128)), O("P", 0, 1280, 1, (0, 64)))
-    ts(O("cap8"), O("c8"), FAR, None, SUB)
-    quant("uq", "uqs", "ut", 0, 128)
-    select(O("ec"), O("ones"), [[-1, 516]], EQ, 0.0, 3, 4)
+    copy(O("lu"), O("k2i"))
+    ts(O("e1"), O("k2i", 12, 15), 320.0, O("kap2"), MUL, SUB)
+    ts(O("L"), O("k2i"), 320.0, None, MUL)
+    copy(O("N"), by(O("wd"), O("lu")), "s")
+    copy(O("tone"), O("t8b"))
     select(O("r16"), O("far"), [[0, 24], [1, 16]], NE, -FAR)
+    select(O("ec"), O("ones"), [[-1, 516]], EQ, 0.0, 3, 4)
 
     lists = [later(ts, O("x3"), O("xf"), 3.0, None, MUL), later(ts, O("t8c"), O("t8"), O("ef"), None, ADD),
              later(ts, O("rl", 0, 12), O("b12"), O("x3"), None, ADD), later(ts, O("t8d"), O("t8c"), 7, None, AND),
@@ -413,6 +416,18 @@ def rank_program(g, core, T, topo):
                 [later(tt, w(2, 3), kept("T4"), O("k1"), ADD), later(tt, O("dB"), kept("T4", 1, 2), kept("T2", 1, 2), SUB)],
                 [later(tt, w(2, 0), O("dB"), w(2, 3), SUB)]]
 
+    def beyond(t):
+        f = first[t]
+        w = lambda r: O("W", 75 + r, 105, 5)
+        end = lambda i: kept("T5", 2 * i, 2 * i + 2)
+        early = [later(narrow, O("LK", 0, 3), label(f + 5)), later(narrow, O("LK", 3, 6), label(f + 4)), later(copy, O("of3", 18, 21), off(f + 4)),
+                 later(tt, O("e3"), O("W", 32, 45, 5), O("D", 6, 9), ADD), later(narrow, O("of3", 21, 24), O("e3"))]
+        starts = [later(ts, O("of3", 3 * z + c, 18, 6), O("T2", 63 + 16 * c, 192, 48), O("LK", 3 - 3 * z + c, 4 - 3 * z + c), None, ADD)
+                  for z in range(2) for c in range(3)]
+        return early, [starts + [later(copy, O("G5"), by(O("P"), O("of3")), "s")], [later(scan, O("T5"), O("rise"), O("G5"))],
+                       [later(tt, w(3), end(1), end(3), SUB), later(tt, O("e6"), end(2), end(0), SUB), later(tt, w(1), end(0), end(3), SUB),
+                        later(tt, w(2), end(3), O("LK"), ADD)], [later(tt, w(0), O("e6"), w(3), SUB)]]
+
     def values(lo, hi, q):
         c = 22 if lo == 7 else 3 * lo
         copy(O("VAL", 48 * lo, 48 * hi), by(O("P"), O("off", c, c + 3 * (hi - lo))), q)
@@ -431,7 +446,7 @@ def rank_program(g, core, T, topo):
         for s in (3, 2, 0, 1):
             quarters("TM", 6, 6 * s, ("PT", 96 * s), s, other if s == 3 else "v", 16)
         weave(between(2), [])
-        ts(O(out), by(O("TM", 0, 24), O("fin")), add, None, ADD)
+        return later(ts, O(out), by(O("TM", 0, 24), O("fin")), add, None, ADD)
 
     units = later(ts, O("lu"), O("L"), 1.0 / 320.0, 0.25, MUL, ADD)
     groups = later(copy, O("OB"), by(O("tone"), O("lu")), "s")
@@ -452,17 +467,20 @@ def rank_program(g, core, T, topo):
     select(O("cpat"), O("c0"), [[0, 24], [1, 8]], EQ, -48.0, -7)
     groups()
     unit = [later(pack, O("eq", 128 * b, 128 * b + 128), O("eqs", 128 * b, 128 * b + 128), O("ec", 3 - b, 515 - b)) for b in range(4)]
-    sp = ahead(0)
+    sp = ahead(0, TQ)
     (la, sa), (lb, sb), (lc, sc) = [(score_list(*p), scored(*p)) for p in ((12, 20), (0, 12), (20, 24))]
-    chain = [c for k in range(7) for c in step(k)] + [later(values, 7, 8, "v")] + lc + sc
+    chain = [c for k in range(7) for c in step(k, k > 0)] + [later(values, 7, 8, "v")] + lc + sc
     more = {0: [later(copy, words(O("uw")), by(words(O("uq")), O("upu"))), later(copy, O("uws"), by(O("uqs"), O("upu")), "s")],
-            1: [later(scan, O("selx"), O("rise", 0, 192), O("sel"))],
-            2: [later(quant, "qc0", "qs0", "xt0", 0, 320), later(scores, 0, 0, 320, "s"), later(send_state, 0)],
-            3: caps[:1], 4: sp[1] + [later(narrow, O("sl"), O("selx", 15, 192, 16), "kap")] + lists[:2], 5: sp[0] + caps[1:] + lists[2:3],
-            6: lists[3:4], 7: lists[4:7], 8: [], 10: lists[7:9], 13: lists[9:10], 14: [later(values, 4, 7, "s")] + lists[10:11], 16: la[:1],
+            1: [later(scan, O("selx"), O("rise", 0, 256), O("sel"))],
+            2: [later(quant, "qc0", "qs0", "xt0", 0, 192), later(ts, O("cap8"), O("c8"), FAR, None, SUB)],
+            3: [later(quant, "qc0", "qs0", "xt0", 192, 320), later(scores, 0, 0, 320, "s"), later(send_state, 0)],
+            4: sp[1] + [later(narrow, O("sl"), O("selx", 15, 256, 16), "kap")] + lists[:2], 5: caps[:1] + sp[0],
+            6: lists[2:4], 7: caps[1:] + lists[4:6], 8: [], 9: lists[6:7], 10: lists[7:9], 12: [later(fill, O("FL", 13, 24), 1.0)], 13: lists[9:10], 14: [later(values, 4, 7, "s")] + lists[10:11], 16: la[:1],
             17: [later(values, 0, 4, "s")] + la[1:], 18: sa[:1], 19: lb[:1], 20: sa[1:2] + lb[1:], 21: sb[:1], 22: sa[2:], 23: sb[1:2], 24: sb[2:],
             25: unit[:1] + lists[11:13], 26: unit[1:2] + lists[13:14]}
-    weave(chain, [(sp[i - 4] if 6 <= i < 22 else []) + more.get(i, []) for i in range(27)])
+    for i, at in enumerate(AT):
+        more[at] = sp[i + 2] + more.get(at, [])
+    weave(chain, [more.get(i, []) for i in range(27)])
     iota(O("q24"), [[1, 4], [0, 6]], 0)
     iota(O("p24"), [[0, 4], [16, 3], [192, 2]], 0)
 
@@ -474,31 +492,42 @@ def rank_program(g, core, T, topo):
         tt(O("FL", 0, n), O("SE", 16 * b[0] + 15, 16 * b[1], 16), O("SE", 16 * a[0] + 15, 16 * a[1], 16), LT)
         if t == 0:
             weave(unit[2:3] + lists[14:15], [])
-        copy(O("d0"), by(O("FL"), O("sl", 0, 5)))
-        tt(O("d1"), by(O("FL"), O("sl", 6, 11)), O("W"), MUL)
+        rows = 7 if t == 1 else 5
+        if t == 1:
+            tt(O("FL", 16, 19), O("SE", 16 * b[0] + 111, 16 * b[0] + 144, 16), O("SE", 16 * a[0] + 111, 16 * a[0] + 144, 16), GE)
         tt(O("M", 0, n), O("FL", 0, n), O("D", 0, n), MUL)
-        if t == 0:
-            weave(unit[3:] + lists[15:], [])
+        tt(O("d1", 0, 16 * rows), by(O("FL"), O("sl", 8, 8 + rows)), O("W", 0, 16 * rows), MUL)
+        copy(O("d0", 0, 16 * rows), by(O("FL"), O("sl", 0, rows)))
+        tt(O("L", *a), O("L", *a), O("M", 0, n), ADD)
+        tt(O("L", *b), O("L", *b), O("M", 0, n), SUB)
 
         def labels(pieces):
             for lo, hi in pieces:
                 copy(O("N", 16 * lo, 16 * hi), by(O("wd"), O("lu", lo, hi)), "s")
 
-        now, then = [([(8, 12), (20, 24)], [(12, 18), (6, 8)]), ([(20, 24)], [(0, 6), (14, 18)]), ([(8, 12), (20, 24)], [])][t]
-        chain = ([later(scan, O("SS"), O("d0"), O("d1"), MUL, ADD), later(narrow, O("off", col(f), col(f) + 9), O("SS", 4, 45, 5))]
-                 + step(f + 4, False) + [c for k in range(f + 5, 7) for c in step(k)] + [later(values, 7, 8, "v")])
-        where = [later(tt, O("PN"), by(O("L"), O("rl", 0, 12)), O("gpat"), NE), later(scan, O("PC"), O("PN"), O("cpat"), MUL, ADD),
-                 later(ts, O("pos"), O("PC", 7, 192, 8), O("lanef"), None, ADD)]
+        now, then = [([(8, 12), (20, 24)], [(12, 18), (6, 8)]), ([], [(0, 6), (14, 18)]), ([(8, 12), (20, 24)], [])][t]
+        five = later(narrow, O("off", col(f), col(f) + 9), O("SS", 4, 45, 5))
+        sixth = lambda: [ts(O("off", col(f + 5) + c, col(f + 5) + c + 1), O("SS", 79 + 5 * c, 80 + 5 * c), O("SS", 94 + 5 * c, 95 + 5 * c), None, ADD)
+                         for c in range(3)]
+        chain = ([later(scan, O("SS", 0, 16 * rows), O("d0", 0, 16 * rows), O("d1", 0, 16 * rows), MUL, ADD)]
+                 + ([sixth] if t == 1 else [five] + step(4, False) + step(5)) + step(6) + [later(values, 7, 8, "v")])
+        where = [later(tt, O("PN", 96 * i, 96 * i + 96), by(O("L"), O("rl", 6 * i, 6 * i + 6)), O("gpat", 96 * i, 96 * i + 96), NE) for i in range(2)]
+        where += [later(scan, O("PC"), O("PN"), O("cpat"), MUL, ADD), later(ts, O("pos"), O("PC", 7, 192, 8), O("lanef"), None, ADD)]
         odd, even, rest = later(values, 4, 7, "s"), later(values, 0, 4, "s"), later(labels, then)
         fp = lambda *planes: later(unpack, t, "fp", "lc", "lp", planes)
-        beside = [[fp(0, 1), later(tt, O("L", *a), O("L", *a), O("M", 0, n), ADD), later(tt, O("L", *b), O("L", *b), O("M", 0, n), SUB)],
-                  [units, later(labels, now), later(narrow, O("e1"), label(f + 5))],
+        beside = [(unit[3:] if t == 0 else []) + [units, later(labels, now), fp(0, 1)] * (t != 1),
+                  [five, units, fp(0, 1)] if t == 1 else [later(narrow, O("e1"), label(5))] + lists[15:] * (t == 0),
                   [later(narrow, O("off", col(f + 1), col(f + 1) + 6), O("SS", 49, 75, 5))], []]
-        spare = list(sp) if t < 2 else [[c] for c in by_position]
+        late = [[lambda: None], [], [], []]
+        if t == 0:
+            early, late = beyond(1)
+            spare = sp[:9] + [sp[9 + i] + early[i:i + 1] for i in range(5)] + sp[14:16] + [late[0][:-1], sp[16], sp[17]]
+        else:
+            spare = list(sp) if t == 1 else [[c] for c in by_position] + [[later(quant, "vq", "vqs", "vt", 0, 128)]]
         take = lambda n: [c for _ in range(min(n, len(spare))) for c in spare.pop(0)]
         if t == 1:
-            beside[2] += [odd, rest]
-            beside += [[even]]
+            beside[1] += [odd, rest]
+            beside[2:] = [[], beside[2] + [even]]
         else:
             beside[2] += [rest, groups]
             beside += [[odd], [], [], [even]]
@@ -506,7 +535,7 @@ def rank_program(g, core, T, topo):
         for i, call in zip(WH[t], where):
             beside[i] = beside[i] + [call]
         weave(chain, [beside[i] + take(TAKE[t][0][i]) for i in range(len(chain))])
-        spread("al%d" % t, "VAL", "pos", 160.0, "s", lambda i: take(TAKE[t][1][i]))
+        spread("al%d" % t, "VAL", "pos", 160.0, "s", lambda i: take(TAKE[t][1][i]))()
         send(t, [(O("pl%d" % t), O("al%d" % t, 0, 20))], "rl%d" % t)
         copy(O("BG"), by(O("P", 0, 320), O("al%d" % t, 0, 20)), "s")
         unpack(t, "fp", "lc", "lp", range(2, 4))
@@ -517,19 +546,16 @@ def rank_program(g, core, T, topo):
         list_b = [later(scan, O("BS"), O("rise", 0, 320), O("BG")), later(narrow, O("bl%d" % t), O("BS", 15, 320, 16))]
         if t < 2:
             la = score_list(*((2, 22) if t == 0 else (0, 24)))
-            fillers = la + list_b + (caps[:2] if t == 0 else [])
+            fillers = la + (caps[:1] + list_b[:1] + caps[1:2] if t == 0 else [lambda: None] + list_b)
             weave([], [take(1) + fillers[i:i + 1] for i in range(TAKE[t][2])])
         else:
-            spread("ow", "OB", "pol", 0.0, "v", lambda i: list_b[i - 1:i])
+            spare = [[spread("ow", "OB", "pol", 0.0, "v", lambda i: list_b[i - 1:i])]]
+        z = [[later(copy, O("zt%d" % t, 4 * lo + b, 4 * hi, 4), by(O("fp%d" % t, 320 * b, 320 * b + 320), O("pl%d" % t, lo // 16, hi // 16)), ZQ[i][b])
+              for b in range(4)] + [later(quant, "zc%d" % t, "zs%d" % t, "zt%d" % t, lo, hi)] for i, (lo, hi) in enumerate(ZCH)]
+        weave(z[0][:4] + z[1][:1] + z[0][4:] + z[1][1:4] + take(1) + z[1][4:], [])
+        weave([list_b[1:], caps[:1], []][t] + take(TAKE[t][3]), [])
         for i, (lo, hi) in enumerate(ZCH):
-            o = O("pl%d" % t, lo // 16, hi // 16)
-            for b in range(4):
-                copy(O("zt%d" % t, 4 * lo + b, 4 * hi, 4), by(O("fp%d" % t, 320 * b, 320 * b + 320), o), ZQ[i][b])
-            weave(take(1), [])
-            quant("zc%d" % t, "zs%d" % t, "zt%d" % t, lo, hi)
-        weave(take(TAKE[t][3]) + (caps[:1] if t == 1 else []) + take(1) + (caps[1:2] if t == 1 else []), [])
-        for i, (lo, hi) in enumerate(ZCH):
-            for b in range(4):
+            for b in RO[i]:
                 p = mx("wq", 128 * b, "zc%d" % t, lo, hi, "zs%d" % t)
                 o = O("rb%d" % b, lo, hi)
                 if RQ[i][b] == "v":
@@ -539,39 +565,45 @@ def rank_program(g, core, T, topo):
         x = lambda lo, hi, b: O("xt%d" % (t + 1), 4 * lo + b, 4 * hi, 4)
         o = O("bl%d" % t)
         own = {b: mx("eq", 128 * b, "qc%d" % t, 0, 320, "qs%d" % t) for b in (2, 3)}
+        part = lambda b, lo, hi: (T[own[b][1][0][0]][:, lo:hi], own[b][1])
+        if t == 2:
+            break
         for b in range(2):
             tt(x(0, 320, b), by(O("rb%d" % b), o), O("fo%d" % t, 320 * b, 320 * b + 320), ADD)
             copy(O("tb%d" % (b + 2)), by(O("rb%d" % (b + 2)), o), "s")
-        if t < 2:
-            caps[2]()
-        else:
-            act(O("olf"), by(O("i320"), O("ow", 0, 20)), 1.0, 160.0)
-            dmas("dout", [("y", T.ol[:], T.olf[0:128:16, 0:320], [], O("olf")[1])])
+            if b == 0 and t == 1:
+                caps[1]()
+        late[0][-1]()
+        caps[2]()
         tt(x(0, 320, 2), O("tb2"), own[2], ADD)
         weave(take(TAKE[t][4]), [])
         for lo, hi in CH:
-            tt(x(lo, hi, 3), O("tb3", lo, hi), (T[own[3][1][0][0]][:, lo:hi], own[3][1]), ADD)
-        if t == 2:
-            break
+            tt(x(lo, hi, 3), O("tb3", lo, hi), part(3, lo, hi), ADD)
         for lo, hi in CH:
             quant("qc%d" % (t + 1), "qs%d" % (t + 1), "xt%d" % (t + 1), lo, hi)
-        if t == 0:
-            quant("vq", "vqs", "vt", 0, 128)
-        weave(take(TAKE[t][5]), [])
+        weave(late[1] + take(TAKE[t][5]), [])
         for i, (lo, hi) in enumerate(CH):
             scores(t + 1, lo, hi, "sv"[i])
+        weave(late[2], [])
         send_state(t + 1)
         unpack(t + 1, "fo", "qc", "qs", range(2))
         sa, sb = [scored(*p) for p in (((2, 12), (12, 22)) if t == 0 else ((0, 12), (12, 24)))]
-        weave(sa, [sb[:1], sb[1:2], sb[2:] + take(9)])
+        weave(sa, [sb[:1], sb[1:2], sb[2:] + late[3] + take(9)])
     scales = lambda q, k: (q, T.osc[4 * k:4 * k + 4, 0:320], T.qs3[32 * k:32 * k + 4, 0:320], [], O("qs3")[1])
     for lo, hi in CH:
-        quant("qc3", "qs3", "xt3", lo, hi)
+        for b in (2, 3):
+            copy(O("tb%d" % b, lo, hi), by(O("rb%d" % b), O("bl2", lo // 16, hi // 16)), "s")
+    act(O("olf"), by(O("i320"), O("ow", 0, 20)), 1.0, 160.0)
+    made = [[later(tt, x(lo, hi, b), by(O("rb%d" % b), O("bl2", lo // 16, hi // 16)), O("fo2", 320 * b + lo, 320 * b + hi), ADD) for b in (0, 1)]
+            + [later(tt, x(lo, hi, b), O("tb%d" % b, lo, hi), part(b, lo, hi), ADD) for b in (2, 3)] + [later(quant, "qc3", "qs3", "xt3", lo, hi)]
+            for lo, hi in CH]
+    weave(made[0][:4] + made[1][:1] + made[0][4:] + made[1][1:], [])
     for i, (lo, hi) in enumerate(CH):
         o, y = O("qc3", lo, hi), O("yb", lo, hi)
-        dmas("dout", [("y", T.oc[:, 4 * lo:4 * hi], codes(o)[0], [], o[1])] + [scales("y", k) for k in range(3 * i)])
+        dmas("dout", [("y", T.oc[:, 4 * lo:4 * hi], codes(o)[0], [], o[1])]
+             + ([scales("y", k) for k in range(3)] if i else [("y", T.ol[:], T.olf[0:128:16, 0:320], [], O("olf")[1])]))
         copy(y, mx("vq", 0, "qc3", lo, hi, "qs3"), "sv"[i])
-        dmas("dout", [scales("s", 3)] * (1 - i) + [("s", T.y[:, lo:hi], y[0], [], y[1])])
+        dmas("dout", [scales("s", 3)] * i + [("s", T.y[:, lo:hi], y[0], [], y[1])])
     for s in SEMAPHORES:
         if total[s]:
             g.wait_ge(T.sem[s], total[s])

from concourse.mybir import dt, AluOpType, ActivationFunctionType

FN = ActivationFunctionType
COPY = FN.Copy
A = AluOpType
ADD, SUB, MUL, MAX, MIN = A.add, A.subtract, A.mult, A.max, A.min
AND, SHR, NE, GE, LT, EQ = A.bitwise_and, A.arith_shift_right, A.not_equal, A.is_ge, A.is_lt, A.is_equal
BIG = 1048576.0
RISE = 8192.0
FAR = 1e29
STEP = [1, 2, 4]
RQ = ["vsss", "vvss"]
ZQ = ["vvss", "vvss"]
TQ = "s"
AT = [6, 7, 8, 9, 10, 11, 13, 14, 15, 16, 17, 18, 19, 21, 22, 23]
RO = [[2, 3, 0, 1], [0, 2, 1, 3]]
WH = [[2, 4, 7, 9], [0, 2, 3, 4], [1, 2, 4, 6]]
TAKE = [[[0, 0, 0, 2, 0, 1, 1, 0, 1, 0, 1, 1], [1, 1, 1], 5, 1, 0, 1], [[0, 0, 0, 2, 0, 1], [1, 1, 1], 6, 1, 1, 2], [[0, 0, 0, 1, 0, 1, 1, 0, 1, 1, 0, 1], [0, 0, 0], 0, 0, 0, 0]]
ZCH = [(0, 192), (192, 320)]
CH = [(0, 192), (192, 320)]

SCRATCH = {}


def _d(name, cols, dtype, where="sbuf"):
    SCRATCH[name] = (where, [128, cols], dtype)


ALIAS = {}


def _share(buf, dtype, *parts):
    at = 0
    for n, c in parts:
        ALIAS[n] = (buf, at, c)
        at += c + (-c) % 8
    _d(buf, at, dtype)


_share("iv", "int32", ("pint", 1), ("lanei", 1), ("xi", 1), ("hi", 1), ("ei", 1), ("quadi", 1), ("upi", 1), ("kk", 24), ("k1i", 24), ("k2i", 24),
       ("t8", 8), ("t8a", 8), ("t8b", 8), ("t8c", 8), ("t8d", 8), ("o32", 32), ("f0", 2), ("f1", 2), ("f2", 2))
_share("fv", "float32", ("lanef", 1), ("xf", 1), ("hf", 1), ("ef", 1), ("quadf", 1), ("upf", 1), ("h8", 1), ("q8", 1), ("x3", 1), ("c5", 1),
       ("kap2", 1), ("kap", 1), ("bb", 24), ("cb", 24), ("k20", 24), ("j16", 3), ("oa", 32), ("ob", 32), ("b12", 12), ("d12", 12), ("c2", 2),
       ("f3", 2), ("f4", 2), ("f5", 2), ("f6", 2), ("q24", 24), ("p24", 24),
       ("i16", 16), ("z16", 16), ("t320", 8), ("tone", 8), ("wd", 8), ("c8", 8), ("cap8", 8))
_share("ov", "float32", ("W", 112), ("a2", 8), ("FL", 24), ("D", 12), ("L", 24), ("M", 12), ("d0", 112), ("d1", 112), ("SS", 112),
       ("LK", 6), ("e3", 3), ("e6", 6),
       ("a1", 6), ("e1", 3), ("k1", 3), ("dB", 3), ("xB", 3))
_share("uv", "uint16", ("ogl", 2), ("upu", 8), ("gl", 24), ("fl", 24), ("fin", 2), ("ln", 24), ("rl", 24), ("sl", 16), ("of3", 24), ("lu", 24), ("ow", 32),
       ("pol", 24))
_share("wv", "float32", ("SC", 48), ("G2", 96), ("T1", 96), ("T2", 96), ("T4", 96), ("T3", 96))
_d("pgi", 40, "int32")
_d("OG", 160, "int32")
for _n, _c in (("rise", 384), ("gpat", 192), ("c0", 192), ("cpat", 192), ("N", 384), ("G", 64), ("sel", 256), ("selx", 256), ("G5", 384), ("T5", 384), ("MK", 384), ("GS", 384), ("TS", 384), ("SE", 384),
               ("PN", 192), ("PC", 192), ("ST", 320), ("BG", 320), ("BS", 320), ("tb2", 320), ("tb3", 320),
               ("rb0", 320), ("rb1", 320), ("rb2", 320), ("rb3", 320), ("olf", 320), ("yb", 320)):
    _d(_n, _c, "float32")
for _n, _c in (("pu", 80), ("off", 26), ("of2", 26), ("pos", 24)):
    _d(_n, _c, "uint16")
for _t in range(3):
    _d("al%d" % _t, 32, "uint16")
    _d("pl%d" % _t, 20, "uint16")
    _d("bl%d" % _t, 20, "uint16")
    _d("fo%d" % _t, 640, "bfloat16")
    _d("fp%d" % _t, 1280, "bfloat16")
    _d("zt%d" % _t, 1280, "bfloat16")
    _d("zc%d" % _t, 320, "float8_e4m3fn_x4")
    _d("zs%d" % _t, 320, "uint8")
    _d("lc%d" % _t, 320, "float8_e4m3fn_x4")
    _d("lp%d" % _t, 320, "uint8")
for _t in range(4):
    _d("xt%d" % _t, 1280, "bfloat16")
    _d("qc%d" % _t, 320, "float8_e4m3fn_x4")
    _d("qs%d" % _t, 320, "uint8")
for _n, _c in (("ones", 516), ("ec", 516), ("i320", 320), ("P", 2560), ("ut", 512), ("vt", 512), ("OB", 384), ("PK", 384), ("PT", 384), ("TM", 32),
               ("OT", 384), ("VAL", 384), ("VT", 384), ("far", 384), ("r16", 384)):
    _d(_n, _c, "bfloat16")
for _n, _c in (("eq", 512), ("wq", 512), ("uq", 128), ("uw", 128), ("vq", 128)):
    _d(_n, _c, "float8_e4m3fn_x4")
    _d(_n + "s", _c, "uint8")
for _k in range(8):
    _d("ps%d" % _k, 512, "float32", "psum")

DMA_SEMS = ["dpg", "dog", "du", "dx", "dw", "dp", "dout"]
SEMAPHORES = ["cv", "cs", "ct", "cg", "left", "rq0", "rq1", "rq2", "rl0", "rl1", "rl2"] + DMA_SEMS


def slot(k):
    return k // 2 + (4 if k % 2 else 0)


def rank_program(g, core, T, topo):
    rank = T.rank_of(core)
    if rank is None:
        return
    queue = {"v": g.vector, "s": g.scalar, "t": g.tensor, "g": g, "y": g.sync}
    total = {s: 0 for s in SEMAPHORES}
    clock = {q: {} for q in queue}
    wrote, read = {}, {}

    def O(name, lo=0, hi=None, step=1, rows=(0, 128)):
        if name in ALIAS:
            name, at, n = ALIAS[name]
            lo, hi = at + lo, at + (n if hi is None else hi)
        hi = SCRATCH[name][1][1] if hi is None else hi
        ap = T[name][rows[0]:rows[1], lo:hi] if step == 1 else T[name][rows[0]:rows[1], lo:hi:step]
        return (ap, [(name, lo, hi, step, lo % step) + rows])

    def codes(o):
        return (o[0].bitcast(dt.uint8), o[1])

    def words(o):
        return (o[0].bitcast(dt.uint32), o[1])

    def by(win, off):
        return (win[0].indirect(off[0]), win[1] + off[1])

    def meet(a, b):
        return a[1] < b[2] and b[1] < a[2] and a[5] < b[6] and b[5] < a[6] and not (a[3] == b[3] > 1 and a[4] != b[4])

    def covers(w, o):
        return w[3] == 1 and w[1] <= o[1] and o[2] <= w[2] and w[5] <= o[5] and o[6] <= w[6]

    def order(q, reads, writes, dma=False):
        evs = []
        writes = writes + [r for r in reads if r[0][:2] == "ps"]
        for r in reads:
            evs += [e for w, e in wrote.get(r[0], []) if meet(r, w)]
        for r in writes:
            evs += [e for w, e in wrote.get(r[0], []) if meet(r, w)]
            evs += [e for w, e in read.get(r[0], []) if meet(r, w) and (dma or e[3] != q or SCRATCH[r[0]][2] == "uint16")]
        want = {}
        for sem, val, snap, who in evs:
            if clock[q].get(sem, 0) < val and want.get(sem, (0,))[0] < val:
                want[sem] = (val, snap)
        for sem in list(want):
            if any(o != sem and want[o][1].get(sem, 0) >= want[sem][0] for o in want):
                del want[sem]
        for sem, (val, snap) in want.items():
            queue[q].wait_ge(T.sem[sem], val)
            for s2, v2 in list(snap.items()) + [(sem, val)]:
                clock[q][s2] = max(clock[q].get(s2, 0), v2)

    def note(reads, writes, ev):
        for r in reads:
            read.setdefault(r[0], []).append((r, ev))
        for w in writes:
            wrote[w[0]] = [(o, e) for o, e in wrote.get(w[0], []) if not covers(w, o)] + [(w, ev)]
            if w[0] in read:
                read[w[0]] = [(o, e) for o, e in read[w[0]] if not covers(w, o)]

    def run(q, outs, ins, call):
        reads = [r for o in ins for r in o[1]]
        writes = [r for o in outs for r in o[1]]
        order(q, reads, writes)
        sem = "c" + q
        total[sem] += 1
        snap = dict(clock[q])
        call().then_inc(T.sem[sem], 1)
        note(reads, writes, (sem, total[sem], snap, q))

    def dmas(sem, items):
        snap = {}
        for q, out, in_, writes, reads in items:
            order(q, reads, writes, True)
            queue[q].dma_start(out, in_).then_inc(T.sem[sem], 16)
            total[sem] += 16
            for s2, v2 in clock[q].items():
                snap[s2] = max(snap.get(s2, 0), v2)
        for q, out, in_, writes, reads in items:
            note(reads, writes, (sem, total[sem], snap, "dma"))

    def copy(out, in_, q="v"):
        if q == "v":
            run(q, [out], [in_], lambda: g.vector.tensor_copy(out[0], in_[0]))
        else:
            run(q, [out], [in_], lambda: g.scalar.activation(out[0], in_[0], COPY))

    def tt(out, a, b, op):
        run("v", [out], [a, b], lambda: g.vector.tensor_tensor(out[0], a[0], b[0], op))

    def ts(out, a, s1, s2, op0, op1=None):
        ins = [a] + [s for s in (s1, s2) if isinstance(s, tuple)]
        v1 = s1[0] if isinstance(s1, tuple) else s1
        v2 = s2[0] if isinstance(s2, tuple) else s2
        if op1 is None:
            run("v", [out], ins, lambda: g.vector.tensor_scalar(out[0], a[0], v1, None, op0))
        else:
            run("v", [out], ins, lambda: g.vector.tensor_scalar(out[0], a[0], v1, v2, op0, op1))

    def act(out, in_, scale, bias):
        run("s", [out], [in_], lambda: g.scalar.activation(out[0], in_[0], FN.Identity, bias=bias, scale=scale))

    def scan(out, d0, d1, op0=ADD, op1=MAX):
        run("v", [out], [d0, d1], lambda: g.vector.tensor_tensor_scan(out[0], d0[0], d1[0], 0.0, op0, op1))

    def turn(out, in_):
        run("v", [out], [in_], lambda: g.vector.transpose(out[0], in_[0]))

    def fill(out, value):
        run("v", [out], [], lambda: g.vector.memset(out[0], value))

    def iota(out, pattern, base, mul=0):
        kw = {} if SCRATCH[out[1][0][0]][2] == "int32" else {"allow_small_or_imprecise_dtypes": True}
        run("g", [out], [], lambda: g.iota(out[0], pattern, base, mul, **kw))

    def select(out, in_, pattern, op, fill_, base=0, mul=0):
        run("g", [out], [in_], lambda: g.affine_select(out[0], in_[0], pattern, op, fill_, base, mul))

    def pack(q, s, x):
        run("v", [q, s], [x], lambda: g.vector.quantize_mx(q[0], s[0], x[0]))

    def quant(cn, sn, xn, lo, hi):
        pack(O(cn, lo, hi), O(sn, lo, hi), O(xn, 4 * lo, 4 * hi))

    bank = [0]

    def mx(an, alo, bn, lo, hi, bsn):
        k = bank[0] % 8
        bank[0] += 1
        out = O("ps%d" % k, 0, hi - lo)
        full = (out[0], O("ps%d" % k)[1])
        a, s = O(an, alo, alo + 128), O(an + "s", alo, alo + 128)
        b, p = O(bn, lo, hi), O(bsn, lo, hi)
        run("t", [full], [a, s, b, p], lambda: g.tensor.matmul_mx(out[0], a[0], s[0], b[0], p[0], True, True))
        return full

    def narrow(out, wide, climb="kap2"):
        ts(out, wide, O(climb), None, SUB)

    def later(f, *args):
        return lambda: f(*args)

    def weave(chain, beside):
        for i in range(max(len(chain), len(beside))):
            for call in chain[i:i + 1] + (beside[i] if i < len(beside) else []):
                call()

    def load(q, name, src, lo, hi, rows=(0, 128)):
        o = O(name, lo, hi, 1, rows)
        return (q, o[0], src, o[1], [])

    dmas("dpg", [load("y", "pgi", T.pg[:], 0, 20), load("s", "pgi", T.pg[0:112, :], 20, 40, (16, 128)),
                 load("y", "pgi", T.pg[112:128, :], 20, 40, (0, 16))])
    dmas("dog", [load("s", "OG", T.og[0:112, :], 20, 40, (16, 128)), load("y", "OG", T.og[:], 0, 20),
                 load("s", "OG", T.og[112:128, :], 20, 40, (0, 16))])
    dmas("dx", [load("y", "xt0", T.x[:], 0, 1280)])
    dmas("du", [load("s", "ut", T.u[:], 0, 512)])
    dmas("dw", [("y", codes(O("wq"))[0], T.wc[:], O("wq")[1], []), ("y", O("wqs")[0], T.ws[:], O("wqs")[1], []),
                load("y", "vt", T.v[:], 0, 512)])

    fill(O("ones"), 1.0)
    iota(O("pint"), [[1, 1]], 0, 1)
    iota(O("i16"), [[1, 16]], 0)
    iota(O("kk"), [[-1, 2], [-2, 4], [0, 3]], 8)
    iota(O("bb"), [[0, 8], [2, 3]], 0)
    iota(O("i320"), [[1, 320]], -160)
    iota(O("t8"), [[-1, 8]], 8)
    iota(O("wd"), [[320, 8]], 0)

    for name, shift, mask in (("lane", 0, 15), ("x", 0, 7), ("h", 4, 7), ("e", 4, 1), ("quad", 5, 3), ("up", 3, 1)):
        ts(O(name + "i"), O("pint"), shift, mask, SHR, AND)
    fill(O("far"), FAR)
    copy(O("fv", 0, 48, 8), O("iv", 8, 56, 8))
    fill(O("sel"), 13.0)
    ts(O("z16"), O("i16"), O("lanef"), None, NE)
    ts(O("ln"), O("ones", 0, 24), O("lanef"), None, MUL)
    ts(O("c5"), O("quadf"), 5.0, O("ef"), MUL, ADD)
    ts(O("k1i"), O("kk"), O("hf"), None, ADD)
    act(O("rise"), by(O("z16"), O("ln")), BIG + RISE, -BIG)
    fill(O("sel", 0, 110, 5), 12.0)
    fill(O("oa"), 0.0)
    ts(O("kap"), O("lanef"), -RISE, 15 * RISE, MUL, ADD)
    ts(O("kap2"), O("lanef"), -RISE, 15 * RISE - 160.0, MUL, ADD)
    ts(O("cb"), O("bb"), O("c5"), 19.0, ADD, MIN)
    ts(O("k2i"), O("k1i"), 7, None, AND)
    ts(O("h8"), O("hf"), 8.0, None, ADD)
    ts(O("j16"), O("cb", 0, 3), 16.0, O("lanef"), MUL, ADD)
    ts(O("k20"), O("k2i"), 20.0, None, MUL)
    fill(O("off"), 0)
    ts(O("c8"), O("i16", 0, 8), O("xf"), 2 * FAR, EQ, MUL)
    ts(O("upu"), O("ones", 0, 8), O("xf"), 16.0, MUL, MUL)
    tt(O("oa", 0, 24), O("k20"), O("cb"), ADD)
    fill(O("ov", 0, 133), 0.0)

    iota(O("sel", 1, 105, 5), [[0, 7], [1, 3]], 0)
    iota(O("sel", 2, 105, 5), [[0, 7], [1, 3]], 3)
    iota(O("sel", 79, 105, 5), [[-10, 2], [1, 3]], 16)
    iota(O("sel", 131, 233, 5), [[0, 7], [1, 3]], 0)
    iota(O("sel", 132, 173, 5), [[1, 9]], 0)
    iota(O("b12"), [[0, 4], [1, 3]], 0)
    iota(O("d12"), [[2, 4], [0, 3]], 0)
    iota(O("c2"), [[16, 2]], -2)

    def quarters(name, width, to, fro, shift, qs, step=1):
        size = [128, 32, 64, 32][shift]
        for n, p in enumerate(range(0, 128, size)):
            at = (p + 32 * shift) % 128
            copy(O(name, to, to + width, 1, (at, at + size)), O(fro[0], fro[1], fro[1] + width * step, step, (p, p + size)), qs[n % len(qs)])

    def table(s, q):
        copy(O("P", 320 * s, 320 * s + 320), by(O("i320"), O("pu", 20 * s, 20 * s + 20)), q)

    copy(O("pu", 0, 40), O("pgi"))
    quarters("pu", 40, 40, ("pgi", 0), 1, "v")
    table(0, "s")
    table(1, "s")
    scan(O("ob"), O("rise", 0, 32), O("oa"))
    quarters("OG", 40, 40, ("OG", 0), 1, "v")
    quarters("P", 640, 1280, ("P", 0), 2, "s")
    table(2, "v")
    narrow(O("ogl"), O("ob", 15, 32, 16), "kap")
    quarters("OG", 80, 80, ("OG", 0), 2, "v")
    table(3, "v")
    copy(O("o32"), by(O("OG"), O("ogl")))
    ts(O("t8a"), O("t8"), O("hf"), None, ADD)
    copy(O("P", 1920, 2560, 1, (0, 64)), O("P", 640, 1280, 1, (64, 128)))
    ts(O("k1i"), O("o32", 0, 24), -1.0, O("h8"), MUL, ADD)
    copy(O("P", 1920, 2560, 1, (64, 128)), O("P", 640, 1280, 1, (0, 64)))
    ts(O("k2i"), O("k1i"), 7, None, AND)
    ts(O("t8b"), O("t8a"), 7, None, AND)
    quant("uq", "uqs", "ut", 0, 128)
    for c in range(3):
        ts(O("off", c, c + 1), O("k2i", c, c + 1), 320.0, O("j16", c, c + 1), MUL, ADD)
    copy(O("lu"), O("k2i"))
    ts(O("e1"), O("k2i", 12, 15), 320.0, O("kap2"), MUL, SUB)
    ts(O("L"), O("k2i"), 320.0, None, MUL)
    copy(O("N"), by(O("wd"), O("lu")), "s")
    copy(O("tone"), O("t8b"))
    select(O("r16"), O("far"), [[0, 24], [1, 16]], NE, -FAR)
    select(O("ec"), O("ones"), [[-1, 516]], EQ, 0.0, 3, 4)

    lists = [later(ts, O("x3"), O("xf"), 3.0, None, MUL), later(ts, O("t8c"), O("t8"), O("ef"), None, ADD),
             later(ts, O("rl", 0, 12), O("b12"), O("x3"), None, ADD), later(ts, O("t8d"), O("t8c"), 7, None, AND),
             later(ts, O("rl", 12, 24), O("d12"), O("upf"), None, ADD), later(ts, O("t320"), O("t8d"), 320.0, None, MUL),
             later(ts, O("f0"), O("c2"), O("lanef"), 0.2, ADD, MUL), later(copy, O("gpat"), by(O("t320"), O("rl", 12, 24)), "s"),
             later(ts, O("q8"), O("quadf"), 8.0, None, ADD), later(ts, O("f3"), O("f0"), -5.0, O("lanef"), MUL, ADD),
             later(ts, O("f1"), O("f0"), -1.0, O("q8"), MUL, ADD), later(tt, O("f4"), O("f3"), O("c2"), ADD),
             later(ts, O("f2"), O("f1"), 3, None, AND), later(ts, O("f5"), O("f2"), 6.0, 2.0, MUL, ADD),
             later(tt, O("f6"), O("f5"), O("f4"), ADD), later(copy, O("fin"), O("f6"))]
    by_position = [later(ts, O("k1i"), O("q24"), O("quadf"), None, ADD), later(ts, O("k2i"), O("k1i"), 3, None, AND),
                   later(ts, O("k20"), O("k2i"), 48.0, O("lanef"), MUL, ADD), later(tt, O("cb"), O("k20"), O("p24"), ADD),
                   later(copy, O("pol"), O("cb"))]

    partner = [T.cores[rank ^ s] for s in STEP]

    def send(t, pairs, sem):
        rid, pid, _s = topo.addr(partner[t])
        eng = topo.engines(core, partner[t])
        for out, in_ in pairs:
            order("g", in_[1], [])
            g.remote_dma(out[0], in_[0], T.sem[sem], T.sem.left, pid=pid, routing_id=rid, dma_engine_mask=sum(1 << e for e in eng))
            total["left"] += len(eng)
            total[sem] += len(eng)
        note([], [r for out, in_ in pairs for r in out[1]], (sem, total[sem], {}, "far"))

    def send_state(t):
        send(t, [(codes(O("lc%d" % t)), codes(O("qc%d" % t))), (O("lp%d" % t), O("qs%d" % t))], "rq%d" % t)

    def scores(t, lo, hi, q):
        copy(O("ST", lo, hi), mx("uw", 0, "qc%d" % t, lo, hi, "qs%d" % t), q)

    def col(k):
        return 22 if k == 7 else 3 * slot(k)

    def off(k):
        return O("off", col(k), col(k) + 3)

    def place(name, k, before=0):
        return O(name, 48 * slot(k) - before, 48 * slot(k) + 48)

    def kept(name, lo=0, hi=1):
        return O(name, 48 * lo + 15, 48 * hi, 16)

    def label(k):
        return O("L", 3 * slot(k), 3 * slot(k) + 3)

    def step(k, wide=True):
        odd = col(k) % 2
        gk = O("G", 16 - 16 * odd, 64)
        pk = by(O("P"), O("off", col(k) - odd, col(k) + 3))
        keep = later(scan, O("SC"), O("rise", 0, 48), O("G", 16, 64))
        if wide:
            return [later(tt, gk, pk, place("N", k + 1, 16 * odd), ADD), keep, later(narrow, off(k + 1), kept("SC"))]
        return [later(copy, gk, pk), keep,
                lambda: [ts(O("off", col(k + 1) + c, col(k + 1) + c + 1), O("SC", 16 * c + 15, 16 * c + 16), O("e1", c, c + 1), None, ADD) for c in range(3)]]

    first = [0, 1, 0]

    def sides(t):
        return ((12, 21), (3, 12)) if t == 1 else ((0, 12), (12, 24))

    def ahead(t, q="v"):
        f = first[t]
        w = lambda q, r, n=1: O("W", 15 * q + r, 15 * (q + n), 5)
        rise = O("rise", 0, 96)
        ps = lambda lo, hi: by(O("P"), O("of2", lo, hi))
        a, b = sides(t)
        return [[later(ts, w(0, 2, 2), O("off", col(f), col(f) + 6), O("kap2"), None, ADD)],
                [later(tt, O("D", 0, a[1] - a[0]), O("L", *b), O("L", *a), SUB)],
                [later(tt, O("a1"), w(0, 2, 2), O("D", 0, 6), ADD), later(copy, w(0, 4, 3), O("D", 0, 9))],
                [later(narrow, O("of2", 0, 6), O("a1"))],
                [later(tt, O("G2"), ps(0, 6), O("N", 48 * slot(f), 48 * slot(f) + 96), ADD)],
                [later(scan, O("T1"), rise, O("G2")), later(ts, w(3, 2, 2), O("off", col(f + 1), col(f + 1) + 6), O("kap2"), None, ADD)],
                [later(narrow, O("of2", 6, 12), kept("T1", 0, 2)), later(tt, w(3, 3), kept("T1"), w(3, 2), SUB)],
                [later(copy, O("G2"), ps(6, 12), q), later(tt, w(4, 1), kept("T1", 1, 2), w(4, 2), SUB)],
                [later(scan, O("T2"), rise, O("G2")), later(ts, w(2, 2), off(f + 4), O("kap2"), None, ADD)],
                [later(tt, O("a2", 0, 3), kept("T2"), label(f + 2), ADD), later(tt, O("a2", 4, 7), kept("T2"), label(f + 3), ADD)],
                [later(narrow, O("of2", 12, 19), O("a2", 0, 7)), later(tt, w(1, 3), O("a2", 0, 3), w(1, 2), SUB)],
                [later(tt, O("G2", 0, 48), ps(12, 15), place("N", f + 3), ADD), later(tt, O("G2", 48, 96), ps(16, 19), place("N", f + 2), ADD),
                 later(tt, O("k1"), label(f + 4), w(2, 2), SUB)],
                [later(scan, O("T3"), rise, O("G2")), later(tt, w(2, 1), kept("T2", 1, 2), O("k1"), ADD)],
                [later(narrow, O("of2", 20, 26), kept("T3", 0, 2)), later(tt, w(4, 3), kept("T3"), w(4, 2), SUB)],
                [later(copy, O("G2"), ps(20, 26), q), later(tt, O("xB"), kept("T3", 1, 2), kept("T1", 1, 2), SUB)],
                [later(scan, O("T4"), rise, O("G2")), later(tt, w(4, 0), O("xB"), w(4, 3), SUB)],
                [later(tt, w(2, 3), kept("T4"), O("k1"), ADD), later(tt, O("dB"), kept("T4", 1, 2), kept("T2", 1, 2), SUB)],
                [later(tt, w(2, 0), O("dB"), w(2, 3), SUB)]]

    def beyond(t):
        f = first[t]
        w = lambda r: O("W", 75 + r, 105, 5)
        end = lambda i: kept("T5", 2 * i, 2 * i + 2)
        early = [later(narrow, O("LK", 0, 3), label(f + 5)), later(narrow, O("LK", 3, 6), label(f + 4)), later(copy, O("of3", 18, 21), off(f + 4)),
                 later(tt, O("e3"), O("W", 32, 45, 5), O("D", 6, 9), ADD), later(narrow, O("of3", 21, 24), O("e3"))]
        starts = [later(ts, O("of3", 3 * z + c, 18, 6), O("T2", 63 + 16 * c, 192, 48), O("LK", 3 - 3 * z + c, 4 - 3 * z + c), None, ADD)
                  for z in range(2) for c in range(3)]
        return early, [starts + [later(copy, O("G5"), by(O("P"), O("of3")), "s")], [later(scan, O("T5"), O("rise"), O("G5"))],
                       [later(tt, w(3), end(1), end(3), SUB), later(tt, O("e6"), end(2), end(0), SUB), later(tt, w(1), end(0), end(3), SUB),
                        later(tt, w(2), end(3), O("LK"), ADD)], [later(tt, w(0), O("e6"), w(3), SUB)]]

    def values(lo, hi, q):
        c = 22 if lo == 7 else 3 * lo
        copy(O("VAL", 48 * lo, 48 * hi), by(O("P"), O("off", c, c + 3 * (hi - lo))), q)

    def unpack(t, name, cn, sn, planes):
        for b in planes:
            copy(O("%s%d" % (name, t), 320 * b, 320 * b + 320), mx("eq", 128 * b, cn + str(t), 0, 320, sn + str(t)), "s")

    def spread(out, win, where, add, other, between=lambda i: []):
        for i, q in enumerate(other + "v"):
            copy(O("PK", 192 * i, 192 * i + 192), by(O(win), O(where, 12 * i, 12 * i + 12)), q)
        weave(between(0), [])
        for i in (1, 0):
            turn(O("PT", 192 * i, 192 * i + 192), O("PK", 192 * i, 192 * i + 192))
        weave(between(1), [])
        for s in (3, 2, 0, 1):
            quarters("TM", 6, 6 * s, ("PT", 96 * s), s, other if s == 3 else "v", 16)
        weave(between(2), [])
        return later(ts, O(out), by(O("TM", 0, 24), O("fin")), add, None, ADD)

    units = later(ts, O("lu"), O("L"), 1.0 / 320.0, 0.25, MUL, ADD)
    groups = later(copy, O("OB"), by(O("tone"), O("lu")), "s")

    caps = [later(turn, O("OT"), O("OB")), later(copy, O("gl"), O("OT", 0, 384, 16)),
            later(copy, O("MK"), by(O("cap8"), O("gl")), "s")]

    def score_list(lo, hi):
        return [later(turn, O("VT", 16 * lo, 16 * hi), O("VAL", 16 * lo, 16 * hi)),
                later(ts, O("fl", lo, hi), O("VT", 16 * lo, 16 * hi, 16), 160.0, None, ADD)]

    def scored(lo, hi):
        w = (16 * lo, 16 * hi)
        return [later(tt, O("GS", *w), by(O("ST"), O("fl", lo, hi)), O("MK", *w), MIN), later(turn, O("TS", *w), O("GS", *w)),
                later(scan, O("SE", *w), O("r16", *w), O("TS", *w), MIN, MAX)]

    iota(O("c0"), [[0, 4], [16, 3], [0, 16]], 336)
    select(O("cpat"), O("c0"), [[0, 24], [1, 8]], EQ, -48.0, -7)
    groups()
    unit = [later(pack, O("eq", 128 * b, 128 * b + 128), O("eqs", 128 * b, 128 * b + 128), O("ec", 3 - b, 515 - b)) for b in range(4)]
    sp = ahead(0, TQ)
    (la, sa), (lb, sb), (lc, sc) = [(score_list(*p), scored(*p)) for p in ((12, 20), (0, 12), (20, 24))]
    chain = [c for k in range(7) for c in step(k, k > 0)] + [later(values, 7, 8, "v")] + lc + sc
    more = {0: [later(copy, words(O("uw")), by(words(O("uq")), O("upu"))), later(copy, O("uws"), by(O("uqs"), O("upu")), "s")],
            1: [later(scan, O("selx"), O("rise", 0, 256), O("sel"))],
            2: [later(quant, "qc0", "qs0", "xt0", 0, 192), later(ts, O("cap8"), O("c8"), FAR, None, SUB)],
            3: [later(quant, "qc0", "qs0", "xt0", 192, 320), later(scores, 0, 0, 320, "s"), later(send_state, 0)],
            4: sp[1] + [later(narrow, O("sl"), O("selx", 15, 256, 16), "kap")] + lists[:2], 5: caps[:1] + sp[0],
            6: lists[2:4], 7: caps[1:] + lists[4:6], 8: [], 9: lists[6:7], 10: lists[7:9], 12: [later(fill, O("FL", 13, 24), 1.0)], 13: lists[9:10], 14: [later(values, 4, 7, "s")] + lists[10:11], 16: la[:1],
            17: [later(values, 0, 4, "s")] + la[1:], 18: sa[:1], 19: lb[:1], 20: sa[1:2] + lb[1:], 21: sb[:1], 22: sa[2:], 23: sb[1:2], 24: sb[2:],
            25: unit[:1] + lists[11:13], 26: unit[1:2] + lists[13:14]}
    for i, at in enumerate(AT):
        more[at] = sp[i + 2] + more.get(at, [])
    weave(chain, [more.get(i, []) for i in range(27)])
    iota(O("q24"), [[1, 4], [0, 6]], 0)
    iota(O("p24"), [[0, 4], [16, 3], [192, 2]], 0)

    for t in range(3):
        f = first[t]
        a, b = sides(t)
        n = a[1] - a[0]
        sp = ahead(t + 1) if t < 2 else [[]] * 18
        tt(O("FL", 0, n), O("SE", 16 * b[0] + 15, 16 * b[1], 16), O("SE", 16 * a[0] + 15, 16 * a[1], 16), LT)
        if t == 0:
            weave(unit[2:3] + lists[14:15], [])
        rows = 7 if t == 1 else 5
        if t == 1:
            tt(O("FL", 16, 19), O("SE", 16 * b[0] + 111, 16 * b[0] + 144, 16), O("SE", 16 * a[0] + 111, 16 * a[0] + 144, 16), GE)
        tt(O("M", 0, n), O("FL", 0, n), O("D", 0, n), MUL)
        tt(O("d1", 0, 16 * rows), by(O("FL"), O("sl", 8, 8 + rows)), O("W", 0, 16 * rows), MUL)
        copy(O("d0", 0, 16 * rows), by(O("FL"), O("sl", 0, rows)))
        tt(O("L", *a), O("L", *a), O("M", 0, n), ADD)
        tt(O("L", *b), O("L", *b), O("M", 0, n), SUB)

        def labels(pieces):
            for lo, hi in pieces:
                copy(O("N", 16 * lo, 16 * hi), by(O("wd"), O("lu", lo, hi)), "s")

        now, then = [([(8, 12), (20, 24)], [(12, 18), (6, 8)]), ([], [(0, 6), (14, 18)]), ([(8, 12), (20, 24)], [])][t]
        five = later(narrow, O("off", col(f), col(f) + 9), O("SS", 4, 45, 5))
        sixth = lambda: [ts(O("off", col(f + 5) + c, col(f + 5) + c + 1), O("SS", 79 + 5 * c, 80 + 5 * c), O("SS", 94 + 5 * c, 95 + 5 * c), None, ADD)
                         for c in range(3)]
        chain = ([later(scan, O("SS", 0, 16 * rows), O("d0", 0, 16 * rows), O("d1", 0, 16 * rows), MUL, ADD)]
                 + ([sixth] if t == 1 else [five] + step(4, False) + step(5)) + step(6) + [later(values, 7, 8, "v")])
        where = [later(tt, O("PN", 96 * i, 96 * i + 96), by(O("L"), O("rl", 6 * i, 6 * i + 6)), O("gpat", 96 * i, 96 * i + 96), NE) for i in range(2)]
        where += [later(scan, O("PC"), O("PN"), O("cpat"), MUL, ADD), later(ts, O("pos"), O("PC", 7, 192, 8), O("lanef"), None, ADD)]
        odd, even, rest = later(values, 4, 7, "s"), later(values, 0, 4, "s"), later(labels, then)
        fp = lambda *planes: later(unpack, t, "fp", "lc", "lp", planes)
        beside = [(unit[3:] if t == 0 else []) + [units, later(labels, now), fp(0, 1)] * (t != 1),
                  [five, units, fp(0, 1)] if t == 1 else [later(narrow, O("e1"), label(5))] + lists[15:] * (t == 0),
                  [later(narrow, O("off", col(f + 1), col(f + 1) + 6), O("SS", 49, 75, 5))], []]
        late = [[lambda: None], [], [], []]
        if t == 0:
            early, late = beyond(1)
            spare = sp[:9] + [sp[9 + i] + early[i:i + 1] for i in range(5)] + sp[14:16] + [late[0][:-1], sp[16], sp[17]]
        else:
            spare = list(sp) if t == 1 else [[c] for c in by_position] + [[later(quant, "vq", "vqs", "vt", 0, 128)]]
        take = lambda n: [c for _ in range(min(n, len(spare))) for c in spare.pop(0)]
        if t == 1:
            beside[1] += [odd, rest]
            beside[2:] = [[], beside[2] + [even]]
        else:
            beside[2] += [rest, groups]
            beside += [[odd], [], [], [even]]
        beside += [[] for _ in range(len(chain) - len(beside))]
        for i, call in zip(WH[t], where):
            beside[i] = beside[i] + [call]
        weave(chain, [beside[i] + take(TAKE[t][0][i]) for i in range(len(chain))])
        spread("al%d" % t, "VAL", "pos", 160.0, "s", lambda i: take(TAKE[t][1][i]))()
        send(t, [(O("pl%d" % t), O("al%d" % t, 0, 20))], "rl%d" % t)
        copy(O("BG"), by(O("P", 0, 320), O("al%d" % t, 0, 20)), "s")
        unpack(t, "fp", "lc", "lp", range(2, 4))
        if t == 0:
            unpack(0, "fo", "qc", "qs", range(2))
        if t == 1:
            groups()
        list_b = [later(scan, O("BS"), O("rise", 0, 320), O("BG")), later(narrow, O("bl%d" % t), O("BS", 15, 320, 16))]
        if t < 2:
            la = score_list(*((2, 22) if t == 0 else (0, 24)))
            fillers = la + (caps[:1] + list_b[:1] + caps[1:2] if t == 0 else [lambda: None] + list_b)
            weave([], [take(1) + fillers[i:i + 1] for i in range(TAKE[t][2])])
        else:
            spare = [[spread("ow", "OB", "pol", 0.0, "v", lambda i: list_b[i - 1:i])]]
        z = [[later(copy, O("zt%d" % t, 4 * lo + b, 4 * hi, 4), by(O("fp%d" % t, 320 * b, 320 * b + 320), O("pl%d" % t, lo // 16, hi // 16)), ZQ[i][b])
              for b in range(4)] + [later(quant, "zc%d" % t, "zs%d" % t, "zt%d" % t, lo, hi)] for i, (lo, hi) in enumerate(ZCH)]
        weave(z[0][:4] + z[1][:1] + z[0][4:] + z[1][1:4] + take(1) + z[1][4:], [])
        weave([list_b[1:], caps[:1], []][t] + take(TAKE[t][3]), [])
        for i, (lo, hi) in enumerate(ZCH):
            for b in RO[i]:
                p = mx("wq", 128 * b, "zc%d" % t, lo, hi, "zs%d" % t)
                o = O("rb%d" % b, lo, hi)
                if RQ[i][b] == "v":
                    ts(o, p, 0.03125, None, MUL)
                else:
                    run("s", [o], [p], lambda: g.scalar.activation(o[0], p[0], COPY, scale=0.03125))
        x = lambda lo, hi, b: O("xt%d" % (t + 1), 4 * lo + b, 4 * hi, 4)
        o = O("bl%d" % t)
        own = {b: mx("eq", 128 * b, "qc%d" % t, 0, 320, "qs%d" % t) for b in (2, 3)}
        part = lambda b, lo, hi: (T[own[b][1][0][0]][:, lo:hi], own[b][1])
        if t == 2:
            break
        for b in range(2):
            tt(x(0, 320, b), by(O("rb%d" % b), o), O("fo%d" % t, 320 * b, 320 * b + 320), ADD)
            copy(O("tb%d" % (b + 2)), by(O("rb%d" % (b + 2)), o), "s")
            if b == 0 and t == 1:
                caps[1]()
        late[0][-1]()
        caps[2]()
        tt(x(0, 320, 2), O("tb2"), own[2], ADD)
        weave(take(TAKE[t][4]), [])
        for lo, hi in CH:
            tt(x(lo, hi, 3), O("tb3", lo, hi), part(3, lo, hi), ADD)
        for lo, hi in CH:
            quant("qc%d" % (t + 1), "qs%d" % (t + 1), "xt%d" % (t + 1), lo, hi)
        weave(late[1] + take(TAKE[t][5]), [])
        for i, (lo, hi) in enumerate(CH):
            scores(t + 1, lo, hi, "sv"[i])
        weave(late[2], [])
        send_state(t + 1)
        unpack(t + 1, "fo", "qc", "qs", range(2))
        sa, sb = [scored(*p) for p in (((2, 12), (12, 22)) if t == 0 else ((0, 12), (12, 24)))]
        weave(sa, [sb[:1], sb[1:2], sb[2:] + late[3] + take(9)])
    scales = lambda q, k: (q, T.osc[4 * k:4 * k + 4, 0:320], T.qs3[32 * k:32 * k + 4, 0:320], [], O("qs3")[1])
    for lo, hi in CH:
        for b in (2, 3):
            copy(O("tb%d" % b, lo, hi), by(O("rb%d" % b), O("bl2", lo // 16, hi // 16)), "s")
    act(O("olf"), by(O("i320"), O("ow", 0, 20)), 1.0, 160.0)
    made = [[later(tt, x(lo, hi, b), by(O("rb%d" % b), O("bl2", lo // 16, hi // 16)), O("fo2", 320 * b + lo, 320 * b + hi), ADD) for b in (0, 1)]
            + [later(tt, x(lo, hi, b), O("tb%d" % b, lo, hi), part(b, lo, hi), ADD) for b in (2, 3)] + [later(quant, "qc3", "qs3", "xt3", lo, hi)]
            for lo, hi in CH]
    weave(made[0][:4] + made[1][:1] + made[0][4:] + made[1][1:], [])
    for i, (lo, hi) in enumerate(CH):
        o, y = O("qc3", lo, hi), O("yb", lo, hi)
        dmas("dout", [("y", T.oc[:, 4 * lo:4 * hi], codes(o)[0], [], o[1])]
             + ([scales("y", k) for k in range(3)] if i else [("y", T.ol[:], T.olf[0:128:16, 0:320], [], O("olf")[1])]))
        copy(y, mx("vq", 0, "qc3", lo, hi, "qs3"), "sv"[i])
        dmas("dout", [scales("s", 3)] * i + [("s", T.y[:, lo:hi], y[0], [], y[1])])
    for s in SEMAPHORES:
        if total[s]:
            g.wait_ge(T.sem[s], total[s])
